import numpy as np, ml_dtypes
CORES = [35,38,43,46]
N = 4
BF = ml_dtypes.bfloat16
H, P, B, T, S = 4096, 1024, 256, 4, 32
BOUND = P + B * (np.arange(T * B) // B)
def parts(rng):
    G = P + T * B
    fe = (256 * (0.6 * rng.random((N, 8, 16, G)) + 0.4 * rng.random((N, 8, 1, G)))).astype(np.int64)
    no = (256 * (0.6 * rng.random((N, 8, 16, H)) + 0.4 * rng.random((N, 8, 1, H)))).astype(np.int64)
    no = np.minimum(no + rng.integers(0, 64, (N, 8, 1, 1)), 255)
    co = rng.integers(0, BOUND, (N, 8, 16, T * B))
    pool = np.argsort(rng.random((N, 8, H)), axis=-1)[..., :256]; ix = (256 * rng.random((N, 8, P)) ** 3).astype(np.int64)
    hv = np.where(rng.random((N, 8, P)) < 0.3, rng.integers(0, H, (N, 8, P)), np.take_along_axis(pool, ix, 2))
    return fe, no, co, hv
def pack(fe, no, co, hv):
    return {"lim": np.ascontiguousarray(no.reshape(N, 128, H)).astype(np.float32).astype(BF), "feat": np.ascontiguousarray(fe.reshape(N, 128, P + T * B)).astype(np.float32).astype(BF),
            "comp": np.ascontiguousarray(co.reshape(N, 128, T * B)).astype(np.int32), "hd": np.ascontiguousarray(hv).astype(np.int32)}
def setup_inputs(rng):
    return pack(*parts(rng))
def setup_inputs_ties(rng):
    fe, no, co, hv = parts(rng)
    d = rng.permutation(np.array([1, 2, S - 1, S, S + 1, S, 1, S + 1])).reshape(1, 8, 1, 1)
    fe = 100 + d * (rng.random(fe.shape) < 0.8).astype(np.int64); no = 100 + d * (rng.random(no.shape) < 0.35).astype(np.int64)
    fe[..., 1::2] = fe[..., 0::2].copy()
    co[:, :, 8:, ::3] = co[:, :, :8, ::3].copy()
    return pack(fe, no, co, hv)
def setup_inputs_alike(rng):
    fe, no, co, hv = parts(rng)
    hv[:, ::2] = rng.choice(np.array([0, H - 1, H // 2, 37]), (N, 4, P)); hv[..., 0] = H - 1; hv[..., P - 1] = 0
    no[:, :4] = rng.integers(200, 256, (N, 4, 16, H))
    co[:, 1] = co[:, 1, :1].copy()
    co[:, 3] = np.where(rng.random((N, 16, T * B)) < 0.5, 0, BOUND - 1)
    co[:, 5] = rng.integers(BOUND - B, BOUND, (N, 16, T * B))
    co[:, 7, 2:] = np.where(rng.random((N, 14, T * B)) < 0.5, co[:, 7, :1], co[:, 7, 1:2])
    return pack(fe, no, co, hv)
def setup_inputs_ends(rng):
    fe, no, co, hv = parts(rng); M = T * B; k = np.arange(16)[:, None]
    for g in range(5): hv[:, g] = rng.permutation(H)[:P]
    no[:, :5] = 255
    o = np.argsort(rng.random((N, 16, M)), axis=1); s = rng.integers(0, P // 2, (N, 1, M))
    fe[:, 0] = 255; fe[:, 0, :, 1:P:2] = 0
    co[:, 0] = np.where(o < 2, 2 * rng.integers(0, P // 2, (N, 1, M)) + 1, 2 * ((s + o) % (P // 2)))
    fe[:, 1, :, :P] = rng.integers(200, 256, (N, 16, P)); fe[:, 1, :, P:] = 255
    lo = np.argsort(rng.random((N, 3, T, B)), axis=-1)
    lo[:, 1:] = 0; lo[:, 2, :, 1:-1] = 1 + np.argsort(rng.random((N, T, B - 1)), axis=-1)[..., :B - 2]
    w = B + rng.integers(0, P - B, (N, 3, 1, M))
    co[:, 2:5] = np.where(k == rng.integers(0, 16, (N, 3, 1, M)), lo.reshape(N, 3, 1, M), w)
    fe[:, 2:5, :, P:] = rng.integers(0, 160, (N, 3, 16, M)); fe[:, 4, :, P::B] = 255
    for g, b in ((5, 254), (6, 0)):
        fe[:, g] = b + (rng.random((N, 16, P + M)) < 0.8).astype(np.int64); no[:, g] = b + (rng.random((N, 16, H)) < 0.3).astype(np.int64)
    return pack(fe, no, co, hv)
def setup_inputs_still(rng):
    fe, no, co, hv = parts(rng); fe = np.maximum(fe, 1)
    z = rng.integers(0, 3, (N, 8, 1, 1)); z[:, 0] = 0; z[:, 1] = 1; z[:, 2] = 2
    return pack(fe, np.where(z == 0, 255, np.where(z == 1, 0, no)), co, hv)
def setup_inputs_spread(rng):
    fe, no, co, hv = parts(rng)
    fe = (np.exp2(8 * rng.random((N, 8, 1, P + T * B))) * rng.random(fe.shape)).astype(np.int64)
    no = (np.exp2(8 * rng.random((N, 8, 1, H))) * rng.random(no.shape)).astype(np.int64)
    hv = (H * rng.random((N, 8, P)) ** 4).astype(np.int64)
    return pack(fe, no, co, hv)
def check_inputs(d):
    bad = []
    for k in ("lim", "feat"):
        x = np.asarray(d[k]).astype(np.float32)
        if not np.all((x >= 0) & (x <= 255) & (x == np.floor(x))): bad.append("whole numbers of " + k)
    if np.min(d["hd"]) < 0 or np.max(d["hd"]) > H - 1: bad.append("range of hd")
    if np.min(d["comp"]) < 0 or not np.all(np.asarray(d["comp"]) < BOUND): bad.append("range of comp")
    return bad
def reference(lim, feat, comp, hd):
    fe = feat.astype(np.float32).astype(np.int16).reshape(N, 8, 16, P + T * B); no = lim.astype(np.float32).astype(np.int16).reshape(N, 8, 16, H)
    co = comp.astype(np.int64).reshape(N, 8, 16, T * B)
    h = np.zeros((N, 8, P + T * B), np.int64); h[:, :, :P] = hd
    kappa = np.zeros(N, np.int64); ranks = np.arange(N)
    for t in range(T):
        fv = fe[..., P + t * B:P + (t + 1) * B]
        ix = co[..., t * B:(t + 1) * B].reshape(N, 8, 16 * B)
        c = np.take_along_axis(h, ix, 2)
        fc = np.take_along_axis(fe, ix[:, :, None, :], 3).reshape(N, 8, 16, 16, B)
        share = np.add.reduce(np.minimum(fv[:, :, :, None, :], fc), axis=2, dtype=np.int64)
        for a in range(N):
            q = (ranks + a) % N
            x = np.take_along_axis(no[q], c[:, :, None, :], 3).reshape(N, 8, 16, 16, B)
            n = np.add.reduce(fv[:, :, :, None, :] > x, axis=2, dtype=np.int64).reshape(N, 8, 16 * B)
            c = np.where(n >= 9, ((c * c >> 5) + c + 613 * n + kappa[q][:, None, None]) & (H - 1), c)
        c = c.reshape(N, 8, 16, B)
        m = np.add.reduce(c[:, :, :, None, :] == c[:, :, None, :, :], axis=3, dtype=np.int64)
        key = 4096 * m + share
        won = np.take_along_axis(c, np.argmax(key, axis=2)[:, :, None, :], 2)[:, :, 0]
        lost = np.take_along_axis(c, np.argmin(key, axis=2)[:, :, None, :], 2)[:, :, 0]
        h[:, :, P + t * B:P + (t + 1) * B] = won
        for r in range(N):
            for g in range(8):
                e, first = np.unique(lost[r, g], return_index=True)
                old = no[r, g][:, e]
                no[r, g][:, e] = old + np.clip(fv[r, g][:, first] - old, -S, S)
        kappa = np.add.reduce(won, axis=(1, 2)) & 255
    return {"yh": h[:, :, P:].astype(np.float32), "yl": no.reshape(N, 128, H).astype(np.float32).astype(BF)}

@@ -1,0 +1,638 @@
+from concourse.bass import DstId, RemoteDMATransfer
+from concourse.mybir import AluOpType as A, ActivationFunctionType as F
+
+NR, RT, H, DUMMY, HALF = 4, 4, 4096, 256, 2048
+MOD = 131072
+KS = 130
+SLOPE = 613 * 32 + MOD * KS
+OFF = MOD * 512
+BV = -256 - MOD * (9 * KS + 1) - OFF
+BS = BV + 8 * SLOPE
+CHUNKS = ((0, 4, "V", "V"), (4, 4, "S", "S"), (8, 5, "V", "S"), (13, 3, "S", "S"))
+SHARE_V = (0, 2)
+PIECE = 512
+CYC, GC, PEC = 0.83e-3 * 1.25, 1.56, 0.68e-3
+
+SCRATCH = {}
+SEMAPHORES = ["cv", "cs", "cp", "cg", "lsend"] + ["d%d" % j for j in range(52)] + ["ls%d" % j for j in range(10)]
+
+
+def _buf(names, cols, dtype, where="sbuf", rows=128):
+    for n in names.split():
+        SCRATCH[n] = (where, [rows] + (cols if isinstance(cols, list) else [cols]), dtype)
+
+
+B16, F32, I32, U16 = "bfloat16", "float32", "int32", "uint16"
+_buf("NB0 NB1 NB2 NB3", H + DUMMY, B16)
+_buf("FE HT", 2048, B16)
+_buf("FVT0 FVT1 FVT2 FVT3 XV0 XV1 XV2 XV3 GS0 GS1 GS2 GS3", 1280, B16)
+_buf("OUTV0 OUTV1 OUTV2 OUTV3", 264, B16)
+_buf("OUTL0 OUTL1 OUTL2 OUTL3 LU", 16, U16)
+for _t in range(RT - 1):
+    for _a in range(NR):
+        SEMAPHORES += ["iv%d_%d" % (_a, _t), "il%d_%d" % (_a, _t)]
+        if _a:
+            _buf("INV%d_%d" % (_a, _t), 264, B16)
+            _buf("INL%d_%d" % (_a, _t), 16, U16)
+for _a in range(1, NR):
+    SEMAPHORES += ["n%d_0" % _a, "n%d_1" % _a]
+_buf("ZL ZR", [32, 16], I32)
+_buf("Z ZT", [32, 32], I32)
+_buf("LT", 1024, U16)
+_buf("HD SPI", 64, I32)
+_buf("HDI", 128, I32)
+_buf("HDB BMW ID IDN IDK ONES", 128, B16)
+_buf("RI", 160, F32)
+_buf("RG", 128, F32)
+_buf("PI PM PG KI KJ", 2, I32)
+_buf("PF", 8, F32)
+_buf("MK DUP KV KW LF DL OF", 16, F32)
+_buf("MB", 160, B16)
+_buf("MIP", 16 * 160, B16)
+_buf("BI", 16 * 128, B16)
+_buf("E1 E05 ES1 ES5 ESN EX", 144, B16)
+_buf("FL OLD DC", 256, B16)
+_buf("SW SL", 1024, F32)
+_buf("TW C32 SQ M1", 256, F32)
+_buf("TRI", [16, 16], B16)
+_buf("SS0 SS1 SS2 SS3 XH0 XH1 GH0 GH1 SH0 SH1", 1024, B16)
+_buf("CL0 CL1 LB", 256, U16)
+_buf("TI CI", 256, I32)
+_buf("CW", 384, F32)
+_buf("EQ", [9, 256], B16)
+_buf("EQT", [16, 256], B16)
+_buf("KK DD", 512, F32)
+_buf("M2", 128, F32)
+_buf("M3", 64, F32)
+_buf("WLI", 32, I32)
+_buf("SPB", 64, B16)
+_buf("KS1", 2, F32)
+_buf("JUNK", 32, F32)
+_buf("YH8", 1024, F32, rows=8)
+_buf("B0 B1 B2 B3 B4 B5 KEY0 KEY1", 512, F32, "psum")
+PSUM = set(n for n in SCRATCH if SCRATCH[n][0] == "psum")
+CSEM = {"V": "cv", "S": "cs", "P": "cp", "G": "cg"}
+
+
+def add(gr, eng, emit, cost, reads=(), writes=(), kind="c", sem=None, val=0, lat=0.0, est=0.0, soft=()):
+    nodes = gr["nodes"]
+    i = len(nodes)
+    deps = set()
+    for w, regs in ((0, reads), (1, writes)):
+        for (b, c0, c1) in regs:
+            if b in PSUM:
+                st = gr["bank"].setdefault(b, [[], [], None])
+                if st[2] != eng:
+                    st[0], st[1], st[2] = st[1], [], eng
+                deps.update(e[0] for e in st[0])
+                deps.update(j for (j, d0, d1, dw) in st[1] if d0 < c1 and c0 < d1 and (w or dw))
+                st[1].append((i, c0, c1, w))
+            else:
+                keep = []
+                for e in gr["acc"].get(b, []):
+                    j, d0, d1, dw = e
+                    if d0 < c1 and c0 < d1 and (w or dw):
+                        deps.add(j)
+                    if not (w and j != i and c0 <= d0 and d1 <= c1):
+                        keep.append(e)
+                gr["acc"][b] = keep + [(i, c0, c1, w)]
+    deps.discard(i)
+    nodes.append({"id": i, "eng": eng, "emit": emit, "cost": cost, "kind": kind, "sem": sem, "val": val, "deps": deps,
+                  "soft": set(soft) - deps, "lat": lat, "est": est, "done": (sem, val)})
+    return i
+
+
+def schedule(gr):
+    nodes = gr["nodes"]
+    succ = [[] for _ in nodes]
+    for n in nodes:
+        for j in n["deps"] | n["soft"]:
+            succ[j].append(n["id"])
+    rank = [0.0] * len(nodes)
+    for n in reversed(nodes):
+        rank[n["id"]] = max([0.0] + [rank[s] for s in succ[n["id"]]]) + n["cost"] + n["lat"] + 0.05
+    left = [len(n["deps"] | n["soft"]) for n in nodes]
+    at = [n["est"] for n in nodes]
+    free, ready = {"R": 0.0}, {}
+    for n in nodes:
+        free[n["eng"]] = 0.0
+        ready.setdefault(n["eng"], set())
+        if left[n["id"]] == 0:
+            ready[n["eng"]].add(n["id"])
+    order = []
+    while len(order) < len(nodes):
+        best = None
+        for e in ready:
+            if ready[e]:
+                s = max(free[e], min(at[i] for i in ready[e]))
+                if best is None or s < best[0]:
+                    best = (s, e)
+        s, e = best
+        i = max((k for k in ready[e] if at[k] <= s), key=lambda k: (rank[k], -k))
+        n = nodes[i]
+        ready[e].discard(i)
+        if e != "R":
+            free[e] = s + n["cost"]
+        order.append(i)
+        for k in succ[i]:
+            left[k] -= 1
+            at[k] = max(at[k], s + n["cost"] + (n["lat"] if i in nodes[k]["deps"] else 0.0))
+            if left[k] == 0:
+                ready[nodes[k]["eng"]].add(k)
+    return order
+
+
+def emit_all(gr, order, g, T):
+    q = {"V": g.vector, "S": g.scalar, "P": g.tensor, "G": g, "Y": g.sync}
+    nodes, clk = gr["nodes"], {}
+    known = dict((e, {}) for e in q)
+    final = {}
+    for i in order:
+        n = nodes[i]
+        if n["kind"] == "r":
+            final[n["sem"]] = n["val"]
+            continue
+        e = n["eng"]
+        cl = dict(known[e])
+        need = {}
+        for j in n["deps"]:
+            d = nodes[j]
+            if not (e == "P" and d["eng"] == "P"):
+                s, v = d["done"]
+                need[s] = max(need.get(s, 0), v)
+        items = sorted(need.items(), key=lambda x: (-x[1], x[0]))
+        for s, v in items:
+            if cl.get(s, 0) >= v or any(s2 != s and clk.get((s2, v2), {}).get(s, 0) >= v and known[e].get(s2, 0) < v2
+                                        for s2, v2 in items):
+                continue
+            q[e].wait_ge(T.sem[s], int(v))
+            cl[s] = v
+            for s3, v3 in clk.get((s, v), {}).items():
+                cl[s3] = max(cl.get(s3, 0), v3)
+        known[e] = cl
+        ins = n["emit"](q[e])
+        if n["kind"] == "c":
+            s = CSEM[e]
+            n["done"] = (s, final.get(s, 0) + 1)
+            ins.then_inc(T.sem[s], 1)
+        elif n["kind"] == "d":
+            ins.then_inc(T.sem[n["sem"]], 16)
+        final[n["done"][0]] = max(final.get(n["done"][0], 0), n["done"][1])
+        clk[n["done"]] = cl
+    for s in sorted(final):
+        if known["G"].get(s, 0) < final[s]:
+            g.wait_ge(T.sem[s], int(final[s]))
+
+
+def build(core, T, topo):
+    rank = T.rank_of(core)
+    gr = {"nodes": [], "acc": {}, "bank": {}}
+    num = {"d": 0, "ls": 0, "x": 0, "s": 0, "b": 0, "lsend": 0}
+    lastd = {}
+
+    def nxt(k, n):
+        num[k] += 1
+        return (num[k] - 1) % n
+
+    def W(n):
+        return (n, 0, 1 << 20)
+
+    def vec(fn, cyc, reads, writes):
+        return add(gr, "V", fn, max(64, cyc) * CYC + 0.04, reads, writes)
+
+    def gps(fn, cyc, writes):
+        return add(gr, "G", fn, cyc * CYC + 0.15, [], writes)
+
+    def dma(eng, out, in_, lat, reads, writes, soft=()):
+        s = "d%d" % nxt("d", 99)
+        lastd[eng] = add(gr, eng, lambda q: q.dma_start(out, in_), 0.06, reads, writes, "d", s, 16, lat,
+                         soft=list(soft) + ([lastd[eng]] if eng in lastd else []))
+
+    def tt(out, in0, in1, op, cyc, reads, writes):
+        return vec(lambda q: q.tensor_tensor(out=out, in0=in0, in1=in1, op=op), cyc, reads, writes)
+
+    def ts(out, in0, s1, op0, cyc, reads, writes, s2=None, op1=None):
+        if op1 is None:
+            return vec(lambda q: q.tensor_scalar(out=out, in0=in0, scalar1=s1, scalar2=None, op0=op0), cyc, reads, writes)
+        return vec(lambda q: q.tensor_scalar(out=out, in0=in0, scalar1=s1, scalar2=s2, op0=op0, op1=op1), cyc, reads, writes)
+
+    def cp(out, in_, cyc, reads, writes):
+        return vec(lambda q: q.tensor_copy(out=out, in_=in_), cyc, reads, writes)
+
+    def fill(ap, val, n, reg):
+        vec(lambda q: q.memset(ap, val), n, [], [reg])
+
+    def act(out, in_, func, cyc, reads, writes, bias=0.0, scale=1.0, accum=None, soft=()):
+        def f(q):
+            if accum is not None:
+                return q.activation(out=out, in_=in_, func=func, bias=bias, scale=scale, accum_out=accum)
+            return q.activation(out=out, in_=in_, func=func, bias=bias, scale=scale)
+        return add(gr, "S", f, max(64, cyc) * CYC + 0.1, reads, writes, soft=soft)
+
+    def mms(lst, reads, writes, soft=()):
+        def f(q):
+            for (o, l, r, st, sp, _) in lst:
+                ins = q.matmul(o, l, r, st, sp)
+            return ins
+        return add(gr, "P", f, sum(max(64, x[5]) for x in lst) * PEC + 0.03, reads, writes, soft=soft)
+
+    def extract(bank, c0, en, x, start, stop, n=64, reg=None):
+        return mms([(T[bank][:, c0:c0 + n], T[en][:, 15 - i:143 - i], T[x][:, i:16 * n:16], start and i == 0, stop and i == 15, n)
+                    for i in range(16)], [(x, 0, 16 * n), W(en)], [reg or (bank, c0, c0 + n)])
+
+    def pieces(n, c):
+        return [(slice(j, min(n, j + PIECE)), slice(c + j // 16, c + min(n, j + PIECE) // 16)) for j in range(0, n, PIECE)]
+
+    def subtract(bank, fv, u, x):
+        m = u.stop - u.start
+        mms([(T[bank][:, 0:m], T.ID[:], T[fv][:, u], True, False, m)], [W("ID"), W(fv)], [W(bank)])
+        mms([(T[bank][:, 0:m], T.IDN[:], T[x][:, u], False, True, m)], [W("IDN"), (x, u.start, u.stop)], [W(bank)])
+
+    dma("S", T.HD[:], T.hd[:], 2.2, [], [W("HD")])
+    for a in range(4):
+        for h in range(2):
+            r0 = 32 * a + 16 * h
+            for e, n, d in (("S", "ZL", 0), ("Y", "ZR", 16)):
+                dma(e, T[n][r0:r0 + 16], T.comp[32 * a + d:32 * a + d + 16, 512 * h:512 * h + 512], 6.5, [], [(n, r0, r0 + 1)])
+    for h in (0, 1):
+        dma("Y", T.NB0[:, HALF * h:HALF * h + HALF], T.lim[:, HALF * h:HALF * h + HALF], 11.0, [], [("NB0", HALF * h, HALF * h + HALF)])
+    dma("S", T.FVT0[:, 0:256], T.feat[:, 1024:1280], 13.0, [], [("FVT0", 0, 256)])
+    dma("S", T.FE[:], T.feat[:], 16.0, [], [W("FE")])
+
+    def load_tiles(t, soft):
+        for j in range(5):
+            dma("Y", T["FVT%d" % t][:, 256 * j:256 * j + 256], T.feat[:, 1024 + 256 * t:1280 + 256 * t],
+                4.0, [], [("FVT%d" % t, 256 * j, 256 * j + 256)], soft)
+
+    gps(lambda q: q.iota(T.PI[:, 0:1], [[1, 1]], 0, 1), 2, [W("PI")])
+    for n, pat, base, c in (("RI", [[1, 160]], 0, 320), ("RG", [[16, 8], [0, 16]], 0, 256),
+                            ("TW", [[-4096, 16], [0, 16]], 15 * 4096, 512), ("DUP", [[16, 16]], H, 32)):
+        gps(lambda q, n=n, pat=pat, base=base: q.iota(T[n][:], pat, base, 0, allow_small_or_imprecise_dtypes=True), c, [W(n)])
+    ts(T.PM[:, 0:1], T.PI[:, 0:1], 15, A.bitwise_and, 1, [W("PI")], [W("PM")])
+    ts(T.PG[:, 0:1], T.PI[:, 0:1], 112, A.bitwise_and, 1, [W("PI")], [W("PG")])
+    for c, s, d in ((0, "PI", 0), (1, "PM", 0), (2, "PG", 0), (3, "PI", 16), (4, "PG", 15)):
+        ts(T.PF[:, c:c + 1], T[s][:, 0:1], d, A.add, 1, [W(s)], [("PF", c, c + 1)])
+    for c, v in ((5, OFF // 32 + 16), (6, -0.5), (7, -OFF)):
+        fill(T.PF[:, c:c + 1], float(v), 1, ("PF", c, c + 1))
+    SQB, HLF, MOFF = ("PF", 5, 6), ("PF", 6, 7), ("PF", 7, 8)
+
+    def eqc(name, n, col, val, src="RI"):
+        ts(T[name][:, 0:n], T[src][:, 0:n], T.PF[:, col:col + 1], A.is_equal, n, [W(src), ("PF", col, col + 1)], [W(name)], val, A.mult)
+    eqc("MB", 160, 3, 1.0)
+    eqc("MK", 16, 1, 1.0)
+    for y in range(16):
+        act(T.MIP[:, 160 * y:160 * y + 160], T.MB[:], F.Copy, 160, [W("MB"), W("MK")], [("MIP", 160 * y, 160 * y + 160)],
+            scale=T.MK[:, y:y + 1], soft=[lastd["S"]])
+    for n, v in (("E1", 1.0), ("ES1", 65536.0), ("E05", 0.5), ("EX", 0.0625), ("ES5", 32768.0), ("ESN", -32768.0)):
+        eqc(n, 144, 4, v)
+    for n, v in (("ID", 1.0), ("IDN", -1.0), ("IDK", float(1 << 28))):
+        eqc(n, 128, 0, v)
+    eqc("BMW", 128, 2, 1.0, "RG")
+    ts(T.DUP[:], T.DUP[:], T.PF[:, 1:2], A.add, 16, [W("DUP"), ("PF", 1, 2)], [W("DUP")])
+    for y in range(16):
+        act(T.BI[:, 128 * y:128 * y + 128], T.BMW[:], F.Copy, 128, [W("BMW"), W("MK")], [("BI", 128 * y, 128 * y + 128)],
+            scale=T.MK[:, y:y + 1], soft=[lastd["S"]])
+        ts(T.TRI[:, y, :], T.RI[:, 0:16], T.PF[:, 1:2], A.is_gt, 16, [W("RI"), ("PF", 1, 2)], [("TRI", 16 * y, 16 * y + 16)])
+    fill(T.ONES[:], 1.0, 64, W("ONES"))
+    fill(T.KV[:, 0:4], float(BV), 4, ("KV", 0, 4))
+    fill(T.KW[:, 0:4], float(BS), 4, ("KW", 0, 4))
+    for t in range(RT - 1):
+        fill(T["OUTV%d" % t][:, 256:264], 0.0, 4, ("OUTV%d" % t, 256, 264))
+    for c0, c1, w in ((256, 512, 256), (512, 1024, 512), (1024, 1280, 256)):
+        cp(T.FVT0[:, c0:c1], T.FVT0[:, 0:w], w // 2, [("FVT0", 0, w)], [("FVT0", c0, c1)])
+
+    ts(T.HDI[:, 0:64], T.HD[:], 4080, A.bitwise_and, 64, [W("HD")], [("HDI", 0, 64)])
+    ts(T.HDI[:, 64:128], T.HD[:], 15, A.bitwise_and, 64, [W("HD")], [("HDI", 64, 128)])
+    cp(T.HDB[:], T.HDI[:], 128, [W("HDI")], [W("HDB")])
+
+    def sel(i, d):
+        return T.MIP[:, 160 * i + 16 + i - d:160 * i + 144 + i - d]
+    for b in range(2):
+        bank = "B%d" % b
+        mms([(T[bank][:, 64 * y:64 * y + 64], sel(8 * b + y, d), T.HDB[:, 64 * d:64 * d + 64], d == 0, d == 1, 64)
+             for y in range(8) for d in (0, 1)], [W("MIP"), W("HDB")], [(bank, 0, 512)])
+        act(T.HT[:, 512 * b:512 * b + 512], T[bank][:], F.Copy, 512, [(bank, 0, 512)], [("HT", 512 * b, 512 * b + 512)])
+
+    def lists(tp):
+        b0 = 16 * tp
+        zr = ("Z", 32 * b0, 32 * b0 + 512)
+        cp(T.Z[:, b0:b0 + 16, 0:16], T.ZL[:, b0:b0 + 16, :], 256, [W("ZL")], [zr])
+        cp(T.Z[:, b0:b0 + 16, 16:32], T.ZR[:, b0:b0 + 16, :], 256, [W("ZR")], [zr])
+        for b in range(b0, b0 + 16):
+            vec(lambda q, b=b: q.transpose(T.ZT[:, :, b], T.Z[:, b, :]), 32, [zr], [("ZT", 512 * tp, 512 * tp + 512)])
+
+    def permute(t):
+        tp, h = t % 2, t // 2
+        cp(T.LT[:, 256 * t:256 * t + 256], T.ZT[:, 16 * h:16 * h + 16, 16 * tp:16 * tp + 16], 256,
+           [("ZT", 512 * tp, 512 * tp + 512)], [("LT", 256 * t, 256 * t + 256)])
+
+    cores = T.cores
+
+    def rel(src, dst):
+        return (src - dst) % NR
+
+    def addr(dst):
+        return topo.addr(cores[dst])[0:2]
+    onchip = [r for r in range(NR) if r != rank and topo.chip(cores[r]) == topo.chip(core)][0]
+    far = [r for r in range(NR) if topo.chip(cores[r]) != topo.chip(core)]
+    cross = topo.engines(core, cores[far[0]])
+    local = [e for e in topo.engines(core, cores[onchip]) if e not in cross]
+    wide = local + cross
+    bulk = []
+
+    def emask(es):
+        return sum(1 << e for e in es)
+
+    def send(src, h, dst, es):
+        s = "ls%d" % nxt("ls", 99)
+        rid, pid = addr(dst)
+        buf = "NB%d" % rel(src, rank)
+        out = T["NB%d" % rel(src, dst)][:, HALF * h:HALF * h + HALF]
+        in_ = T[buf][:, HALF * h:HALF * h + HALF]
+        rs = T.sem["n%d_%d" % (rel(src, dst), h)]
+        bulk.append(add(gr, "G", lambda q: q.remote_dma(out, in_, rs, T.sem[s], pid, rid, emask(es)), 0.8,
+                        [(buf, HALF * h, HALF * h + HALF)], [], "s", s, len(es), 6.0, soft=bulk[-1:]))
+
+    def recv(src, h, est, n):
+        a = rel(src, rank)
+        add(gr, "R", None, 0.0, [], [("NB%d" % a, HALF * h, HALF * h + HALF)], "r", "n%d_%d" % (a, h), n, est=est)
+
+    first = rank if (rank - 1) % NR in far else onchip
+    o_first = [r for r in far if (r - 1) % NR not in far][0]
+    o_second = [r for r in far if r != o_first][0]
+    gate, mygate = (first - 1) % NR, (o_first - 1) % NR
+    nown = len(wide) if rank == first else len(local)
+    recv(onchip, 1, 10.0, nown)
+    recv(onchip, 0, 14.0, nown)
+    late = 0.0 if rank == mygate else 6.0
+    nin = len(cross) if rank == mygate else len(wide)
+    for src, e in ((o_first, 24.0), (o_second, 34.0)):
+        for h in range(2):
+            recv(src, h, e + late, nin)
+    if rank == first:
+        for h in range(2):
+            send(rank, h, gate, cross)
+        for h in range(2):
+            send(rank, h, onchip, local)
+    else:
+        for h in range(2):
+            send(rank, h, onchip, wide)
+        for h in range(2):
+            send(rank, h, gate, cross)
+    if rank == mygate:
+        for src in (o_first, o_second):
+            for h in range(2):
+                send(src, h, onchip, wide)
+
+    def shares(t):
+        fv, n, kb = "FVT%d" % t, 1024 + 256 * t, W("KEY1")
+        for ch in sorted(range(4), key=lambda x: x not in SHARE_V):
+            c = 256 * t + 64 * ch
+            if ch in SHARE_V:
+                x = "XH%d" % (ch // 2)
+                tt(T[x][:], T.FE[:, 0:n].indirect(T.LT[:, c:c + 64]), T[fv][:, 0:1024], A.min, 1024 * GC,
+                   [W("FE"), ("LT", c, c + 64), W(fv)], [W(x)])
+                extract("KEY1", 64 * ch, "ES1", x, True, True, reg=kb)
+            else:
+                x, s = "GH%d" % (ch % 2), "SH%d" % (ch % 2)
+                for u, o in pieces(1024, c):
+                    act(T[x][:, u], T.FE[:, 0:n].indirect(T.LT[:, o]), F.Copy, (u.stop - u.start) * GC,
+                        [W("FE"), ("LT", o.start, o.stop)], [(x, u.start, u.stop)])
+                    subtract("B5", fv, u, x)
+                    act(T[s][:, u], T.B5[:], F.Abs, u.stop - u.start, [W("B5")], [(s, u.start, u.stop)])
+                extract("KEY1", 64 * ch, "ES5", fv, True, False, reg=kb)
+                extract("KEY1", 64 * ch, "ES5", x, False, False, reg=kb)
+                extract("KEY1", 64 * ch, "ESN", s, False, True, reg=kb)
+        c = slice(256 * t, 256 * t + 256)
+        tt(T.SW[:, c], T.KEY1[:, 0:256], T.TW[:], A.add, 256, [kb, W("TW")], [("SW", c.start, c.stop)])
+        tt(T.SL[:, c], T.TW[:], T.KEY1[:, 0:256], A.subtract, 256, [kb, W("TW")], [("SL", c.start, c.stop)])
+
+    def square(sl):
+        r = sl.start, sl.stop
+        act(T.SQ[:, sl], T.C32[:, sl], F.Square, r[1] - r[0], [("C32",) + r, SQB], [("SQ",) + r], bias=T.PF[:, 5:6], scale=1.0 / 32)
+
+    def gather_headings(t):
+        n = 1024 + 256 * t
+        for k0, kn, _, eng in CHUNKS:
+            c, w = 256 * t + 16 * k0, 16 * kn
+            x = "XV%d" % nxt("x", 4) if eng == "V" else "GS%d" % nxt("s", 4)
+            for u, o in pieces(16 * w, c):
+                src, m = T.HT[:, 0:n].indirect(T.LT[:, o]), (u.stop - u.start) * GC
+                rd, wr = [("HT", 0, n), ("LT", o.start, o.stop)], [(x, u.start, u.stop)]
+                if eng == "V":
+                    cp(T[x][:, u], src, m, rd, wr)
+                else:
+                    act(T[x][:, u], src, F.Copy, m, rd, wr)
+            bank = "B%d" % nxt("b", 3)
+            extract(bank, 0, "E1", x, True, True, w)
+            sl = slice(16 * k0, 16 * k0 + w)
+            cp(T.CL0[:, sl], T[bank][:, 0:w], w, [(bank, 0, w)], [("CL0", sl.start, sl.stop)])
+            act(T.C32[:, sl], T[bank][:, 0:w], F.Identity, w, [(bank, 0, w), MOFF], [("C32", sl.start, sl.stop)],
+                bias=T.PF[:, 7:8], scale=32.0)
+            square(sl)
+
+    def visits(t):
+        fv = "FVT%d" % t
+        for a in range(NR):
+            nb, cl, cln = "NB%d" % a, "CL%d" % (a % 2), "CL%d" % (1 - a % 2)
+            if a > 0 and t > 0:
+                apply_update(t - 1, a)
+            for k0, kn, eng, _ in CHUNKS:
+                w = 16 * kn
+                e16 = 16 * w
+                sl = slice(16 * k0, 16 * k0 + w)
+                bank = "B%d" % nxt("b", 3)
+                win = T[nb][:, 0:H]
+
+                def C(n):
+                    return (n, sl.start, sl.stop)
+                if eng == "V":
+                    x, kb = "XV%d" % nxt("x", 4), "KV"
+                    for u, o in pieces(e16, sl.start):
+                        tt(T[x][:, u], win.indirect(T[cl][:, o]), T[fv][:, u], A.is_lt, (u.stop - u.start) * GC,
+                           [(nb, 0, H), (cl, o.start, o.stop), W(fv)], [(x, u.start, u.stop)])
+                    extract(bank, 0, "E1", x, True, True, w)
+                else:
+                    j = nxt("s", 4)
+                    x, s, kb = "GS%d" % j, "SS%d" % j, "KW"
+                    for u, o in pieces(e16, sl.start):
+                        act(T[x][:, u], win.indirect(T[cl][:, o]), F.Copy, (u.stop - u.start) * GC,
+                            [(nb, 0, H), (cl, o.start, o.stop)], [(x, u.start, u.stop)])
+                    for hh, (u, _) in enumerate(pieces(e16, 0)):
+                        db = "B%d" % (3 + hh)
+                        subtract(db, fv, u, x)
+                        act(T[s][:, u], T[db][:, 0:u.stop - u.start], F.Sign, u.stop - u.start, [W(db), HLF], [(s, u.start, u.stop)],
+                            bias=T.PF[:, 6:7])
+                    extract(bank, 0, "E05", s, True, True, w)
+                P, pr, kc = T[bank][:, 0:w], (bank, 0, w), 4 * t + a
+                ts(P, P, float(SLOPE), A.mult, w, [pr, (kb, kc, kc + 1)], [pr], T[kb][:, kc:kc + 1], A.add)
+                tt(P, P, T.SQ[:, sl], A.add, w, [pr, C("SQ")], [pr])
+                tt(T.TI[:, sl], P, T.C32[:, sl], A.max, w, [pr, C("C32")], [C("TI")])
+                ts(T.CI[:, sl], T.TI[:, sl], 5, A.arith_shift_right, w, [C("TI")], [C("CI")], 4095, A.bitwise_and)
+                if a < NR - 1:
+                    cp(T[cln][:, sl], T.CI[:, sl], w, [C("CI")], [C(cln)])
+                    ts(T.C32[:, sl], T.CI[:, sl], 32.0, A.mult, w, [C("CI")], [C("C32")], float(-OFF), A.add)
+                    square(sl)
+                else:
+                    cp(T.CW[:, sl], T.CI[:, sl], w, [C("CI")], [C("CW")])
+
+    def election(t):
+        C2, kr, z = ("B2", 0, 256), ("KEY0", 0, 256), slice(256 * t, 256 * t + 256)
+        act(T.B2[:, 0:256], T.CW[:, 0:256], F.Copy, 256, [("CW", 0, 256)], [C2])
+        act(T.CW[:, 256:384], T.CW[:, 0:128], F.Copy, 128, [("CW", 0, 128)], [("CW", 256, 384)])
+
+        def K(a, b):
+            return T.KEY0[:, a:b]
+        for d in range(1, 9):
+            n, s, e = (256 if d < 8 else 128), 16 * d, ("EQ", 256 * d, 256 * d + 256)
+            tt(T.EQ[:, d, 0:n], T.B2[:, 0:n], T.CW[:, s:s + n], A.is_equal, n, [C2, ("CW", s, s + n)], [e])
+            lst = [(K(0, n), T.IDK[:], T.EQ[:, d, 0:n], d == 1, False, n),
+                   (K(s, 256), T.IDK[:], T.EQ[:, d, 0:256 - s], False, d == 8, 256 - s)]
+            if d < 8:
+                lst.append((K(0, s), T.IDK[:], T.EQ[:, d, 256 - s:256], False, False, s))
+            mms(lst, [e, W("IDK")], [kr])
+        tt(T.KK[:, 256:512], T.SL[:, z], K(0, 256), A.subtract, 256, [("SL", z.start, z.stop), kr], [("KK", 256, 512)])
+        tt(T.KK[:, 0:256], K(0, 256), T.SW[:, z], A.add, 256, [("SW", z.start, z.stop), kr], [("KK", 0, 256)])
+
+        def tree(src, w, out, oc):
+            n, s, so = 128, src, 256 * w
+            for m in ("M1", "M2", "M3", None):
+                dst, do = (out, oc) if m is None else (m, n * w)
+                tt(T[dst][:, do:do + n], T[s][:, so:so + n], T[s][:, so + n:so + 2 * n], A.max, 2 * n, [(s, so, so + 2 * n)], [(dst, do, do + n)])
+                n, s, so = n // 2, dst, do
+        tree("KK", 1, "B4", 0)
+        tree("KK", 0, "B3", 0)
+        n = 16
+        while n < 256:
+            for b in ("B4", "B3"):
+                cp(T[b][:, n:2 * n], T[b][:, 0:n], n, [(b, 0, n)], [(b, n, 2 * n)])
+            n *= 2
+        for b, w in (("B4", 1), ("B3", 0)):
+            c = slice(256 * w, 256 * w + 256)
+            q = ("DD", c.start, c.stop)
+            tt(T.DD[:, c], T.KK[:, c], T[b][:, 0:256], A.subtract, 256, [("KK", c.start, c.stop), (b, 0, 256)], [q])
+            tt(T.DD[:, c], T.DD[:, c], T.B2[:, 0:256], A.add, 256, [q, C2], [q])
+            tree("DD", w, "WLI", 16 * w)
+        for w in (1, 0):
+            rd, o = ("WLI", 16 * w, 16 * w + 16), 32 * w
+            for d, m in ((0, 4080), (16, 15)):
+                ts(T.SPI[:, o + d:o + d + 16], T.WLI[:, 16 * w:16 * w + 16], m, A.bitwise_and, 16, [rd], [("SPI", o + d, o + d + 16)])
+            cp(T.SPB[:, o:o + 32], T.SPI[:, o:o + 32], 32, [("SPI", o, o + 32)], [("SPB", o, o + 32)])
+        for n in ("LF", "LU"):
+            cp(T[n][:], T.WLI[:, 16:32], 16, [("WLI", 16, 32)], [W(n)])
+
+    def headings_out(t, soft=()):
+        mms([(T.B0[:, i:256:16], sel(i, d), T.SPB[:, 16 * d:16 * d + 16], d == 0, d == 1, 16) for i in range(16) for d in (0, 1)],
+            [("SPB", 0, 32), W("MIP")], [("B0", 0, 256)], soft)
+        c = 1024 + 256 * t
+        act(T.HT[:, c:c + 256], T.B0[:, 0:256], F.Copy, 256, [("B0", 0, 256)], [("HT", c, c + 256)])
+
+    def write_yh(t):
+        c, y = 1024 + 256 * t, ("YH8", 256 * t, 256 * t + 256)
+        mms([(T.B5[0:8, 0:256], T.BMW[:, 0:128:16], T.HT[:, c:c + 256], True, True, 256)], [W("BMW"), ("HT", c, c + 256)], [("B5", 0, 256)])
+        act(T.YH8[:, 256 * t:256 * t + 256], T.B5[0:8, 0:256], F.Copy, 256, [("B5", 0, 256)], [y])
+        dma("Y", T.yh[:, 256 * t:256 * t + 256], T.YH8[:, 256 * t:256 * t + 256], 2.5, [y], [])
+
+    def notes(t):
+        fv, ov, ol = "FVT%d" % t, "OUTV%d" % t, "OUTL%d" % t
+        b1, b3, b4 = ("B1", 0, 256), ("B3", 0, 256), ("B4", 0, 256)
+        act(T.OLD[:], T.NB0[:, 0:H].indirect(T.LU[:, 0:16]), F.Copy, 256 * GC, [("NB0", 0, H), W("LU")], [W("OLD")])
+        mms([(T.B3[:, 0:256], T.ID[:], T[fv][:, 0:256], True, False, 256), (T.B3[:, 0:256], T.IDN[:], T.OLD[:], False, True, 256)],
+            [W("ID"), W("IDN"), W(fv), W("OLD")], [b3])
+        ts(T.DC[:], T.B3[:, 0:256], 32.0, A.min, 256, [b3], [W("DC")], -32.0, A.max)
+        mms([(T.B4[:, 0:256], T.ID[:], T.OLD[:], True, False, 256), (T.B4[:, 0:256], T.ID[:], T.DC[:], False, True, 256)],
+            [W("ID"), W("OLD"), W("DC")], [b4])
+        act(T[ov][:, 0:256], T.B4[:, 0:256], F.Copy, 256, [b4], [(ov, 0, 256)])
+        mms([(T.B1[:, i:256:16], T.BI[:, 128 * i:128 * i + 128], T.SPB[:, 32 + 16 * d:48 + 16 * d], d == 0, d == 1, 16)
+             for i in range(16) for d in (0, 1)], [("SPB", 32, 64), W("BI")], [b1])
+        cp(T.LB[:], T.B1[:, 0:256], 256, [b1], [W("LB")])
+        for lo in (0, 8):
+            er = ("EQT", 256 * lo, 256 * lo + 2048)
+            for mb in range(lo, lo + 8):
+                n = 256 - 16 * mb
+                ts(T.EQT[:, mb, 0:n], T.LB[:, 16 * mb:256], T.LF[:, mb:mb + 1], A.is_equal, n * 0.5, [W("LB"), W("LF")], [("EQT", 256 * mb, 256 * mb + 256)])
+            tt(T.EQT[:, lo:lo + 8, 0:16], T.EQT[:, lo:lo + 8, 0:16], T.TRI[:, lo:lo + 8, :], A.mult, 256, [er, W("TRI")], [er])
+            mms([(T.B1[:, 16 * mb:256], T.BMW[:], T.EQT[:, mb, 0:256 - 16 * mb], mb == 0, mb == 15, 256 - 16 * mb) for mb in range(lo, lo + 8)],
+                [W("BMW"), er], [b1])
+        ts(T.FL[:], T.B1[:, 0:256], 0.5, A.is_gt, 256, [b1], [W("FL")])
+        mms([(T.B1[:, 256:272], T.EX[:, 15 - i:143 - i], T.FL[:, i:256:16], i == 0, i == 15, 16) for i in range(16)],
+            [W("EX"), W("FL")], [("B1", 256, 272)])
+        tt(T.DL[:], T.DUP[:], T.LF[:], A.subtract, 32, [W("DUP"), W("LF")], [W("DL")])
+        tt(T.OF[:], T.B1[:, 256:272], T.DL[:], A.mult, 32, [("B1", 256, 272), W("DL")], [W("OF")])
+        tt(T.OF[:], T.OF[:], T.LF[:], A.add, 32, [W("OF"), W("LF")], [W("OF")])
+        cp(T[ol][:], T.OF[:], 16, [W("OF")], [W(ol)])
+        scatter("NB0", ov, ol)
+
+    def scatter(nb, ov, ol):
+        vec(lambda q: q.tensor_copy(out=T[nb][:, 0:H + DUMMY].indirect(T[ol][:, 0:16]), in_=T[ov][:, 0:256]), 256 * 3,
+            [(ov, 0, 256), W(ol)], [(nb, 0, H + DUMMY)])
+
+    def bias(t, a, src):
+        c = 4 * (t + 1) + a
+        for kb in ("KV", "KW"):
+            act(T[kb][:, c:c + 1], T[src][:, 256:257], F.Identity, 1, [(src, 256, 257), (kb, 0, 1)], [(kb, c, c + 1)], bias=T[kb][:, 0:1], scale=32.0)
+
+    def kappa(t):
+        ov = "OUTV%d" % t
+        mms([(T.B0[:, 0:32], T.ONES[:], T.SPB[:, 0:32], True, True, 32)], [W("ONES"), ("SPB", 0, 32)], [("B0", 0, 32)])
+        act(T.JUNK[:], T.B0[:, 0:32], F.Copy, 32, [("B0", 0, 32)], [W("KS1"), W("JUNK")], accum=T.KS1[:, 0:1])
+        cp(T.KI[:, 0:1], T.KS1[:, 0:1], 1, [W("KS1")], [W("KI")])
+        ts(T.KJ[:, 0:1], T.KI[:, 0:1], 255, A.bitwise_and, 1, [W("KI")], [W("KJ")])
+        cp(T[ov][:, 256:257], T.KJ[:, 0:1], 1, [W("KJ")], [(ov, 256, 257)])
+        bias(t, 0, ov)
+
+    sent = {}
+
+    def send_update(t):
+        dsts = [(rank - a) % NR for a in range(1, NR)]
+        ids = [DstId(rid=addr(x)[0], pnc=addr(x)[1]) for x in dsts]
+        for nm, inn, sm in (("OUTL%d" % t, "INL%d_%d", "il%d_%d"), ("OUTV%d" % t, "INV%d_%d", "iv%d_%d")):
+            def f(q, nm=nm, inn=inn, sm=sm):
+                tr = RemoteDMATransfer(dst_ids=ids, dma_engine_mask=emask(cross), remote_sem=T.sem[sm % (rank, t)], srcs=[T[nm][:]],
+                                       dsts=[T[inn % (rel(rank, x), t)][:] for x in dsts])
+                return q.remote_dma_fused([tr], local_sem=T.sem.lsend)
+            num["lsend"] += len(cross)
+            bulk.append(add(gr, "G", f, 1.2, [W(nm)], [], "s", "lsend", num["lsend"], soft=bulk[-1:]))
+        sent[t] = bulk[-1]
+
+    def apply_update(t, a):
+        iv, il = "INV%d_%d" % (a, t), "INL%d_%d" % (a, t)
+        src = (rank + a) % NR
+        for nm, sm in ((il, "il%d_%d"), (iv, "iv%d_%d")):
+            gr["nodes"][add(gr, "R", None, 0.0, [], [W(nm)], "r", sm % (src, t), len(cross), 3.5)]["soft"].add(sent[t])
+        bias(t, a, iv)
+        scatter("NB%d" % a, iv, il)
+
+    lists(0)
+    permute(0)
+    gather_headings(0)
+    first_v = len(gr["nodes"]) - 1
+    lists(1)
+    shares(0)
+    for t in range(1, RT):
+        permute(t)
+        load_tiles(t, [first_v])
+        shares(t)
+    for t in range(RT):
+        visits(t)
+        election(t)
+        if t + 1 < RT:
+            headings_out(t)
+            notes(t)
+            gather_headings(t + 1)
+            kappa(t)
+            send_update(t)
+        else:
+            notes(t)
+            headings_out(t, [len(gr["nodes"]) - 1])
+        write_yh(t)
+    for j, e in ((0, "S"), (1, "Y")):
+        dma(e, T.yl[:, HALF * j:HALF * j + HALF], T.NB0[:, HALF * j:HALF * j + HALF], 5.0, [("NB0", HALF * j, HALF * j + HALF)], [])
+    return gr
+
+
+def rank_program(g, core, T, topo):
+    if T.rank_of(core) is None:
+        return
+    gr = build(core, T, topo)
+    emit_all(gr, schedule(gr), g, T)

@@ -8,13 +8,15 @@ SLOPE = 613 * 32 + MOD * KS
 OFF = MOD * 512
 BV = -256 - MOD * (9 * KS + 1) - OFF
 BS = BV + 8 * SLOPE
-CHUNKS = ((0, 4, "V", "V"), (4, 4, "S", "S"), (8, 5, "V", "S"), (13, 3, "S", "S"))
-SHARE_V = (0, 2)
+CHUNKS = ((0, 72, "V", "S", "V"), (72, 56, "S", "S", "V"), (128, 72, "V", "S", "V"), (200, 56, "S", "S", "V"))
+SHARE = ("VS", "VS", "VS", "VS")
+EXPAND = "VVVVVVVVVVVVGGGG"
 PIECE = 512
-CYC, GC, PEC = 0.83e-3 * 1.25, 1.56, 0.68e-3
+BIG = float(1 << 24)
+CYC, GC, PEC = 0.83e-3 * 1.25, 1.56, 0.6e-3
 
 SCRATCH = {}
-SEMAPHORES = ["cv", "cs", "cp", "cg", "lsend"] + ["d%d" % j for j in range(52)] + ["ls%d" % j for j in range(10)]
+SEMAPHORES = ["cv", "cs", "cp", "cg", "lsend"] + ["d%d" % j for j in range(30)] + ["ls%d" % j for j in range(10)]
 
 
 def _buf(names, cols, dtype, where="sbuf", rows=128):
@@ -25,7 +27,8 @@ def _buf(names, cols, dtype, where="sbuf", rows=128):
 B16, F32, I32, U16 = "bfloat16", "float32", "int32", "uint16"
 _buf("NB0 NB1 NB2 NB3", H + DUMMY, B16)
 _buf("FE HT", 2048, B16)
-_buf("FVT0 FVT1 FVT2 FVT3 XV0 XV1 XV2 XV3 GS0 GS1 GS2 GS3", 1280, B16)
+_buf("FX0 FX1 FX2 FX3 XH0 XH1 XH2 XH3", 4096, B16)
+_buf("XV0 XV1 XV2 GS0 GS1 GS2 GS3 SS0 SS1 SS2 SS3", 16 * max(c[1] for c in CHUNKS), B16)
 _buf("OUTV0 OUTV1 OUTV2 OUTV3", 264, B16)
 _buf("OUTL0 OUTL1 OUTL2 OUTL3 LU", 16, U16)
 for _t in range(RT - 1):
@@ -36,40 +39,35 @@ for _t in range(RT - 1):
             _buf("INL%d_%d" % (_a, _t), 16, U16)
 for _a in range(1, NR):
     SEMAPHORES += ["n%d_0" % _a, "n%d_1" % _a]
-_buf("ZL ZR", [32, 16], I32)
-_buf("Z ZT", [32, 32], I32)
+_buf("CMP", 1024, I32)
 _buf("LT", 1024, U16)
-_buf("HD SPI", 64, I32)
-_buf("HDI", 128, I32)
-_buf("HDB BMW ID IDN IDK ONES", 128, B16)
+_buf("HD", 64, I32)
+_buf("HDB BMW BMN BO BD ID IDN IDK", 128, B16)
 _buf("RI", 160, F32)
-_buf("RG", 128, F32)
+_buf("RG ONES", 128, F32)
 _buf("PI PM PG KI KJ", 2, I32)
-_buf("PF", 8, F32)
-_buf("MK DUP KV KW LF DL OF", 16, F32)
+_buf("PF", 16, F32)
+_buf("MK DUP LF OF", 16, F32)
+_buf("KV", 32, F32)
 _buf("MB", 160, B16)
 _buf("MIP", 16 * 160, B16)
-_buf("BI", 16 * 128, B16)
-_buf("E1 E05 ES1 ES5 ESN EX", 144, B16)
-_buf("FL OLD DC", 256, B16)
-_buf("SW SL", 1024, F32)
-_buf("TW C32 SQ M1", 256, F32)
-_buf("TRI", [16, 16], B16)
-_buf("SS0 SS1 SS2 SS3 XH0 XH1 GH0 GH1 SH0 SH1", 1024, B16)
+_buf("E1 E05 EX", 144, B16)
+_buf("FL OLD DC LR WB0 WB1", 256, B16)
+_buf("C32 SQ CW THR PW", 256, F32)
+_buf("GH0 GH1", PIECE, B16)
 _buf("CL0 CL1 LB", 256, U16)
 _buf("TI CI", 256, I32)
-_buf("CW", 384, F32)
-_buf("EQ", [9, 256], B16)
+_buf("IDW", [8, 24], F32)
+_buf("DF", [8, 17], F32)
+_buf("CD", [16, 16], F32)
+_buf("RST0 RST1 RUN0 RUN1 GO0 GO1 PICK0 PICK1", 272, F32)
+_buf("EQ", [3, 16, 40], B16)
+_buf("ENDS", 32, B16)
 _buf("EQT", [16, 256], B16)
-_buf("KK DD", 512, F32)
-_buf("M2", 128, F32)
-_buf("M3", 64, F32)
-_buf("WLI", 32, I32)
-_buf("SPB", 64, B16)
 _buf("KS1", 2, F32)
-_buf("JUNK", 32, F32)
 _buf("YH8", 1024, F32, rows=8)
-_buf("B0 B1 B2 B3 B4 B5 KEY0 KEY1", 512, F32, "psum")
+_buf("B0 B1 B2 B3 B4 B5 KEY", 512, F32, "psum")
+_buf("CT", [16, 32], F32, "psum")
 PSUM = set(n for n in SCRATCH if SCRATCH[n][0] == "psum")
 CSEM = {"V": "cv", "S": "cs", "P": "cp", "G": "cg"}
 
@@ -187,7 +185,7 @@ def emit_all(gr, order, g, T):
 def build(core, T, topo):
     rank = T.rank_of(core)
     gr = {"nodes": [], "acc": {}, "bank": {}}
-    num = {"d": 0, "ls": 0, "x": 0, "s": 0, "b": 0, "lsend": 0}
+    num = {"d": 0, "ls": 0, "x": 0, "s": 0, "b": 0, "h": 0, "u": 0, "lsend": 0}
     lastd = {}
 
     def nxt(k, n):
@@ -200,8 +198,8 @@ def build(core, T, topo):
     def vec(fn, cyc, reads, writes):
         return add(gr, "V", fn, max(64, cyc) * CYC + 0.04, reads, writes)
 
-    def gps(fn, cyc, writes):
-        return add(gr, "G", fn, cyc * CYC + 0.15, [], writes)
+    def gps(fn, cyc, writes, reads=()):
+        return add(gr, "G", fn, cyc * CYC + 0.17, reads, writes)
 
     def dma(eng, out, in_, lat, reads, writes, soft=()):
         s = "d%d" % nxt("d", 99)
@@ -218,6 +216,9 @@ def build(core, T, topo):
 
     def cp(out, in_, cyc, reads, writes):
         return vec(lambda q: q.tensor_copy(out=out, in_=in_), cyc, reads, writes)
+
+    def scan(out, d0, d1, op0, op1, cyc, reads, writes):
+        return vec(lambda q: q.tensor_tensor_scan(out, d0, d1, 0.0, op0, op1), cyc, reads, writes)
 
     def fill(ap, val, n, reg):
         vec(lambda q: q.memset(ap, val), n, [], [reg])
@@ -236,45 +237,40 @@ def build(core, T, topo):
             return ins
         return add(gr, "P", f, sum(max(64, x[5]) for x in lst) * PEC + 0.03, reads, writes, soft=soft)
 
-    def extract(bank, c0, en, x, start, stop, n=64, reg=None):
-        return mms([(T[bank][:, c0:c0 + n], T[en][:, 15 - i:143 - i], T[x][:, i:16 * n:16], start and i == 0, stop and i == 15, n)
-                    for i in range(16)], [(x, 0, 16 * n), W(en)], [reg or (bank, c0, c0 + n)])
+    def extract(bank, c0, en, x, n):
+        return mms([(T[bank][:, c0:c0 + n], T[en][:, 15 - i:143 - i], T[x][:, i:16 * n:16], i == 0, i == 15, n)
+                    for i in range(16)], [(x, 0, 16 * n), W(en)], [(bank, c0, c0 + n)])
 
-    def pieces(n, c):
-        return [(slice(j, min(n, j + PIECE)), slice(c + j // 16, c + min(n, j + PIECE) // 16)) for j in range(0, n, PIECE)]
+    def pieces(n):
+        return [(j, min(PIECE, n - j)) for j in range(0, n, PIECE)]
 
-    def subtract(bank, fv, u, x):
-        m = u.stop - u.start
-        mms([(T[bank][:, 0:m], T.ID[:], T[fv][:, u], True, False, m)], [W("ID"), W(fv)], [W(bank)])
-        mms([(T[bank][:, 0:m], T.IDN[:], T[x][:, u], False, True, m)], [W("IDN"), (x, u.start, u.stop)], [W(bank)])
+    def subtract(bank, fx, f0, x, x0, m):
+        mms([(T[bank][:, 0:m], T.ID[:], T[fx][:, f0:f0 + m], True, False, m)], [W("ID"), (fx, f0, f0 + m)], [W(bank)])
+        mms([(T[bank][:, 0:m], T.IDN[:], T[x][:, x0:x0 + m], False, True, m)], [W("IDN"), (x, x0, x0 + m)], [W(bank)])
 
-    dma("S", T.HD[:], T.hd[:], 2.2, [], [W("HD")])
-    for a in range(4):
-        for h in range(2):
-            r0 = 32 * a + 16 * h
-            for e, n, d in (("S", "ZL", 0), ("Y", "ZR", 16)):
-                dma(e, T[n][r0:r0 + 16], T.comp[32 * a + d:32 * a + d + 16, 512 * h:512 * h + 512], 6.5, [], [(n, r0, r0 + 1)])
+    def load(e, n, src, c0, c1, lat):
+        dma(e, T[n][:, c0:c1], T[src][:, c0:c1], lat, [], [(n, c0, c1)])
+    dma("Y", T.HD[:], T.hd[:], 2.2, [], [W("HD")])
+    load("S", "FE", "feat", 1024, 1280, 2.6)
+    load("S", "CMP", "comp", 0, 256, 3.2)
     for h in (0, 1):
-        dma("Y", T.NB0[:, HALF * h:HALF * h + HALF], T.lim[:, HALF * h:HALF * h + HALF], 11.0, [], [("NB0", HALF * h, HALF * h + HALF)])
-    dma("S", T.FVT0[:, 0:256], T.feat[:, 1024:1280], 13.0, [], [("FVT0", 0, 256)])
-    dma("S", T.FE[:], T.feat[:], 16.0, [], [W("FE")])
-
-    def load_tiles(t, soft):
-        for j in range(5):
-            dma("Y", T["FVT%d" % t][:, 256 * j:256 * j + 256], T.feat[:, 1024 + 256 * t:1280 + 256 * t],
-                4.0, [], [("FVT%d" % t, 256 * j, 256 * j + 256)], soft)
+        load("Y", "NB0", "lim", HALF * h, HALF * h + HALF, 6.0 + 2.5 * h)
+    load("S", "FE", "feat", 0, 1024, 10.0)
+    load("S", "FE", "feat", 1280, 2048, 11.0)
+    load("Y", "CMP", "comp", 256, 1024, 13.0)
 
     gps(lambda q: q.iota(T.PI[:, 0:1], [[1, 1]], 0, 1), 2, [W("PI")])
-    for n, pat, base, c in (("RI", [[1, 160]], 0, 320), ("RG", [[16, 8], [0, 16]], 0, 256),
-                            ("TW", [[-4096, 16], [0, 16]], 15 * 4096, 512), ("DUP", [[16, 16]], H, 32)):
-        gps(lambda q, n=n, pat=pat, base=base: q.iota(T[n][:], pat, base, 0, allow_small_or_imprecise_dtypes=True), c, [W(n)])
+    for ap, n, pat, base, c in ((T.RI[:], "RI", [[1, 160]], 0, 320), (T.RG[:], "RG", [[16, 8], [0, 16]], 0, 256),
+                                (T.IDW[:, :, 0:16], "IDW", [[16, 8], [1, 16]], 0, 256), (T.IDW[:, :, 16:24], "IDW", [[16, 8], [1, 8]], 0, 128),
+                                (T.DUP[:], "DUP", [[16, 16]], H, 32)):
+        gps(lambda q, ap=ap, pat=pat, base=base: q.iota(ap, pat, base, 0, allow_small_or_imprecise_dtypes=True), c, [W(n)])
     ts(T.PM[:, 0:1], T.PI[:, 0:1], 15, A.bitwise_and, 1, [W("PI")], [W("PM")])
     ts(T.PG[:, 0:1], T.PI[:, 0:1], 112, A.bitwise_and, 1, [W("PI")], [W("PG")])
     for c, s, d in ((0, "PI", 0), (1, "PM", 0), (2, "PG", 0), (3, "PI", 16), (4, "PG", 15)):
         ts(T.PF[:, c:c + 1], T[s][:, 0:1], d, A.add, 1, [W(s)], [("PF", c, c + 1)])
-    for c, v in ((5, OFF // 32 + 16), (6, -0.5), (7, -OFF)):
+    for c, v in ((5, OFF // 32 + 16), (6, -0.5), (7, -OFF), (8, 16)):
         fill(T.PF[:, c:c + 1], float(v), 1, ("PF", c, c + 1))
-    SQB, HLF, MOFF = ("PF", 5, 6), ("PF", 6, 7), ("PF", 7, 8)
+    SQB, HLF, MOFF, P16, P2 = ("PF", 5, 6), ("PF", 6, 7), ("PF", 7, 8), ("PF", 8, 9), ("PF", 9, 10)
 
     def eqc(name, n, col, val, src="RI"):
         ts(T[name][:, 0:n], T[src][:, 0:n], T.PF[:, col:col + 1], A.is_equal, n, [W(src), ("PF", col, col + 1)], [W(name)], val, A.mult)
@@ -283,27 +279,41 @@ def build(core, T, topo):
     for y in range(16):
         act(T.MIP[:, 160 * y:160 * y + 160], T.MB[:], F.Copy, 160, [W("MB"), W("MK")], [("MIP", 160 * y, 160 * y + 160)],
             scale=T.MK[:, y:y + 1], soft=[lastd["S"]])
-    for n, v in (("E1", 1.0), ("ES1", 65536.0), ("E05", 0.5), ("EX", 0.0625), ("ES5", 32768.0), ("ESN", -32768.0)):
+    for n, v in (("E1", 1.0), ("E05", 0.5), ("EX", 0.0625)):
         eqc(n, 144, 4, v)
-    for n, v in (("ID", 1.0), ("IDN", -1.0), ("IDK", float(1 << 28))):
+    for n, v in (("ID", 1.0), ("IDN", -1.0), ("IDK", 4096.0)):
         eqc(n, 128, 0, v)
-    eqc("BMW", 128, 2, 1.0, "RG")
+    for n, v in (("BMW", 1.0), ("BMN", -1.0), ("BO", 2.0)):
+        eqc(n, 128, 2, v, "RG")
     ts(T.DUP[:], T.DUP[:], T.PF[:, 1:2], A.add, 16, [W("DUP"), ("PF", 1, 2)], [W("DUP")])
     for y in range(16):
-        act(T.BI[:, 128 * y:128 * y + 128], T.BMW[:], F.Copy, 128, [W("BMW"), W("MK")], [("BI", 128 * y, 128 * y + 128)],
-            scale=T.MK[:, y:y + 1], soft=[lastd["S"]])
-        ts(T.TRI[:, y, :], T.RI[:, 0:16], T.PF[:, 1:2], A.is_gt, 16, [W("RI"), ("PF", 1, 2)], [("TRI", 16 * y, 16 * y + 16)])
-    fill(T.ONES[:], 1.0, 64, W("ONES"))
-    fill(T.KV[:, 0:4], float(BV), 4, ("KV", 0, 4))
-    fill(T.KW[:, 0:4], float(BS), 4, ("KW", 0, 4))
+        fill(T.THR[:, y:256:16], 2.0 ** (1 - y), 16, W("THR"))
+    tt(T.PW[:, 0:16], T.THR[:, 0:16], T.MK[:], A.mult, 32, [W("THR"), W("MK")], [W("PW")])
+    act(T.PW[:, 16:32], T.PW[:, 0:16], F.Copy, 16, [W("PW")], [W("PW"), P2], scale=0.5, accum=T.PF[:, 9:10])
+    ts(T.BD[:], T.BMW[:], T.PF[:, 9:10], A.mult, 64, [W("BMW"), P2], [W("BD")])
+    ts(T.IDW[:], T.IDW[:], T.PF[:, 0:1], A.is_equal, 192, [W("IDW"), ("PF", 0, 1)], [W("IDW")])
+    fill(T.DF[:], 0.0, 136, W("DF"))
+    ts(T.DF[:, :, 0:16], T.IDW[:, :, 0:16], -1.0, A.mult, 128, [W("IDW")], [W("DF")])
+    tt(T.DF[:, :, 1:17], T.DF[:, :, 1:17], T.IDW[:, :, 0:16], A.add, 256, [W("IDW"), W("DF")], [W("DF")])
+    for w in (0, 1):
+        fill(T["RST%d" % w][:], 0.0, 256, W("RST%d" % w))
+        for c in (slice(0, 1), slice(16, 272, 17)):
+            fill(T["RST%d" % w][:, c], BIG if w else -BIG, 16, W("RST%d" % w))
+        fill(T["GO%d" % w][:, 0:1], 0.0, 16, W("GO%d" % w))
+        fill(T["WB%d" % w][:], 0.0, 128, W("WB%d" % w))
+        fill(T.ENDS[:, 16 * w:16 * w + 16], BIG / 16 if w else -BIG / 16, 16, W("ENDS"))
+    fill(T.EQ[:], 0.0, 960, W("EQ"))
+    fill(T.ONES[:], 32.0, 128, W("ONES"))
+    fill(T.KV[:, 0:8:2], float(BV), 4, ("KV", 0, 8))
+    fill(T.KV[:, 1:8:2], float(BS), 4, ("KV", 0, 8))
     for t in range(RT - 1):
         fill(T["OUTV%d" % t][:, 256:264], 0.0, 4, ("OUTV%d" % t, 256, 264))
-    for c0, c1, w in ((256, 512, 256), (512, 1024, 512), (1024, 1280, 256)):
-        cp(T.FVT0[:, c0:c1], T.FVT0[:, 0:w], w // 2, [("FVT0", 0, w)], [("FVT0", c0, c1)])
 
-    ts(T.HDI[:, 0:64], T.HD[:], 4080, A.bitwise_and, 64, [W("HD")], [("HDI", 0, 64)])
-    ts(T.HDI[:, 64:128], T.HD[:], 15, A.bitwise_and, 64, [W("HD")], [("HDI", 64, 128)])
-    cp(T.HDB[:], T.HDI[:], 128, [W("HDI")], [W("HDB")])
+    def hilo(dst, hi, lo, src, n, reads):
+        cp(hi, src, n, reads, [W(dst)])
+        tt(lo, src, hi, A.subtract, 2 * n, reads + [W(dst)], [W(dst)])
+
+    hilo("HDB", T.HDB[:, 0:64], T.HDB[:, 64:128], T.HD[:], 64, [W("HD")])
 
     def sel(i, d):
         return T.MIP[:, 160 * i + 16 + i - d:160 * i + 144 + i - d]
@@ -313,18 +323,23 @@ def build(core, T, topo):
              for y in range(8) for d in (0, 1)], [W("MIP"), W("HDB")], [(bank, 0, 512)])
         act(T.HT[:, 512 * b:512 * b + 512], T[bank][:], F.Copy, 512, [(bank, 0, 512)], [("HT", 512 * b, 512 * b + 512)])
 
-    def lists(tp):
-        b0 = 16 * tp
-        zr = ("Z", 32 * b0, 32 * b0 + 512)
-        cp(T.Z[:, b0:b0 + 16, 0:16], T.ZL[:, b0:b0 + 16, :], 256, [W("ZL")], [zr])
-        cp(T.Z[:, b0:b0 + 16, 16:32], T.ZR[:, b0:b0 + 16, :], 256, [W("ZR")], [zr])
-        for b in range(b0, b0 + 16):
-            vec(lambda q, b=b: q.transpose(T.ZT[:, :, b], T.Z[:, b, :]), 32, [zr], [("ZT", 512 * tp, 512 * tp + 512)])
+    def lists(t):
+        c = 256 * t
+        cp(T.LT[:, c:c + 256], T.CMP[:, c:c + 256], 256, [("CMP", c, c + 256)], [("LT", c, c + 256)])
 
-    def permute(t):
-        tp, h = t % 2, t // 2
-        cp(T.LT[:, 256 * t:256 * t + 256], T.ZT[:, 16 * h:16 * h + 16, 16 * tp:16 * tp + 16], 256,
-           [("ZT", 512 * tp, 512 * tp + 512)], [("LT", 256 * t, 256 * t + 256)])
+    def expand(t):
+        fx, c = "FX%d" % t, 1024 + 256 * t
+        done = []
+        for k in range(16):
+            out, in_, rd, wr = T[fx][:, k:4096:16], T.FE[:, c:c + 256], [("FE", c, c + 256)], [(fx + "k", k, k + 1)]
+            e = EXPAND[k] if t == 0 else "G"
+            if e == "G":
+                done.append(gps(lambda q, out=out, in_=in_: q.affine_select(out, in_, [[0, 256]], A.is_equal, 0.0, 0, 0), 512, wr, rd))
+            elif e == "V":
+                done.append(cp(out, in_, 128, rd, wr))
+            else:
+                done.append(act(out, in_, F.Copy, 256, rd, wr))
+        gr["acc"][fx] = [(j, 0, 4096, 1) for j in done]
 
     cores = T.cores
 
@@ -362,11 +377,11 @@ def build(core, T, topo):
     o_second = [r for r in far if r != o_first][0]
     gate, mygate = (first - 1) % NR, (o_first - 1) % NR
     nown = len(wide) if rank == first else len(local)
-    recv(onchip, 1, 10.0, nown)
+    recv(onchip, 1, 14.0, nown)
     recv(onchip, 0, 14.0, nown)
     late = 0.0 if rank == mygate else 6.0
     nin = len(cross) if rank == mygate else len(wide)
-    for src, e in ((o_first, 24.0), (o_second, 34.0)):
+    for src, e in ((o_first, 22.0), (o_second, 30.0)):
         for h in range(2):
             recv(src, h, e + late, nin)
     if rank == first:
@@ -385,199 +400,182 @@ def build(core, T, topo):
                 send(src, h, onchip, wide)
 
     def shares(t):
-        fv, n, kb = "FVT%d" % t, 1024 + 256 * t, W("KEY1")
-        for ch in sorted(range(4), key=lambda x: x not in SHARE_V):
-            c = 256 * t + 64 * ch
-            if ch in SHARE_V:
-                x = "XH%d" % (ch // 2)
-                tt(T[x][:], T.FE[:, 0:n].indirect(T.LT[:, c:c + 64]), T[fv][:, 0:1024], A.min, 1024 * GC,
-                   [W("FE"), ("LT", c, c + 64), W(fv)], [W(x)])
-                extract("KEY1", 64 * ch, "ES1", x, True, True, reg=kb)
-            else:
-                x, s = "GH%d" % (ch % 2), "SH%d" % (ch % 2)
-                for u, o in pieces(1024, c):
-                    act(T[x][:, u], T.FE[:, 0:n].indirect(T.LT[:, o]), F.Copy, (u.stop - u.start) * GC,
-                        [W("FE"), ("LT", o.start, o.stop)], [(x, u.start, u.stop)])
-                    subtract("B5", fv, u, x)
-                    act(T[s][:, u], T.B5[:], F.Abs, u.stop - u.start, [W("B5")], [(s, u.start, u.stop)])
-                extract("KEY1", 64 * ch, "ES5", fv, True, False, reg=kb)
-                extract("KEY1", 64 * ch, "ES5", x, False, False, reg=kb)
-                extract("KEY1", 64 * ch, "ESN", s, False, True, reg=kb)
-        c = slice(256 * t, 256 * t + 256)
-        tt(T.SW[:, c], T.KEY1[:, 0:256], T.TW[:], A.add, 256, [kb, W("TW")], [("SW", c.start, c.stop)])
-        tt(T.SL[:, c], T.TW[:], T.KEY1[:, 0:256], A.subtract, 256, [kb, W("TW")], [("SL", c.start, c.stop)])
+        fx, xh, n = "FX%d" % t, "XH%d" % t, 1024 + 256 * t
+        for h in range(2):
+            for j, m in pieces(HALF):
+                u = HALF * h + j
+                c = 256 * t + u // 16
+                src, rd = T.FE[:, 0:n].indirect(T.LT[:, c:c + m // 16]), [("FE", 0, n), ("LT", c, c + m // 16)]
+                if SHARE[t][h] == "V":
+                    tt(T[xh][:, u:u + m], src, T[fx][:, u:u + m], A.min, m * GC, rd + [(fx, u, u + m)], [(xh, u, u + m)])
+                else:
+                    x = "GH%d" % nxt("h", 2)
+                    act(T[x][:, 0:m], src, F.Copy, m * GC, rd, [W(x)])
+                    subtract("B5", fx, u, x, 0, m)
+                    act(T[xh][:, u:u + m], T.B5[:, 0:m], F.Relu, m, [W("B5")], [(xh, u, u + m)])
 
-    def square(sl):
-        r = sl.start, sl.stop
-        act(T.SQ[:, sl], T.C32[:, sl], F.Square, r[1] - r[0], [("C32",) + r, SQB], [("SQ",) + r], bias=T.PF[:, 5:6], scale=1.0 / 32)
+    def share_keys(t):
+        xh = "XH%d" % t
+        for h in range(2):
+            sg = "BMW" if SHARE[t][h] == "V" else "BMN"
+            for k0 in (0, 8):
+                mms([(T.KEY[:, 136 * h + k:136 * h + 136:17], T[xh][:, HALF * h + k:HALF * h + HALF:16], T[sg][:, 0:128:16],
+                      h == 0 and k == 0, False, 64) for k in range(k0, k0 + 8)], [(xh, HALF * h, HALF * h + HALF), W(sg)], [W("KEY")])
+        ends(0, False)
+
+    def ends(w, alone):
+        mms([(T.KEY[:, 16:272:17], T.ID[:], T.ENDS[:, 16 * w:16 * w + 16], alone, alone, 16)], [W("ID"), W("ENDS")], [W("KEY")])
 
     def gather_headings(t):
         n = 1024 + 256 * t
-        for k0, kn, _, eng in CHUNKS:
-            c, w = 256 * t + 16 * k0, 16 * kn
-            x = "XV%d" % nxt("x", 4) if eng == "V" else "GS%d" % nxt("s", 4)
-            for u, o in pieces(16 * w, c):
-                src, m = T.HT[:, 0:n].indirect(T.LT[:, o]), (u.stop - u.start) * GC
-                rd, wr = [("HT", 0, n), ("LT", o.start, o.stop)], [(x, u.start, u.stop)]
+        for m0, w, _, eng, _ in sorted(CHUNKS, key=lambda c: c[2] != "V"):
+            x = "XV%d" % nxt("x", 3) if eng == "V" else "GS%d" % nxt("s", 4)
+            for j, m in pieces(16 * w):
+                c = 256 * t + m0 + j // 16
+                src = T.HT[:, 0:n].indirect(T.LT[:, c:c + m // 16])
+                rd, wr = [("HT", 0, n), ("LT", c, c + m // 16)], [(x, j, j + m)]
                 if eng == "V":
-                    cp(T[x][:, u], src, m, rd, wr)
+                    cp(T[x][:, j:j + m], src, m * GC, rd, wr)
                 else:
-                    act(T[x][:, u], src, F.Copy, m, rd, wr)
+                    act(T[x][:, j:j + m], src, F.Copy, m * GC, rd, wr)
             bank = "B%d" % nxt("b", 3)
-            extract(bank, 0, "E1", x, True, True, w)
-            sl = slice(16 * k0, 16 * k0 + w)
-            cp(T.CL0[:, sl], T[bank][:, 0:w], w, [(bank, 0, w)], [("CL0", sl.start, sl.stop)])
-            act(T.C32[:, sl], T[bank][:, 0:w], F.Identity, w, [(bank, 0, w), MOFF], [("C32", sl.start, sl.stop)],
-                bias=T.PF[:, 7:8], scale=32.0)
-            square(sl)
+            extract(bank, 0, "E1", x, w)
+            sl, pr = slice(m0, m0 + w), (bank, 0, w)
+            cp(T.CL0[:, sl], T[bank][:, 0:w], w, [pr], [("CL0", m0, m0 + w)])
+            act(T.C32[:, sl], T[bank][:, 0:w], F.Identity, w, [pr, MOFF], [("C32", m0, m0 + w)], bias=T.PF[:, 7:8], scale=32.0)
+            act(T.SQ[:, sl], T[bank][:, 0:w], F.Square, w, [pr, P16], [("SQ", m0, m0 + w)], bias=T.PF[:, 8:9])
 
     def visits(t):
-        fv = "FVT%d" % t
+        fx = "FX%d" % t
         for a in range(NR):
             nb, cl, cln = "NB%d" % a, "CL%d" % (a % 2), "CL%d" % (1 - a % 2)
             if a > 0 and t > 0:
                 apply_update(t - 1, a)
-            for k0, kn, eng, _ in CHUNKS:
-                w = 16 * kn
-                e16 = 16 * w
-                sl = slice(16 * k0, 16 * k0 + w)
+            for m0, w, eng, _, first_op in CHUNKS:
+                sl = slice(m0, m0 + w)
                 bank = "B%d" % nxt("b", 3)
                 win = T[nb][:, 0:H]
 
                 def C(n):
-                    return (n, sl.start, sl.stop)
+                    return (n, m0, m0 + w)
+                j0 = nxt("x", 3) if eng == "V" else nxt("s", 4)
+                x, s = ("XV%d" if eng == "V" else "GS%d") % j0, "SS%d" % j0
+                for j, m in pieces(16 * w):
+                    c, u = m0 + j // 16, 16 * m0 + j
+                    src, rd = win.indirect(T[cl][:, c:c + m // 16]), [(nb, 0, H), (cl, c, c + m // 16)]
+                    if eng == "V":
+                        tt(T[x][:, j:j + m], src, T[fx][:, u:u + m], A.is_lt, m * GC, rd + [(fx, u, u + m)], [(x, j, j + m)])
+                    else:
+                        act(T[x][:, j:j + m], src, F.Copy, m * GC, rd, [(x, j, j + m)])
                 if eng == "V":
-                    x, kb = "XV%d" % nxt("x", 4), "KV"
-                    for u, o in pieces(e16, sl.start):
-                        tt(T[x][:, u], win.indirect(T[cl][:, o]), T[fv][:, u], A.is_lt, (u.stop - u.start) * GC,
-                           [(nb, 0, H), (cl, o.start, o.stop), W(fv)], [(x, u.start, u.stop)])
-                    extract(bank, 0, "E1", x, True, True, w)
+                    extract(bank, 0, "E1", x, w)
                 else:
-                    j = nxt("s", 4)
-                    x, s, kb = "GS%d" % j, "SS%d" % j, "KW"
-                    for u, o in pieces(e16, sl.start):
-                        act(T[x][:, u], win.indirect(T[cl][:, o]), F.Copy, (u.stop - u.start) * GC,
-                            [(nb, 0, H), (cl, o.start, o.stop)], [(x, u.start, u.stop)])
-                    for hh, (u, _) in enumerate(pieces(e16, 0)):
-                        db = "B%d" % (3 + hh)
-                        subtract(db, fv, u, x)
-                        act(T[s][:, u], T[db][:, 0:u.stop - u.start], F.Sign, u.stop - u.start, [W(db), HLF], [(s, u.start, u.stop)],
-                            bias=T.PF[:, 6:7])
-                    extract(bank, 0, "E05", s, True, True, w)
-                P, pr, kc = T[bank][:, 0:w], (bank, 0, w), 4 * t + a
-                ts(P, P, float(SLOPE), A.mult, w, [pr, (kb, kc, kc + 1)], [pr], T[kb][:, kc:kc + 1], A.add)
+                    for j, m in pieces(16 * w):
+                        db = "B%d" % (3 + nxt("u", 2))
+                        subtract(db, fx, 16 * m0 + j, x, j, m)
+                        act(T[s][:, j:j + m], T[db][:, 0:m], F.Sign, m, [W(db), HLF], [(s, j, j + m)], bias=T.PF[:, 6:7])
+                    extract(bank, 0, "E05", s, w)
+                P, pr, kc = T[bank][:, 0:w], (bank, 0, w), 2 * (4 * t + a) + (eng == "S")
+                if first_op == "V":
+                    ts(P, P, float(SLOPE), A.mult, w, [pr, ("KV", kc, kc + 1)], [pr], T.KV[:, kc:kc + 1], A.add)
+                else:
+                    act(P, P, F.Identity, w, [pr, ("KV", kc, kc + 1)], [pr], bias=T.KV[:, kc:kc + 1], scale=float(SLOPE))
                 tt(P, P, T.SQ[:, sl], A.add, w, [pr, C("SQ")], [pr])
                 tt(T.TI[:, sl], P, T.C32[:, sl], A.max, w, [pr, C("C32")], [C("TI")])
                 ts(T.CI[:, sl], T.TI[:, sl], 5, A.arith_shift_right, w, [C("TI")], [C("CI")], 4095, A.bitwise_and)
                 if a < NR - 1:
                     cp(T[cln][:, sl], T.CI[:, sl], w, [C("CI")], [C(cln)])
                     ts(T.C32[:, sl], T.CI[:, sl], 32.0, A.mult, w, [C("CI")], [C("C32")], float(-OFF), A.add)
-                    square(sl)
+                    act(T.SQ[:, sl], T.C32[:, sl], F.Square, w, [C("C32"), SQB], [C("SQ")], bias=T.PF[:, 5:6], scale=1.0 / 32)
                 else:
                     cp(T.CW[:, sl], T.CI[:, sl], w, [C("CI")], [C("CW")])
 
     def election(t):
-        C2, kr, z = ("B2", 0, 256), ("KEY0", 0, 256), slice(256 * t, 256 * t + 256)
-        act(T.B2[:, 0:256], T.CW[:, 0:256], F.Copy, 256, [("CW", 0, 256)], [C2])
-        act(T.CW[:, 256:384], T.CW[:, 0:128], F.Copy, 128, [("CW", 0, 128)], [("CW", 256, 384)])
-
-        def K(a, b):
-            return T.KEY0[:, a:b]
+        for h in range(2):
+            c = T.CW[:, 128 * h:128 * h + 128]
+            rd = ("CW", 128 * h, 128 * h + 128)
+            mms([(T.CT[:, 8 * h:8 * h + 8, 0:24], c, T.IDW[:], True, True, 4 * 192)], [rd, W("IDW")], [("CT", h, h + 1)])
+        act(T.CD[:], T.CT[:, :, 0:16], F.Copy, 256, [W("CT")], [W("CD")])
+        for h in range(2):
+            c = T.CW[:, 128 * h:128 * h + 128]
+            rd = ("CW", 128 * h, 128 * h + 128)
+            mms([(T.B3[:, 136 * h:136 * h + 136], c, T.DF[:], True, True, 4 * 136)], [rd, W("DF")], [("B3", 136 * h, 136 * h + 136)])
         for d in range(1, 9):
-            n, s, e = (256 if d < 8 else 128), 16 * d, ("EQ", 256 * d, 256 * d + 256)
-            tt(T.EQ[:, d, 0:n], T.B2[:, 0:n], T.CW[:, s:s + n], A.is_equal, n, [C2, ("CW", s, s + n)], [e])
-            lst = [(K(0, n), T.IDK[:], T.EQ[:, d, 0:n], d == 1, False, n),
-                   (K(s, 256), T.IDK[:], T.EQ[:, d, 0:256 - s], False, d == 8, 256 - s)]
-            if d < 8:
-                lst.append((K(0, s), T.IDK[:], T.EQ[:, d, 256 - s:256], False, False, s))
-            mms(lst, [e, W("IDK")], [kr])
-        tt(T.KK[:, 256:512], T.SL[:, z], K(0, 256), A.subtract, 256, [("SL", z.start, z.stop), kr], [("KK", 256, 512)])
-        tt(T.KK[:, 0:256], K(0, 256), T.SW[:, z], A.add, 256, [("SW", z.start, z.stop), kr], [("KK", 0, 256)])
+            j = d % 3
+            e = ("EQ", j, j + 1)
+            tt(T.EQ[:, j, :, 8:24], T.CT[:, :, d:d + 16], T.CD[:], A.is_equal, 256, [W("CT"), W("CD")], [e])
+            mms([(T.KEY[:, 0:272], T.IDK[:], T.EQ[:, j, :, o:o + 17], False, d == 8, 272) for o in ((8, 8 - d, 24 - d) if d < 8 else (8,))],
+                [e, W("IDK")], [W("KEY")])
 
-        def tree(src, w, out, oc):
-            n, s, so = 128, src, 256 * w
-            for m in ("M1", "M2", "M3", None):
-                dst, do = (out, oc) if m is None else (m, n * w)
-                tt(T[dst][:, do:do + n], T[s][:, so:so + n], T[s][:, so + n:so + 2 * n], A.max, 2 * n, [(s, so, so + 2 * n)], [(dst, do, do + n)])
-                n, s, so = n // 2, dst, do
-        tree("KK", 1, "B4", 0)
-        tree("KK", 0, "B3", 0)
-        n = 16
-        while n < 256:
-            for b in ("B4", "B3"):
-                cp(T[b][:, n:2 * n], T[b][:, 0:n], n, [(b, 0, n)], [(b, n, 2 * n)])
-            n *= 2
-        for b, w in (("B4", 1), ("B3", 0)):
-            c = slice(256 * w, 256 * w + 256)
-            q = ("DD", c.start, c.stop)
-            tt(T.DD[:, c], T.KK[:, c], T[b][:, 0:256], A.subtract, 256, [("KK", c.start, c.stop), (b, 0, 256)], [q])
-            tt(T.DD[:, c], T.DD[:, c], T.B2[:, 0:256], A.add, 256, [q, C2], [q])
-            tree("DD", w, "WLI", 16 * w)
-        for w in (1, 0):
-            rd, o = ("WLI", 16 * w, 16 * w + 16), 32 * w
-            for d, m in ((0, 4080), (16, 15)):
-                ts(T.SPI[:, o + d:o + d + 16], T.WLI[:, 16 * w:16 * w + 16], m, A.bitwise_and, 16, [rd], [("SPI", o + d, o + d + 16)])
-            cp(T.SPB[:, o:o + 32], T.SPI[:, o:o + 32], 32, [("SPI", o, o + 32)], [("SPB", o, o + 32)])
-        for n in ("LF", "LU"):
-            cp(T[n][:], T.WLI[:, 16:32], 16, [("WLI", 16, 32)], [W(n)])
+    def pick(w, bank):
+        run, go, pk, wb = "RUN%d" % w, "GO%d" % w, "PICK%d" % w, "WB%d" % w
+        if w:
+            ends(1, True)
+        scan(T[run][:], T["RST%d" % w][:], T.KEY[:, 0:272], A.add, A.min if w else A.max, 272, [W("RST%d" % w), W("KEY")], [W(run)])
+        tt(T[go][:, 1:272], T.KEY[:, 1:272], T[run][:, 0:271], A.is_ge if w else A.is_le, 272, [W("KEY"), W(run)], [W(go)])
+        scan(T[pk][:], T.B3[:, 0:272], T[go][:], A.add, A.mult, 272, [("B3", 0, 272), W(go)], [W(pk)])
+        hilo(wb, T[wb][:, 0:256:16], T[wb][:, 1:256:16], T[pk][:, 16:272:17], 16, [W(pk)])
+        mms([(T[bank][:, 128 * h:128 * h + 128], T[wb][:, 128 * h:128 * h + 128], T.ID[:], True, True, 128) for h in range(2)],
+            [W(wb), W("ID")], [(bank, 0, 256)])
 
-    def headings_out(t, soft=()):
-        mms([(T.B0[:, i:256:16], sel(i, d), T.SPB[:, 16 * d:16 * d + 16], d == 0, d == 1, 16) for i in range(16) for d in (0, 1)],
-            [("SPB", 0, 32), W("MIP")], [("B0", 0, 256)], soft)
+    def headings_out(t):
+        pick(0, "B0")
         c = 1024 + 256 * t
-        act(T.HT[:, c:c + 256], T.B0[:, 0:256], F.Copy, 256, [("B0", 0, 256)], [("HT", c, c + 256)])
+        act(T.HT[:, c:c + 256], T.B0[:, 0:256], F.Copy, 256, [("B0", 0, 256)], [("HT", c, c + 256), W("KS1")], accum=T.KS1[:, 0:1])
 
     def write_yh(t):
         c, y = 1024 + 256 * t, ("YH8", 256 * t, 256 * t + 256)
-        mms([(T.B5[0:8, 0:256], T.BMW[:, 0:128:16], T.HT[:, c:c + 256], True, True, 256)], [W("BMW"), ("HT", c, c + 256)], [("B5", 0, 256)])
-        act(T.YH8[:, 256 * t:256 * t + 256], T.B5[0:8, 0:256], F.Copy, 256, [("B5", 0, 256)], [y])
+        mms([(T.CT[0:8, 0:8, :], T.BMW[:, 0:128:16], T.HT[:, c:c + 256], True, True, 256)], [W("BMW"), ("HT", c, c + 256)], [W("CT")])
+        act(T.YH8[:, 256 * t:256 * t + 256], T.CT[0:8, 0:8, :], F.Copy, 256, [W("CT")], [y])
         dma("Y", T.yh[:, 256 * t:256 * t + 256], T.YH8[:, 256 * t:256 * t + 256], 2.5, [y], [])
 
     def notes(t):
-        fv, ov, ol = "FVT%d" % t, "OUTV%d" % t, "OUTL%d" % t
-        b1, b3, b4 = ("B1", 0, 256), ("B3", 0, 256), ("B4", 0, 256)
+        c, ov, ol = 1024 + 256 * t, "OUTV%d" % t, "OUTL%d" % t
+        pick(1, "B4")
+        act(T.LR[:], T.B4[:, 0:256], F.Copy, 256, [("B4", 0, 256)], [W("LR")])
+        mms([(T.B4[:, 256:512], T.BMW[:], T.LR[:], True, True, 256)], [W("BMW"), W("LR")], [("B4", 256, 512)])
+        extract("B3", 288, "E1", "LR", 16)
+        cp(T.LB[:], T.B4[:, 256:512], 256, [("B4", 256, 512)], [W("LB")])
+        for n in ("LF", "LU"):
+            cp(T[n][:], T.B3[:, 288:304], 16, [("B3", 288, 304)], [W(n)])
+        lo3, hi3, lo4 = ("B3", 0, 256), ("B3", 256, 512), ("B4", 0, 256)
         act(T.OLD[:], T.NB0[:, 0:H].indirect(T.LU[:, 0:16]), F.Copy, 256 * GC, [("NB0", 0, H), W("LU")], [W("OLD")])
-        mms([(T.B3[:, 0:256], T.ID[:], T[fv][:, 0:256], True, False, 256), (T.B3[:, 0:256], T.IDN[:], T.OLD[:], False, True, 256)],
-            [W("ID"), W("IDN"), W(fv), W("OLD")], [b3])
-        ts(T.DC[:], T.B3[:, 0:256], 32.0, A.min, 256, [b3], [W("DC")], -32.0, A.max)
-        mms([(T.B4[:, 0:256], T.ID[:], T.OLD[:], True, False, 256), (T.B4[:, 0:256], T.ID[:], T.DC[:], False, True, 256)],
-            [W("ID"), W("OLD"), W("DC")], [b4])
-        act(T[ov][:, 0:256], T.B4[:, 0:256], F.Copy, 256, [b4], [(ov, 0, 256)])
-        mms([(T.B1[:, i:256:16], T.BI[:, 128 * i:128 * i + 128], T.SPB[:, 32 + 16 * d:48 + 16 * d], d == 0, d == 1, 16)
-             for i in range(16) for d in (0, 1)], [("SPB", 32, 64), W("BI")], [b1])
-        cp(T.LB[:], T.B1[:, 0:256], 256, [b1], [W("LB")])
+        mms([(T.B3[:, 0:256], T.ID[:], T.FE[:, c:c + 256], True, False, 256), (T.B3[:, 0:256], T.IDN[:], T.OLD[:], False, True, 256)],
+            [W("ID"), W("IDN"), ("FE", c, c + 256), W("OLD")], [lo3])
+        ts(T.DC[:], T.B3[:, 0:256], 32.0, A.min, 256, [lo3], [W("DC")], -32.0, A.max)
+        mms([(T.B3[:, 256:512], T.ID[:], T.OLD[:], True, False, 256), (T.B3[:, 256:512], T.ID[:], T.DC[:], False, True, 256)],
+            [W("ID"), W("OLD"), W("DC")], [hi3])
+        act(T[ov][:, 0:256], T.B3[:, 256:512], F.Copy, 256, [hi3], [(ov, 0, 256)])
         for lo in (0, 8):
-            er = ("EQT", 256 * lo, 256 * lo + 2048)
             for mb in range(lo, lo + 8):
                 n = 256 - 16 * mb
-                ts(T.EQT[:, mb, 0:n], T.LB[:, 16 * mb:256], T.LF[:, mb:mb + 1], A.is_equal, n * 0.5, [W("LB"), W("LF")], [("EQT", 256 * mb, 256 * mb + 256)])
-            tt(T.EQT[:, lo:lo + 8, 0:16], T.EQT[:, lo:lo + 8, 0:16], T.TRI[:, lo:lo + 8, :], A.mult, 256, [er, W("TRI")], [er])
-            mms([(T.B1[:, 16 * mb:256], T.BMW[:], T.EQT[:, mb, 0:256 - 16 * mb], mb == 0, mb == 15, 256 - 16 * mb) for mb in range(lo, lo + 8)],
-                [W("BMW"), er], [b1])
-        ts(T.FL[:], T.B1[:, 0:256], 0.5, A.is_gt, 256, [b1], [W("FL")])
-        mms([(T.B1[:, 256:272], T.EX[:, 15 - i:143 - i], T.FL[:, i:256:16], i == 0, i == 15, 16) for i in range(16)],
-            [W("EX"), W("FL")], [("B1", 256, 272)])
-        tt(T.DL[:], T.DUP[:], T.LF[:], A.subtract, 32, [W("DUP"), W("LF")], [W("DL")])
-        tt(T.OF[:], T.B1[:, 256:272], T.DL[:], A.mult, 32, [("B1", 256, 272), W("DL")], [W("OF")])
-        tt(T.OF[:], T.OF[:], T.LF[:], A.add, 32, [W("OF"), W("LF")], [W("OF")])
+                ts(T.EQT[:, mb, 0:n], T.LB[:, 16 * mb:256], T.LF[:, mb:mb + 1], A.is_equal, n * 0.5, [W("LB"), W("LF")], [("EQT", mb, mb + 1)])
+            lst = [(T.B4[:, 16 * mb + 16:256], T.BO[:], T.EQT[:, mb, 16:256 - 16 * mb], mb == 0, False, 240 - 16 * mb)
+                   for mb in range(lo, min(lo + 8, 15))]
+            if lo:
+                lst.append((T.B4[:, 0:16], T.BD[:], T.EQT[:, 0, 0:16], False, False, 16))
+                lst.append((T.B4[:, 16:256], T.BD[:], T.EQT[:, 1:16, 0:16], False, True, 240))
+            mms(lst, [W("BO"), W("BD"), ("EQT", 0, lo + 8)], [lo4])
+        tt(T.FL[:], T.B4[:, 0:256], T.THR[:], A.is_ge, 256, [lo4, W("THR")], [W("FL")])
+        extract("B4", 256, "EX", "FL", 16)
+        tt(T.OF[:], T.B4[:, 256:272], T.DUP[:], A.mult, 16, [("B4", 256, 272), W("DUP")], [W("OF")])
+        tt(T.OF[:], T.OF[:], T.LF[:], A.max, 32, [W("OF"), W("LF")], [W("OF")])
         cp(T[ol][:], T.OF[:], 16, [W("OF")], [W(ol)])
         scatter("NB0", ov, ol)
 
     def scatter(nb, ov, ol):
-        vec(lambda q: q.tensor_copy(out=T[nb][:, 0:H + DUMMY].indirect(T[ol][:, 0:16]), in_=T[ov][:, 0:256]), 256 * 3,
+        vec(lambda q: q.tensor_copy(out=T[nb][:, 0:H + DUMMY].indirect(T[ol][:, 0:16]), in_=T[ov][:, 0:256]), 256 * 3.8,
             [(ov, 0, 256), W(ol)], [(nb, 0, H + DUMMY)])
 
     def bias(t, a, src):
-        c = 4 * (t + 1) + a
-        for kb in ("KV", "KW"):
-            act(T[kb][:, c:c + 1], T[src][:, 256:257], F.Identity, 1, [(src, 256, 257), (kb, 0, 1)], [(kb, c, c + 1)], bias=T[kb][:, 0:1], scale=32.0)
+        c = 2 * (4 * (t + 1) + a)
+        act(T.KV[:, c:c + 2], T.KV[:, 0:2], F.Identity, 2, [(src, 256, 257), ("KV", 0, 2)], [("KV", c, c + 2)], bias=T[src][:, 256:257])
 
     def kappa(t):
         ov = "OUTV%d" % t
-        mms([(T.B0[:, 0:32], T.ONES[:], T.SPB[:, 0:32], True, True, 32)], [W("ONES"), ("SPB", 0, 32)], [("B0", 0, 32)])
-        act(T.JUNK[:], T.B0[:, 0:32], F.Copy, 32, [("B0", 0, 32)], [W("KS1"), W("JUNK")], accum=T.KS1[:, 0:1])
-        cp(T.KI[:, 0:1], T.KS1[:, 0:1], 1, [W("KS1")], [W("KI")])
-        ts(T.KJ[:, 0:1], T.KI[:, 0:1], 255, A.bitwise_and, 1, [W("KI")], [W("KJ")])
+        mms([(T.CT[:, 0, 0:1], T.ONES[:], T.KS1[:, 0:1], True, True, 256)], [W("ONES"), W("KS1")], [W("CT")])
+        cp(T.KI[:, 0:1], T.CT[:, 0, 0:1], 1, [W("CT")], [W("KI")])
+        ts(T.KJ[:, 0:1], T.KI[:, 0:1], 255 * 32, A.bitwise_and, 1, [W("KI")], [W("KJ")])
         cp(T[ov][:, 256:257], T.KJ[:, 0:1], 1, [W("KJ")], [(ov, 256, 257)])
         bias(t, 0, ov)
 
@@ -586,7 +584,7 @@ def build(core, T, topo):
     def send_update(t):
         dsts = [(rank - a) % NR for a in range(1, NR)]
         ids = [DstId(rid=addr(x)[0], pnc=addr(x)[1]) for x in dsts]
-        for nm, inn, sm in (("OUTL%d" % t, "INL%d_%d", "il%d_%d"), ("OUTV%d" % t, "INV%d_%d", "iv%d_%d")):
+        for nm, inn, sm in (("OUTV%d" % t, "INV%d_%d", "iv%d_%d"), ("OUTL%d" % t, "INL%d_%d", "il%d_%d")):
             def f(q, nm=nm, inn=inn, sm=sm):
                 tr = RemoteDMATransfer(dst_ids=ids, dma_engine_mask=emask(cross), remote_sem=T.sem[sm % (rank, t)], srcs=[T[nm][:]],
                                        dsts=[T[inn % (rel(rank, x), t)][:] for x in dsts])
@@ -603,28 +601,22 @@ def build(core, T, topo):
         bias(t, a, iv)
         scatter("NB%d" % a, iv, il)
 
-    lists(0)
-    permute(0)
+    for t in range(RT):
+        lists(t)
+        expand(t)
     gather_headings(0)
-    first_v = len(gr["nodes"]) - 1
-    lists(1)
-    shares(0)
-    for t in range(1, RT):
-        permute(t)
-        load_tiles(t, [first_v])
+    for t in range(RT):
         shares(t)
     for t in range(RT):
+        share_keys(t)
         visits(t)
         election(t)
+        headings_out(t)
+        notes(t)
         if t + 1 < RT:
-            headings_out(t)
-            notes(t)
             gather_headings(t + 1)
             kappa(t)
             send_update(t)
-        else:
-            notes(t)
-            headings_out(t, [len(gr["nodes"]) - 1])
         write_yh(t)
     for j, e in ((0, "S"), (1, "Y")):
         dma(e, T.yl[:, HALF * j:HALF * j + HALF], T.NB0[:, HALF * j:HALF * j + HALF], 5.0, [("NB0", HALF * j, HALF * j + HALF)], [])

@@ -7,11 +7,13 @@ KS = 130
 SLOPE = 613 * 32 + MOD * KS
 OFF = MOD * 512
 BV = -256 - MOD * (9 * KS + 1) - OFF
-BS = BV + 8 * SLOPE
-CHUNKS = ((0, 72, "V", "S", "V"), (72, 56, "S", "S", "V"), (128, 72, "V", "S", "V"), (200, 56, "S", "S", "V"))
+CHUNKS = ((128, 64, "V", "V", "V"), (192, 64, "S", "S", "V"), (0, 72, "V", "S", "V"), (72, 56, "S", "S", "V"))
 SHARE = ("VS", "VS", "VS", "VS")
 EXPAND = "VVVVVVVVVVVVGGGG"
 PIECE = 512
+PASSES, WAKE = 6, 0.06
+SUBH = 0
+JOIN = 1
 BIG = float(1 << 24)
 CYC, GC, PEC = 0.83e-3 * 1.25, 1.56, 0.6e-3
 
@@ -28,15 +30,14 @@ B16, F32, I32, U16 = "bfloat16", "float32", "int32", "uint16"
 _buf("NB0 NB1 NB2 NB3", H + DUMMY, B16)
 _buf("FE HT", 2048, B16)
 _buf("FX0 FX1 FX2 FX3 XH0 XH1 XH2 XH3", 4096, B16)
-_buf("XV0 XV1 XV2 GS0 GS1 GS2 GS3 SS0 SS1 SS2 SS3", 16 * max(c[1] for c in CHUNKS), B16)
-_buf("OUTV0 OUTV1 OUTV2 OUTV3", 264, B16)
-_buf("OUTL0 OUTL1 OUTL2 OUTL3 LU", 16, U16)
+for _j, _c in enumerate(CHUNKS):
+    _buf("X%d SS%d" % (_j, _j) if _c[2] == "S" else "X%d" % _j, 16 * _c[1], B16)
+VW = 264
+_buf("NV0 NV1 NV2 NV3", RT * VW, B16)
+_buf("NL0 NL1 NL2 NL3", RT * 16, U16)
 for _t in range(RT - 1):
     for _a in range(NR):
         SEMAPHORES += ["iv%d_%d" % (_a, _t), "il%d_%d" % (_a, _t)]
-        if _a:
-            _buf("INV%d_%d" % (_a, _t), 264, B16)
-            _buf("INL%d_%d" % (_a, _t), 16, U16)
 for _a in range(1, NR):
     SEMAPHORES += ["n%d_0" % _a, "n%d_1" % _a]
 _buf("CMP", 1024, I32)
@@ -47,26 +48,31 @@ _buf("RI", 160, F32)
 _buf("RG ONES", 128, F32)
 _buf("PI PM PG KI KJ", 2, I32)
 _buf("PF", 16, F32)
-_buf("MK DUP LF OF", 16, F32)
-_buf("KV", 32, F32)
+_buf("MK", 16, F32)
+_buf("DUP LF0 LF1 OF0 OF1", 8, F32)
+_buf("LU0 LU1", 8, U16)
+_buf("KV", 16, F32)
+_buf("HALVES", 128, B16)
 _buf("MB", 160, B16)
 _buf("MIP", 16 * 160, B16)
 _buf("E1 E05 EX", 144, B16)
-_buf("FL OLD DC LR WB0 WB1", 256, B16)
-_buf("C32 SQ CW THR PW", 256, F32)
+_buf("FL0 FL1 OLD0 OLD1 DC0 DC1 LR0 LR1 WB0 WB1 WB2 WB3", 128, B16)
+_buf("C32 SQ CW", 256, F32)
+_buf("THR", 128, F32)
 _buf("GH0 GH1", PIECE, B16)
-_buf("CL0 CL1 LB", 256, U16)
+_buf("CL0 CL1", 256, U16)
+_buf("LB0 LB1", 128, U16)
 _buf("TI CI", 256, I32)
-_buf("IDW", [8, 24], F32)
+_buf("IDW", [8, 32], F32)
 _buf("DF", [8, 17], F32)
-_buf("CD", [16, 16], F32)
-_buf("RST0 RST1 RUN0 RUN1 GO0 GO1 PICK0 PICK1", 272, F32)
-_buf("EQ", [3, 16, 40], B16)
-_buf("ENDS", 32, B16)
-_buf("EQT", [16, 256], B16)
+_buf("CD", [16, 24], F32)
+_buf("RST0 RST1 RUN0 RUN1 GO0 GO1 PICK0 PICK1", 136, F32)
+_buf("EQ", [3, 8, 32], B16)
+_buf("ENDS", 16, B16)
+_buf("EQT0 EQT1", [8, 128], B16)
 _buf("KS1", 2, F32)
 _buf("YH8", 1024, F32, rows=8)
-_buf("B0 B1 B2 B3 B4 B5 KEY", 512, F32, "psum")
+_buf("B0 B1 B3 B4 B5 KEY0 KEY1", 512, F32, "psum")
 _buf("CT", [16, 32], F32, "psum")
 PSUM = set(n for n in SCRATCH if SCRATCH[n][0] == "psum")
 CSEM = {"V": "cv", "S": "cs", "P": "cp", "G": "cg"}
@@ -102,42 +108,48 @@ def add(gr, eng, emit, cost, reads=(), writes=(), kind="c", sem=None, val=0, lat
 
 def schedule(gr):
     nodes = gr["nodes"]
-    succ = [[] for _ in nodes]
+    succ, pred = [[] for _ in nodes], [[] for _ in nodes]
     for n in nodes:
         for j in n["deps"] | n["soft"]:
-            succ[j].append(n["id"])
+            gap = (nodes[j]["lat"] + (WAKE if nodes[j]["eng"] != n["eng"] else 0.0)) if j in n["deps"] else 0.0
+            succ[j].append((n["id"], gap))
+            pred[n["id"]].append((j, gap))
+
+    def lay(rank, after, before, at):
+        left = [len(b) for b in before]
+        free, ready, end, order = {}, {}, [0.0] * len(nodes), []
+        for n in nodes:
+            free[n["eng"]] = 0.0
+            ready.setdefault(n["eng"], set())
+            if left[n["id"]] == 0:
+                ready[n["eng"]].add(n["id"])
+        while len(order) < len(nodes):
+            s, e = min((max(free[e], min(at[i] for i in ready[e])), e) for e in ready if ready[e])
+            i = max((k for k in ready[e] if at[k] <= s), key=lambda k: (rank[k], -k))
+            ready[e].discard(i)
+            end[i] = s + nodes[i]["cost"]
+            if e != "R":
+                free[e] = end[i]
+            order.append(i)
+            for k, gap in after[i]:
+                left[k] -= 1
+                at[k] = max(at[k], end[i] + gap)
+                if left[k] == 0:
+                    ready[nodes[k]["eng"]].add(k)
+        return order, end
+
     rank = [0.0] * len(nodes)
     for n in reversed(nodes):
-        rank[n["id"]] = max([0.0] + [rank[s] for s in succ[n["id"]]]) + n["cost"] + n["lat"] + 0.05
-    left = [len(n["deps"] | n["soft"]) for n in nodes]
-    at = [n["est"] for n in nodes]
-    free, ready = {"R": 0.0}, {}
-    for n in nodes:
-        free[n["eng"]] = 0.0
-        ready.setdefault(n["eng"], set())
-        if left[n["id"]] == 0:
-            ready[n["eng"]].add(n["id"])
-    order = []
-    while len(order) < len(nodes):
-        best = None
-        for e in ready:
-            if ready[e]:
-                s = max(free[e], min(at[i] for i in ready[e]))
-                if best is None or s < best[0]:
-                    best = (s, e)
-        s, e = best
-        i = max((k for k in ready[e] if at[k] <= s), key=lambda k: (rank[k], -k))
-        n = nodes[i]
-        ready[e].discard(i)
-        if e != "R":
-            free[e] = s + n["cost"]
-        order.append(i)
-        for k in succ[i]:
-            left[k] -= 1
-            at[k] = max(at[k], s + n["cost"] + (n["lat"] if i in nodes[k]["deps"] else 0.0))
-            if left[k] == 0:
-                ready[nodes[k]["eng"]].add(k)
-    return order
+        rank[n["id"]] = max([n["lat"]] + [rank[s] + gap for s, gap in succ[n["id"]]]) + n["cost"] + 0.05
+    best = None
+    for _ in range(PASSES):
+        order, end = lay(rank, succ, pred, [n["est"] for n in nodes])
+        total = max(end[n["id"]] + n["lat"] for n in nodes)
+        if best is None or total < best[0]:
+            best = (total, order)
+        rank = lay(end, pred, succ, [n["lat"] for n in nodes])[1]
+    gr["total"] = best[0]
+    return best[1]
 
 
 def emit_all(gr, order, g, T):
@@ -185,7 +197,7 @@ def emit_all(gr, order, g, T):
 def build(core, T, topo):
     rank = T.rank_of(core)
     gr = {"nodes": [], "acc": {}, "bank": {}}
-    num = {"d": 0, "ls": 0, "x": 0, "s": 0, "b": 0, "h": 0, "u": 0, "lsend": 0}
+    num = {"d": 0, "ls": 0, "x": 0, "s": 0, "b": 0, "h": 0, "u": 0, "e": 0, "lsend": 0}
     lastd = {}
 
     def nxt(k, n):
@@ -237,9 +249,10 @@ def build(core, T, topo):
             return ins
         return add(gr, "P", f, sum(max(64, x[5]) for x in lst) * PEC + 0.03, reads, writes, soft=soft)
 
-    def extract(bank, c0, en, x, n):
-        return mms([(T[bank][:, c0:c0 + n], T[en][:, 15 - i:143 - i], T[x][:, i:16 * n:16], i == 0, i == 15, n)
-                    for i in range(16)], [(x, 0, 16 * n), W(en)], [(bank, c0, c0 + n)])
+    def extract(bank, c0, en, x, n, signs=False):
+        lst = [(T[bank][:, c0:c0 + n], T.BMW[:], T.HALVES[:, 0:n], True, False, n)] if signs else []
+        return mms(lst + [(T[bank][:, c0:c0 + n], T[en][:, 15 - i:143 - i], T[x][:, i:16 * n:16], i == 0 and not signs, i == 15, n)
+                          for i in range(16)], [(x, 0, 16 * n), W(en), W("BMW"), W("HALVES")], [(bank, c0, c0 + n)])
 
     def pieces(n):
         return [(j, min(PIECE, n - j)) for j in range(0, n, PIECE)]
@@ -261,8 +274,8 @@ def build(core, T, topo):
 
     gps(lambda q: q.iota(T.PI[:, 0:1], [[1, 1]], 0, 1), 2, [W("PI")])
     for ap, n, pat, base, c in ((T.RI[:], "RI", [[1, 160]], 0, 320), (T.RG[:], "RG", [[16, 8], [0, 16]], 0, 256),
-                                (T.IDW[:, :, 0:16], "IDW", [[16, 8], [1, 16]], 0, 256), (T.IDW[:, :, 16:24], "IDW", [[16, 8], [1, 8]], 0, 128),
-                                (T.DUP[:], "DUP", [[16, 16]], H, 32)):
+                                (T.IDW[:, :, 0:8], "IDW", [[16, 8], [1, 8]], 8, 128), (T.IDW[:, :, 8:24], "IDW", [[16, 8], [1, 16]], 0, 256),
+                                (T.IDW[:, :, 24:32], "IDW", [[16, 8], [1, 8]], 0, 128), (T.DUP[:], "DUP", [[16, 8]], H, 32)):
         gps(lambda q, ap=ap, pat=pat, base=base: q.iota(ap, pat, base, 0, allow_small_or_imprecise_dtypes=True), c, [W(n)])
     ts(T.PM[:, 0:1], T.PI[:, 0:1], 15, A.bitwise_and, 1, [W("PI")], [W("PM")])
     ts(T.PG[:, 0:1], T.PI[:, 0:1], 112, A.bitwise_and, 1, [W("PI")], [W("PG")])
@@ -287,27 +300,28 @@ def build(core, T, topo):
         eqc(n, 128, 2, v, "RG")
     ts(T.DUP[:], T.DUP[:], T.PF[:, 1:2], A.add, 16, [W("DUP"), ("PF", 1, 2)], [W("DUP")])
     for y in range(16):
-        fill(T.THR[:, y:256:16], 2.0 ** (1 - y), 16, W("THR"))
-    tt(T.PW[:, 0:16], T.THR[:, 0:16], T.MK[:], A.mult, 32, [W("THR"), W("MK")], [W("PW")])
-    act(T.PW[:, 16:32], T.PW[:, 0:16], F.Copy, 16, [W("PW")], [W("PW"), P2], scale=0.5, accum=T.PF[:, 9:10])
+        fill(T.THR[:, y:128:16], 2.0 ** (1 - y), 16, W("THR"))
+    tt(T.CW[:, 0:16], T.THR[:, 0:16], T.MK[:], A.mult, 32, [W("THR"), W("MK")], [W("CW")])
+    act(T.CW[:, 16:32], T.CW[:, 0:16], F.Copy, 16, [W("CW")], [W("CW"), P2], scale=0.5, accum=T.PF[:, 9:10])
     ts(T.BD[:], T.BMW[:], T.PF[:, 9:10], A.mult, 64, [W("BMW"), P2], [W("BD")])
-    ts(T.IDW[:], T.IDW[:], T.PF[:, 0:1], A.is_equal, 192, [W("IDW"), ("PF", 0, 1)], [W("IDW")])
+    ts(T.IDW[:], T.IDW[:], T.PF[:, 0:1], A.is_equal, 256, [W("IDW"), ("PF", 0, 1)], [W("IDW")])
     fill(T.DF[:], 0.0, 136, W("DF"))
-    ts(T.DF[:, :, 0:16], T.IDW[:, :, 0:16], -1.0, A.mult, 128, [W("IDW")], [W("DF")])
-    tt(T.DF[:, :, 1:17], T.DF[:, :, 1:17], T.IDW[:, :, 0:16], A.add, 256, [W("IDW"), W("DF")], [W("DF")])
+    ts(T.DF[:, :, 0:16], T.IDW[:, :, 8:24], -1.0, A.mult, 128, [W("IDW")], [W("DF")])
+    tt(T.DF[:, :, 1:17], T.DF[:, :, 1:17], T.IDW[:, :, 8:24], A.add, 256, [W("IDW"), W("DF")], [W("DF")])
     for w in (0, 1):
-        fill(T["RST%d" % w][:], 0.0, 256, W("RST%d" % w))
-        for c in (slice(0, 1), slice(16, 272, 17)):
+        fill(T["RST%d" % w][:], 0.0, 136, W("RST%d" % w))
+        for c in (slice(0, 1), slice(16, 136, 17)):
             fill(T["RST%d" % w][:, c], BIG if w else -BIG, 16, W("RST%d" % w))
         fill(T["GO%d" % w][:, 0:1], 0.0, 16, W("GO%d" % w))
-        fill(T["WB%d" % w][:], 0.0, 128, W("WB%d" % w))
-        fill(T.ENDS[:, 16 * w:16 * w + 16], BIG / 16 if w else -BIG / 16, 16, W("ENDS"))
-    fill(T.EQ[:], 0.0, 960, W("EQ"))
+        fill(T.ENDS[:, 8 * w:8 * w + 8], BIG / 16 if w else -BIG / 16, 16, W("ENDS"))
+    for w in range(4):
+        fill(T["WB%d" % w][:], 0.0, 64, W("WB%d" % w))
+    fill(T.EQ[:, :, :, 24], 0.0, 24, W("EQ"))
     fill(T.ONES[:], 32.0, 128, W("ONES"))
-    fill(T.KV[:, 0:8:2], float(BV), 4, ("KV", 0, 8))
-    fill(T.KV[:, 1:8:2], float(BS), 4, ("KV", 0, 8))
+    fill(T.KV[:, 0:4], float(BV), 4, ("KV", 0, 4))
+    fill(T.HALVES[:], 0.5, 64, W("HALVES"))
     for t in range(RT - 1):
-        fill(T["OUTV%d" % t][:, 256:264], 0.0, 4, ("OUTV%d" % t, 256, 264))
+        fill(T.NV0[:, VW * t + 256:VW * t + VW], 0.0, 4, ("NV0", VW * t + 256, VW * t + VW))
 
     def hilo(dst, hi, lo, src, n, reads):
         cp(hi, src, n, reads, [W(dst)])
@@ -419,17 +433,17 @@ def build(core, T, topo):
         for h in range(2):
             sg = "BMW" if SHARE[t][h] == "V" else "BMN"
             for k0 in (0, 8):
-                mms([(T.KEY[:, 136 * h + k:136 * h + 136:17], T[xh][:, HALF * h + k:HALF * h + HALF:16], T[sg][:, 0:128:16],
-                      h == 0 and k == 0, False, 64) for k in range(k0, k0 + 8)], [(xh, HALF * h, HALF * h + HALF), W(sg)], [W("KEY")])
-        ends(0, False)
+                mms([(T["KEY%d" % h][:, k:136:17], T[xh][:, HALF * h + k:HALF * h + HALF:16], T[sg][:, 0:128:16], k == 0, False, 64)
+                     for k in range(k0, k0 + 8)], [(xh, HALF * h, HALF * h + HALF), W(sg)], [W("KEY%d" % h)])
+            ends(0, h, False)
 
-    def ends(w, alone):
-        mms([(T.KEY[:, 16:272:17], T.ID[:], T.ENDS[:, 16 * w:16 * w + 16], alone, alone, 16)], [W("ID"), W("ENDS")], [W("KEY")])
+    def ends(w, h, alone):
+        mms([(T["KEY%d" % h][:, 16:136:17], T.ID[:], T.ENDS[:, 8 * w:8 * w + 8], alone, alone, 8)], [W("ID"), W("ENDS")], [("KEY%d" % h, 0, 136)])
 
     def gather_headings(t):
-        n = 1024 + 256 * t
-        for m0, w, _, eng, _ in sorted(CHUNKS, key=lambda c: c[2] != "V"):
-            x = "XV%d" % nxt("x", 3) if eng == "V" else "GS%d" % nxt("s", 4)
+        n, got = 1024 + 256 * t, [0, 0]
+        for j0, (m0, w, _, eng, _) in enumerate(CHUNKS):
+            x = "X%d" % j0
             for j, m in pieces(16 * w):
                 c = 256 * t + m0 + j // 16
                 src = T.HT[:, 0:n].indirect(T.LT[:, c:c + m // 16])
@@ -438,28 +452,33 @@ def build(core, T, topo):
                     cp(T[x][:, j:j + m], src, m * GC, rd, wr)
                 else:
                     act(T[x][:, j:j + m], src, F.Copy, m * GC, rd, wr)
-            bank = "B%d" % nxt("b", 3)
-            extract(bank, 0, "E1", x, w)
-            sl, pr = slice(m0, m0 + w), (bank, 0, w)
-            cp(T.CL0[:, sl], T[bank][:, 0:w], w, [pr], [("CL0", m0, m0 + w)])
-            act(T.C32[:, sl], T[bank][:, 0:w], F.Identity, w, [pr, MOFF], [("C32", m0, m0 + w)], bias=T.PF[:, 7:8], scale=32.0)
-            act(T.SQ[:, sl], T[bank][:, 0:w], F.Square, w, [pr, P16], [("SQ", m0, m0 + w)], bias=T.PF[:, 8:9])
+            bank = "B%d" % (m0 // 128)
+            o = m0 % 128
+            extract(bank, o, "E1", x, w)
+            cp(T.CL0[:, m0:m0 + w], T[bank][:, o:o + w], w, [(bank, o, o + w)], [("CL0", m0, m0 + w)])
+            got[m0 // 128] += w
+            if JOIN:
+                if got[m0 // 128] % 128:
+                    continue
+                m0, w, o = m0 // 128 * 128, 128, 0
+            sl, pr, P = slice(m0, m0 + w), (bank, o, o + w), T[bank][:, o:o + w]
+            act(T.C32[:, sl], P, F.Identity, w, [pr, MOFF], [("C32", m0, m0 + w)], bias=T.PF[:, 7:8], scale=32.0)
+            act(T.SQ[:, sl], P, F.Square, w, [pr, P16], [("SQ", m0, m0 + w)], bias=T.PF[:, 8:9])
 
     def visits(t):
-        fx = "FX%d" % t
+        fx, left, got = "FX%d" % t, [128, 128], [0, 0]
         for a in range(NR):
             nb, cl, cln = "NB%d" % a, "CL%d" % (a % 2), "CL%d" % (1 - a % 2)
             if a > 0 and t > 0:
                 apply_update(t - 1, a)
-            for m0, w, eng, _, first_op in CHUNKS:
+            for j0, (m0, w, eng, _, first_op) in enumerate(CHUNKS):
                 sl = slice(m0, m0 + w)
-                bank = "B%d" % nxt("b", 3)
+                bank = "B%d" % (m0 // 128)
                 win = T[nb][:, 0:H]
 
                 def C(n):
                     return (n, m0, m0 + w)
-                j0 = nxt("x", 3) if eng == "V" else nxt("s", 4)
-                x, s = ("XV%d" if eng == "V" else "GS%d") % j0, "SS%d" % j0
+                x, s = "X%d" % j0, "SS%d" % j0
                 for j, m in pieces(16 * w):
                     c, u = m0 + j // 16, 16 * m0 + j
                     src, rd = win.indirect(T[cl][:, c:c + m // 16]), [(nb, 0, H), (cl, c, c + m // 16)]
@@ -468,14 +487,21 @@ def build(core, T, topo):
                     else:
                         act(T[x][:, j:j + m], src, F.Copy, m * GC, rd, [(x, j, j + m)])
                 if eng == "V":
-                    extract(bank, 0, "E1", x, w)
+                    extract(bank, m0 % 128, "E1", x, w)
                 else:
                     for j, m in pieces(16 * w):
-                        db = "B%d" % (3 + nxt("u", 2))
+                        db = "B%d" % (3 + (m0 // 128 if SUBH else nxt("u", 2)))
                         subtract(db, fx, 16 * m0 + j, x, j, m)
                         act(T[s][:, j:j + m], T[db][:, 0:m], F.Sign, m, [W(db), HLF], [(s, j, j + m)], bias=T.PF[:, 6:7])
-                    extract(bank, 0, "E05", s, w)
-                P, pr, kc = T[bank][:, 0:w], (bank, 0, w), 2 * (4 * t + a) + (eng == "S")
+                    extract(bank, m0 % 128, "E05", s, w, True)
+                got[m0 // 128] += w
+                if JOIN:
+                    if got[m0 // 128] % 128:
+                        continue
+                    m0, w = m0 // 128 * 128, 128
+                    sl = slice(m0, m0 + w)
+                o = m0 % 128
+                P, pr, kc = T[bank][:, o:o + w], (bank, o, o + w), 4 * t + a
                 if first_op == "V":
                     ts(P, P, float(SLOPE), A.mult, w, [pr, ("KV", kc, kc + 1)], [pr], T.KV[:, kc:kc + 1], A.add)
                 else:
@@ -489,39 +515,48 @@ def build(core, T, topo):
                     act(T.SQ[:, sl], T.C32[:, sl], F.Square, w, [C("C32"), SQB], [C("SQ")], bias=T.PF[:, 5:6], scale=1.0 / 32)
                 else:
                     cp(T.CW[:, sl], T.CI[:, sl], w, [C("CI")], [C("CW")])
+                    left[m0 // 128] -= w
+                    if left[m0 // 128] == 0:
+                        finish(t, m0 // 128)
 
-    def election(t):
-        for h in range(2):
-            c = T.CW[:, 128 * h:128 * h + 128]
-            rd = ("CW", 128 * h, 128 * h + 128)
-            mms([(T.CT[:, 8 * h:8 * h + 8, 0:24], c, T.IDW[:], True, True, 4 * 192)], [rd, W("IDW")], [("CT", h, h + 1)])
-        act(T.CD[:], T.CT[:, :, 0:16], F.Copy, 256, [W("CT")], [W("CD")])
-        for h in range(2):
-            c = T.CW[:, 128 * h:128 * h + 128]
-            rd = ("CW", 128 * h, 128 * h + 128)
-            mms([(T.B3[:, 136 * h:136 * h + 136], c, T.DF[:], True, True, 4 * 136)], [rd, W("DF")], [("B3", 136 * h, 136 * h + 136)])
+    def election(h):
+        key, s = "KEY%d" % h, slice(8 * h, 8 * h + 8)
+        c, rd, ct, cd = T.CW[:, 128 * h:128 * h + 128], ("CW", 128 * h, 128 * h + 128), ("CT", h, h + 1), ("CD", h, h + 1)
+        mms([(T.CT[:, s, :], c, T.IDW[:], True, True, 4 * 256)], [rd, W("IDW")], [ct])
+        mms([(T[key][:, 136:272], c, T.DF[:], False, False, 4 * 136)], [rd, W("DF")], [W(key)])
+        act(T.CD[:, s, :], T.CT[:, s, 0:24], F.Copy, 192, [ct], [cd])
         for d in range(1, 9):
-            j = d % 3
+            j, b = nxt("e", 3), (d if d < 8 else 0)
             e = ("EQ", j, j + 1)
-            tt(T.EQ[:, j, :, 8:24], T.CT[:, :, d:d + 16], T.CD[:], A.is_equal, 256, [W("CT"), W("CD")], [e])
-            mms([(T.KEY[:, 0:272], T.IDK[:], T.EQ[:, j, :, o:o + 17], False, d == 8, 272) for o in ((8, 8 - d, 24 - d) if d < 8 else (8,))],
-                [e, W("IDK")], [W("KEY")])
+            tt(T.EQ[:, j, :, 8 - b:24], T.CT[:, s, 8 - b + d:24 + d], T.CD[:, s, 8 - b:24], A.is_equal, 8 * (16 + b), [ct, cd], [e])
+            mms([(T[key][:, 0:136], T.IDK[:], T.EQ[:, j, :, o:o + 17], False, d == 8, 136) for o in ((8, 8 - d) if d < 8 else (8,))],
+                [e, W("IDK")], [W(key)])
 
-    def pick(w, bank):
-        run, go, pk, wb = "RUN%d" % w, "GO%d" % w, "PICK%d" % w, "WB%d" % w
+    def pick(w, h):
+        key, run, go, pk, wb = "KEY%d" % h, "RUN%d" % w, "GO%d" % w, "PICK%d" % w, "WB%d" % (2 * w + h)
         if w:
-            ends(1, True)
-        scan(T[run][:], T["RST%d" % w][:], T.KEY[:, 0:272], A.add, A.min if w else A.max, 272, [W("RST%d" % w), W("KEY")], [W(run)])
-        tt(T[go][:, 1:272], T.KEY[:, 1:272], T[run][:, 0:271], A.is_ge if w else A.is_le, 272, [W("KEY"), W(run)], [W(go)])
-        scan(T[pk][:], T.B3[:, 0:272], T[go][:], A.add, A.mult, 272, [("B3", 0, 272), W(go)], [W(pk)])
-        hilo(wb, T[wb][:, 0:256:16], T[wb][:, 1:256:16], T[pk][:, 16:272:17], 16, [W(pk)])
-        mms([(T[bank][:, 128 * h:128 * h + 128], T[wb][:, 128 * h:128 * h + 128], T.ID[:], True, True, 128) for h in range(2)],
-            [W(wb), W("ID")], [(bank, 0, 256)])
+            ends(1, h, True)
+        scan(T[run][:], T["RST%d" % w][:], T[key][:, 0:136], A.add, A.min if w else A.max, 136, [W("RST%d" % w), (key, 0, 136)], [W(run)])
+        tt(T[go][:, 1:136], T[key][:, 1:136], T[run][:, 0:135], A.is_ge if w else A.is_le, 136, [(key, 0, 136), W(run)], [W(go)])
+        scan(T[pk][:], T[key][:, 136:272], T[go][:], A.add, A.mult, 136, [(key, 136, 272), W(go)], [W(pk)])
+        hilo(wb, T[wb][:, 0:128:16], T[wb][:, 1:128:16], T[pk][:, 16:136:17], 8, [W(pk)])
 
-    def headings_out(t):
-        pick(0, "B0")
-        c = 1024 + 256 * t
-        act(T.HT[:, c:c + 256], T.B0[:, 0:256], F.Copy, 256, [("B0", 0, 256)], [("HT", c, c + 256), W("KS1")], accum=T.KS1[:, 0:1])
+    def row(w, h, c0):
+        key, wb = "KEY%d" % h, "WB%d" % (2 * w + h)
+        mms([(T[key][:, c0:c0 + 128], T[wb][:], T.ID[:], True, True, 128)], [W(wb), W("ID")], [(key, c0, c0 + 128)])
+
+    def headings_out(t, h):
+        key, c = "KEY%d" % h, 1024 + 256 * t + 128 * h
+        row(0, h, 272)
+        act(T.HT[:, c:c + 128], T[key][:, 272:400], F.Copy, 128, [(key, 272, 400)], [("HT", c, c + 128), ("KS1", h, h + 1)],
+            accum=T.KS1[:, h:h + 1])
+
+    def finish(t, h):
+        election(h)
+        pick(0, h)
+        pick(1, h)
+        headings_out(t, h)
+        notes(t, h)
 
     def write_yh(t):
         c, y = 1024 + 256 * t, ("YH8", 256 * t, 256 * t + 256)
@@ -529,77 +564,77 @@ def build(core, T, topo):
         act(T.YH8[:, 256 * t:256 * t + 256], T.CT[0:8, 0:8, :], F.Copy, 256, [W("CT")], [y])
         dma("Y", T.yh[:, 256 * t:256 * t + 256], T.YH8[:, 256 * t:256 * t + 256], 2.5, [y], [])
 
-    def notes(t):
-        c, ov, ol = 1024 + 256 * t, "OUTV%d" % t, "OUTL%d" % t
-        pick(1, "B4")
-        act(T.LR[:], T.B4[:, 0:256], F.Copy, 256, [("B4", 0, 256)], [W("LR")])
-        mms([(T.B4[:, 256:512], T.BMW[:], T.LR[:], True, True, 256)], [W("BMW"), W("LR")], [("B4", 256, 512)])
-        extract("B3", 288, "E1", "LR", 16)
-        cp(T.LB[:], T.B4[:, 256:512], 256, [("B4", 256, 512)], [W("LB")])
-        for n in ("LF", "LU"):
-            cp(T[n][:], T.B3[:, 288:304], 16, [("B3", 288, 304)], [W(n)])
-        lo3, hi3, lo4 = ("B3", 0, 256), ("B3", 256, 512), ("B4", 0, 256)
-        act(T.OLD[:], T.NB0[:, 0:H].indirect(T.LU[:, 0:16]), F.Copy, 256 * GC, [("NB0", 0, H), W("LU")], [W("OLD")])
-        mms([(T.B3[:, 0:256], T.ID[:], T.FE[:, c:c + 256], True, False, 256), (T.B3[:, 0:256], T.IDN[:], T.OLD[:], False, True, 256)],
-            [W("ID"), W("IDN"), ("FE", c, c + 256), W("OLD")], [lo3])
-        ts(T.DC[:], T.B3[:, 0:256], 32.0, A.min, 256, [lo3], [W("DC")], -32.0, A.max)
-        mms([(T.B3[:, 256:512], T.ID[:], T.OLD[:], True, False, 256), (T.B3[:, 256:512], T.ID[:], T.DC[:], False, True, 256)],
-            [W("ID"), W("OLD"), W("DC")], [hi3])
-        act(T[ov][:, 0:256], T.B3[:, 256:512], F.Copy, 256, [hi3], [(ov, 0, 256)])
-        for lo in (0, 8):
-            for mb in range(lo, lo + 8):
-                n = 256 - 16 * mb
-                ts(T.EQT[:, mb, 0:n], T.LB[:, 16 * mb:256], T.LF[:, mb:mb + 1], A.is_equal, n * 0.5, [W("LB"), W("LF")], [("EQT", mb, mb + 1)])
-            lst = [(T.B4[:, 16 * mb + 16:256], T.BO[:], T.EQT[:, mb, 16:256 - 16 * mb], mb == 0, False, 240 - 16 * mb)
-                   for mb in range(lo, min(lo + 8, 15))]
-            if lo:
-                lst.append((T.B4[:, 0:16], T.BD[:], T.EQT[:, 0, 0:16], False, False, 16))
-                lst.append((T.B4[:, 16:256], T.BD[:], T.EQT[:, 1:16, 0:16], False, True, 240))
-            mms(lst, [W("BO"), W("BD"), ("EQT", 0, lo + 8)], [lo4])
-        tt(T.FL[:], T.B4[:, 0:256], T.THR[:], A.is_ge, 256, [lo4, W("THR")], [W("FL")])
-        extract("B4", 256, "EX", "FL", 16)
-        tt(T.OF[:], T.B4[:, 256:272], T.DUP[:], A.mult, 16, [("B4", 256, 272), W("DUP")], [W("OF")])
-        tt(T.OF[:], T.OF[:], T.LF[:], A.max, 32, [W("OF"), W("LF")], [W("OF")])
-        cp(T[ol][:], T.OF[:], 16, [W("OF")], [W(ol)])
-        scatter("NB0", ov, ol)
+    def notes(t, h):
+        key, c, ov, ol = "KEY%d" % h, 1024 + 256 * t + 128 * h, VW * t + 128 * h, 16 * t + 8 * h
+        K = T[key]
+        lr, lb, lf, lu, old, dc, fl, of, eqt = (n + str(h) for n in ("LR", "LB", "LF", "LU", "OLD", "DC", "FL", "OF", "EQT"))
+        r0, r1, r2, r3 = (key, 0, 128), (key, 128, 256), (key, 256, 272), (key, 272, 400)
+        row(1, h, 0)
+        act(T[lr][:], K[:, 0:128], F.Copy, 128, [r0], [W(lr)])
+        mms([(K[:, 128:256], T.BMW[:], T[lr][:], True, True, 128)], [W("BMW"), W(lr)], [r1])
+        extract(key, 256, "E1", lr, 8)
+        cp(T[lb][:], K[:, 128:256], 128, [r1], [W(lb)])
+        for n in (lf, lu):
+            cp(T[n][:], K[:, 256:264], 8, [r2], [W(n)])
+        for mb in range(8):
+            n = 128 - 16 * mb
+            ts(T[eqt][:, mb, 0:n], T[lb][:, 16 * mb:128], T[lf][:, mb:mb + 1], A.is_equal, n * 0.5, [W(lb), W(lf)], [(eqt, mb, mb + 1)])
+        act(T[old][:], T.NB0[:, 0:H].indirect(T[lu][:]), F.Copy, 128 * GC, [("NB0", 0, H), W(lu)], [W(old)])
+        mms([(K[:, 272:400], T.ID[:], T.FE[:, c:c + 128], True, False, 128), (K[:, 272:400], T.IDN[:], T[old][:], False, True, 128)],
+            [W("ID"), W("IDN"), ("FE", c, c + 128), W(old)], [r3])
+        mms([(K[:, 16 * mb + 16:128], T.BO[:], T[eqt][:, mb, 16:128 - 16 * mb], mb == 0, False, 112 - 16 * mb) for mb in range(7)]
+            + [(K[:, 0:16], T.BD[:], T[eqt][:, 0, 0:16], False, False, 16), (K[:, 16:128], T.BD[:], T[eqt][:, 1:8, 0:16], False, True, 112)],
+            [W("BO"), W("BD"), W(eqt)], [r0])
+        tt(T[fl][:], K[:, 0:128], T.THR[:], A.is_ge, 128, [r0, W("THR")], [W(fl)])
+        ts(T[dc][:], K[:, 272:400], 32.0, A.min, 128, [r3], [W(dc)], -32.0, A.max)
+        mms([(K[:, 128:256], T.ID[:], T[old][:], True, False, 128), (K[:, 128:256], T.ID[:], T[dc][:], False, True, 128)],
+            [W("ID"), W(old), W(dc)], [r1])
+        extract(key, 256, "EX", fl, 8)
+        tt(T[of][:], K[:, 256:264], T.DUP[:], A.mult, 8, [r2, W("DUP")], [W(of)])
+        act(T.NV0[:, ov:ov + 128], K[:, 128:256], F.Copy, 128, [r1], [("NV0", ov, ov + 128)])
+        tt(T[of][:], T[of][:], T[lf][:], A.max, 16, [W(of), W(lf)], [W(of)])
+        cp(T.NL0[:, ol:ol + 8], T[of][:], 8, [W(of)], [("NL0", ol, ol + 8)])
 
-    def scatter(nb, ov, ol):
-        vec(lambda q: q.tensor_copy(out=T[nb][:, 0:H + DUMMY].indirect(T[ol][:, 0:16]), in_=T[ov][:, 0:256]), 256 * 3.8,
-            [(ov, 0, 256), W(ol)], [(nb, 0, H + DUMMY)])
+    def scatter(t, a):
+        nb, nv, nl = "NB%d" % a, "NV%d" % a, "NL%d" % a
+        for h in (1, 0):
+            ov, ol = VW * t + 128 * h, 16 * t + 8 * h
+            cp(T[nb][:, 0:H + DUMMY].indirect(T[nl][:, ol:ol + 8]), T[nv][:, ov:ov + 128], 128 * 3.8,
+               [(nv, ov, ov + 128), (nl, ol, ol + 8)], [(nb, 0, H + DUMMY)])
 
-    def bias(t, a, src):
-        c = 2 * (4 * (t + 1) + a)
-        act(T.KV[:, c:c + 2], T.KV[:, 0:2], F.Identity, 2, [(src, 256, 257), ("KV", 0, 2)], [("KV", c, c + 2)], bias=T[src][:, 256:257])
+    def bias(t, a):
+        c, nv, k = 4 * (t + 1) + a, "NV%d" % a, VW * t + 256
+        act(T.KV[:, c:c + 1], T.KV[:, 0:1], F.Identity, 1, [(nv, k, k + 1), ("KV", 0, 1)], [("KV", c, c + 1)], bias=T[nv][:, k:k + 1])
 
     def kappa(t):
-        ov = "OUTV%d" % t
-        mms([(T.CT[:, 0, 0:1], T.ONES[:], T.KS1[:, 0:1], True, True, 256)], [W("ONES"), W("KS1")], [W("CT")])
+        k = VW * t + 256
+        mms([(T.CT[:, 0, 0:1], T.ONES[:], T.KS1[:, h:h + 1], h == 0, h == 1, 256) for h in range(2)], [W("ONES"), W("KS1")], [W("CT")])
         cp(T.KI[:, 0:1], T.CT[:, 0, 0:1], 1, [W("CT")], [W("KI")])
         ts(T.KJ[:, 0:1], T.KI[:, 0:1], 255 * 32, A.bitwise_and, 1, [W("KI")], [W("KJ")])
-        cp(T[ov][:, 256:257], T.KJ[:, 0:1], 1, [W("KJ")], [(ov, 256, 257)])
-        bias(t, 0, ov)
+        cp(T.NV0[:, k:k + 1], T.KJ[:, 0:1], 1, [W("KJ")], [("NV0", k, k + 1)])
+        bias(t, 0)
 
     sent = {}
+    UPDATE = (("NV%d", VW, "iv%d_%d"), ("NL%d", 16, "il%d_%d"))
 
     def send_update(t):
         dsts = [(rank - a) % NR for a in range(1, NR)]
         ids = [DstId(rid=addr(x)[0], pnc=addr(x)[1]) for x in dsts]
-        for nm, inn, sm in (("OUTV%d" % t, "INV%d_%d", "iv%d_%d"), ("OUTL%d" % t, "INL%d_%d", "il%d_%d")):
-            def f(q, nm=nm, inn=inn, sm=sm):
-                tr = RemoteDMATransfer(dst_ids=ids, dma_engine_mask=emask(cross), remote_sem=T.sem[sm % (rank, t)], srcs=[T[nm][:]],
-                                       dsts=[T[inn % (rel(rank, x), t)][:] for x in dsts])
+        for nm, w, sm in UPDATE:
+            def f(q, nm=nm, w=w, sm=sm):
+                tr = RemoteDMATransfer(dst_ids=ids, dma_engine_mask=emask(cross), remote_sem=T.sem[sm % (rank, t)],
+                                       srcs=[T[nm % 0][:, w * t:w * t + w]], dsts=[T[nm % rel(rank, x)][:, w * t:w * t + w] for x in dsts])
                 return q.remote_dma_fused([tr], local_sem=T.sem.lsend)
             num["lsend"] += len(cross)
-            bulk.append(add(gr, "G", f, 1.2, [W(nm)], [], "s", "lsend", num["lsend"], soft=bulk[-1:]))
+            bulk.append(add(gr, "G", f, 1.2, [(nm % 0, w * t, w * t + w)], [], "s", "lsend", num["lsend"], soft=bulk[-1:]))
         sent[t] = bulk[-1]
 
     def apply_update(t, a):
-        iv, il = "INV%d_%d" % (a, t), "INL%d_%d" % (a, t)
         src = (rank + a) % NR
-        for nm, sm in ((il, "il%d_%d"), (iv, "iv%d_%d")):
-            gr["nodes"][add(gr, "R", None, 0.0, [], [W(nm)], "r", sm % (src, t), len(cross), 3.5)]["soft"].add(sent[t])
-        bias(t, a, iv)
-        scatter("NB%d" % a, iv, il)
+        for nm, w, sm in UPDATE:
+            gr["nodes"][add(gr, "R", None, 0.0, [], [(nm % a, w * t, w * t + w)], "r", sm % (src, t), len(cross), 3.5)]["soft"].add(sent[t])
+        bias(t, a)
+        scatter(t, a)
 
     for t in range(RT):
         lists(t)
@@ -610,9 +645,7 @@ def build(core, T, topo):
     for t in range(RT):
         share_keys(t)
         visits(t)
-        election(t)
-        headings_out(t)
-        notes(t)
+        scatter(t, 0)
         if t + 1 < RT:
             gather_headings(t + 1)
             kappa(t)

@@ -7,18 +7,21 @@ KS = 130
 SLOPE = 613 * 32 + MOD * KS
 OFF = MOD * 512
 BV = -256 - MOD * (9 * KS + 1) - OFF
-CHUNKS = ((128, 64, "V", "V", "V"), (192, 64, "S", "S", "V"), (0, 72, "V", "S", "V"), (72, 56, "S", "S", "V"))
-SHARE = ("VS", "VS", "VS", "VS")
+CHUNKS = ((128, 72, "V", "V"), (200, 56, "S", "V"), (0, 72, "V", "V"), (72, 56, "S", "V"))
+HEADS = ("VSVS", "VSSS", "VSSS", "VSSS")
+SHARE = ("VS", "FF", "FF", "FF")
 EXPAND = "VVVVVVVVVVVVGGGG"
-PIECE = 512
-PASSES, WAKE = 6, 0.06
+PIECE = {"V": 640, "S": 512, "head": 640, "share": 512}
+PASSES, WAKE, SELF = 6, 0.06, 0.06
+OV, OS = 0.02, 0.06
 SUBH = 0
 JOIN = 1
 BIG = float(1 << 24)
 CYC, GC, PEC = 0.83e-3 * 1.25, 1.56, 0.6e-3
 
 SCRATCH = {}
-SEMAPHORES = ["cv", "cs", "cp", "cg", "lsend"] + ["d%d" % j for j in range(30)] + ["ls%d" % j for j in range(10)]
+SEMAPHORES = ["cv", "cs", "cp", "cg", "lsend"] + ["d%d" % j for j in range(30)] + ["ls%d" % j for j in range(18)]
+SEMAPHORES += [s + "%d_%d" % (t, h) for s in ("fo", "fb") for t in range(RT) for h in range(2)]
 
 
 def _buf(names, cols, dtype, where="sbuf", rows=128):
@@ -28,7 +31,7 @@ def _buf(names, cols, dtype, where="sbuf", rows=128):
 
 B16, F32, I32, U16 = "bfloat16", "float32", "int32", "uint16"
 _buf("NB0 NB1 NB2 NB3", H + DUMMY, B16)
-_buf("FE HT", 2048, B16)
+_buf("FE HT XG0 XG1", 2048, B16)
 _buf("FX0 FX1 FX2 FX3 XH0 XH1 XH2 XH3", 4096, B16)
 for _j, _c in enumerate(CHUNKS):
     _buf("X%d SS%d" % (_j, _j) if _c[2] == "S" else "X%d" % _j, 16 * _c[1], B16)
@@ -59,7 +62,7 @@ _buf("E1 E05 EX", 144, B16)
 _buf("FL0 FL1 OLD0 OLD1 DC0 DC1 LR0 LR1 WB0 WB1 WB2 WB3", 128, B16)
 _buf("C32 SQ CW", 256, F32)
 _buf("THR", 128, F32)
-_buf("GH0 GH1", PIECE, B16)
+_buf("GH0 GH1", 512, B16)
 _buf("CL0 CL1", 256, U16)
 _buf("LB0 LB1", 128, U16)
 _buf("TI CI", 256, I32)
@@ -111,7 +114,7 @@ def schedule(gr):
     succ, pred = [[] for _ in nodes], [[] for _ in nodes]
     for n in nodes:
         for j in n["deps"] | n["soft"]:
-            gap = (nodes[j]["lat"] + (WAKE if nodes[j]["eng"] != n["eng"] else 0.0)) if j in n["deps"] else 0.0
+            gap = nodes[j]["lat"] + (WAKE if nodes[j]["eng"] != n["eng"] else SELF * (n["eng"] != "P")) if j in n["deps"] else 0.0
             succ[j].append((n["id"], gap))
             pred[n["id"]].append((j, gap))
 
@@ -208,7 +211,7 @@ def build(core, T, topo):
         return (n, 0, 1 << 20)
 
     def vec(fn, cyc, reads, writes):
-        return add(gr, "V", fn, max(64, cyc) * CYC + 0.04, reads, writes)
+        return add(gr, "V", fn, max(64, cyc) * CYC + OV, reads, writes)
 
     def gps(fn, cyc, writes, reads=()):
         return add(gr, "G", fn, cyc * CYC + 0.17, reads, writes)
@@ -240,7 +243,7 @@ def build(core, T, topo):
             if accum is not None:
                 return q.activation(out=out, in_=in_, func=func, bias=bias, scale=scale, accum_out=accum)
             return q.activation(out=out, in_=in_, func=func, bias=bias, scale=scale)
-        return add(gr, "S", f, max(64, cyc) * CYC + 0.1, reads, writes, soft=soft)
+        return add(gr, "S", f, max(64, cyc) * CYC + OS, reads, writes, soft=soft)
 
     def mms(lst, reads, writes, soft=()):
         def f(q):
@@ -254,8 +257,9 @@ def build(core, T, topo):
         return mms(lst + [(T[bank][:, c0:c0 + n], T[en][:, 15 - i:143 - i], T[x][:, i:16 * n:16], i == 0 and not signs, i == 15, n)
                           for i in range(16)], [(x, 0, 16 * n), W(en), W("BMW"), W("HALVES")], [(bank, c0, c0 + n)])
 
-    def pieces(n):
-        return [(j, min(PIECE, n - j)) for j in range(0, n, PIECE)]
+    def pieces(n, most=512):
+        step = -(-n // (32 * -(-n // most))) * 32
+        return [(j, min(step, n - j)) for j in range(0, n, step)]
 
     def subtract(bank, fx, f0, x, x0, m):
         mms([(T[bank][:, 0:m], T.ID[:], T[fx][:, f0:f0 + m], True, False, m)], [W("ID"), (fx, f0, f0 + m)], [W(bank)])
@@ -290,8 +294,11 @@ def build(core, T, topo):
     eqc("MB", 160, 3, 1.0)
     eqc("MK", 16, 1, 1.0)
     for y in range(16):
-        act(T.MIP[:, 160 * y:160 * y + 160], T.MB[:], F.Copy, 160, [W("MB"), W("MK")], [("MIP", 160 * y, 160 * y + 160)],
-            scale=T.MK[:, y:y + 1], soft=[lastd["S"]])
+        out, rd, wr = T.MIP[:, 160 * y:160 * y + 160], [W("MB"), W("MK")], [("MIP", 160 * y, 160 * y + 160)]
+        if y % 3 == 0:
+            act(out, T.MB[:], F.Copy, 160, rd, wr, scale=T.MK[:, y:y + 1], soft=[lastd["S"]])
+        else:
+            ts(out, T.MB[:], T.MK[:, y:y + 1], A.mult, 80, rd, wr)
     for n, v in (("E1", 1.0), ("E05", 0.5), ("EX", 0.0625)):
         eqc(n, 144, 4, v)
     for n, v in (("ID", 1.0), ("IDN", -1.0), ("IDK", 4096.0)):
@@ -334,8 +341,12 @@ def build(core, T, topo):
     for b in range(2):
         bank = "B%d" % b
         mms([(T[bank][:, 64 * y:64 * y + 64], sel(8 * b + y, d), T.HDB[:, 64 * d:64 * d + 64], d == 0, d == 1, 64)
-             for y in range(8) for d in (0, 1)], [W("MIP"), W("HDB")], [(bank, 0, 512)])
-        act(T.HT[:, 512 * b:512 * b + 512], T[bank][:], F.Copy, 512, [(bank, 0, 512)], [("HT", 512 * b, 512 * b + 512)])
+             for y in range(8) for d in (0, 1)], [("MIP", 1280 * b, 1280 * b + 1280), W("HDB")], [(bank, 0, 512)])
+        out, rd, wr = T.HT[:, 512 * b:512 * b + 512], [(bank, 0, 512)], [("HT", 512 * b, 512 * b + 512)]
+        if b:
+            cp(out, T[bank][:], 512, rd, wr)
+        else:
+            act(out, T[bank][:], F.Copy, 512, rd, wr)
 
     def lists(t):
         c = 256 * t
@@ -416,22 +427,41 @@ def build(core, T, topo):
     def shares(t):
         fx, xh, n = "FX%d" % t, "XH%d" % t, 1024 + 256 * t
         for h in range(2):
-            for j, m in pieces(HALF):
+            for j, m in pieces(HALF, PIECE["share"] if SHARE[t][h] == "V" else 512):
                 u = HALF * h + j
                 c = 256 * t + u // 16
                 src, rd = T.FE[:, 0:n].indirect(T.LT[:, c:c + m // 16]), [("FE", 0, n), ("LT", c, c + m // 16)]
                 if SHARE[t][h] == "V":
                     tt(T[xh][:, u:u + m], src, T[fx][:, u:u + m], A.min, m * GC, rd + [(fx, u, u + m)], [(xh, u, u + m)])
+                elif SHARE[t][h] == "F":
+                    act(T["XG%d" % h][:, j:j + m], src, F.Copy, m * GC, rd, [("XG%d" % h, j, j + m)])
+                    if j + m == HALF:
+                        fold(t, h)
                 else:
                     x = "GH%d" % nxt("h", 2)
                     act(T[x][:, 0:m], src, F.Copy, m * GC, rd, [W(x)])
                     subtract("B5", fx, u, x, 0, m)
                     act(T[xh][:, u:u + m], T.B5[:, 0:m], F.Relu, m, [W("B5")], [(xh, u, u + m)])
 
+    folds = []
+
+    def fold(t, h):
+        fx, xh, xg, u = "FX%d" % t, "XH%d" % t, "XG%d" % h, slice(HALF * h, HALF * h + HALF)
+        rid, pid = topo.addr(helper(core, T, topo))[0:2]
+        s = "ls%d" % nxt("ls", 99)
+
+        def f(q):
+            tr = RemoteDMATransfer(dst_ids=[DstId(rid=rid, pnc=pid)], dma_engine_mask=emask(local), remote_sem=T.sem["fo%d_%d" % (t, h)],
+                                   srcs=[T[xg][:], T[fx][:, u]], dsts=[T[xh][:, u]], alu_op=3)
+            return q.remote_dma_fused([tr], local_sem=T.sem[s])
+        folds.append(add(gr, "G", f, 1.0, [W(xg), (fx, u.start, u.stop)], [], "s", s, len(local), 6.0, soft=folds[-1:] + [bulk[-1]]))
+        back = add(gr, "R", None, 0.0, [], [(xh, u.start, u.stop)], "r", "fb%d_%d" % (t, h), len(wide), 12.0)
+        gr["nodes"][back]["soft"].add(folds[-1])
+
     def share_keys(t):
         xh = "XH%d" % t
         for h in range(2):
-            sg = "BMW" if SHARE[t][h] == "V" else "BMN"
+            sg = "BMN" if SHARE[t][h] == "S" else "BMW"
             for k0 in (0, 8):
                 mms([(T["KEY%d" % h][:, k:136:17], T[xh][:, HALF * h + k:HALF * h + HALF:16], T[sg][:, 0:128:16], k == 0, False, 64)
                      for k in range(k0, k0 + 8)], [(xh, HALF * h, HALF * h + HALF), W(sg)], [W("KEY%d" % h)])
@@ -442,9 +472,9 @@ def build(core, T, topo):
 
     def gather_headings(t):
         n, got = 1024 + 256 * t, [0, 0]
-        for j0, (m0, w, _, eng, _) in enumerate(CHUNKS):
-            x = "X%d" % j0
-            for j, m in pieces(16 * w):
+        for j0, (m0, w, _, _) in enumerate(CHUNKS):
+            x, eng = "X%d" % j0, HEADS[t][j0]
+            for j, m in pieces(16 * w, PIECE["head"]):
                 c = 256 * t + m0 + j // 16
                 src = T.HT[:, 0:n].indirect(T.LT[:, c:c + m // 16])
                 rd, wr = [("HT", 0, n), ("LT", c, c + m // 16)], [(x, j, j + m)]
@@ -471,7 +501,7 @@ def build(core, T, topo):
             nb, cl, cln = "NB%d" % a, "CL%d" % (a % 2), "CL%d" % (1 - a % 2)
             if a > 0 and t > 0:
                 apply_update(t - 1, a)
-            for j0, (m0, w, eng, _, first_op) in enumerate(CHUNKS):
+            for j0, (m0, w, eng, first_op) in enumerate(CHUNKS):
                 sl = slice(m0, m0 + w)
                 bank = "B%d" % (m0 // 128)
                 win = T[nb][:, 0:H]
@@ -479,7 +509,7 @@ def build(core, T, topo):
                 def C(n):
                     return (n, m0, m0 + w)
                 x, s = "X%d" % j0, "SS%d" % j0
-                for j, m in pieces(16 * w):
+                for j, m in pieces(16 * w, PIECE[eng]):
                     c, u = m0 + j // 16, 16 * m0 + j
                     src, rd = win.indirect(T[cl][:, c:c + m // 16]), [(nb, 0, H), (cl, c, c + m // 16)]
                     if eng == "V":
@@ -656,8 +686,35 @@ def build(core, T, topo):
     return gr
 
 
+def helper(core, T, topo):
+    return [c for c in topo.cores_of(core) if topo.die(c) == topo.die(core) and T.rank_of(c) is None][0]
+
+
+def hand_back(core, home, T, topo):
+    gr = {"nodes": [], "acc": {}, "bank": {}}
+    es = topo.engines(core, home)
+    half = [e for e in es if e not in topo.engines(home, [c for c in T.cores if topo.chip(c) != topo.chip(home)][0])]
+    rid, pid = topo.addr(home)[0:2]
+    last = []
+    for t in range(RT):
+        for h in range(2):
+            if SHARE[t][h] == "F":
+                xh, reg = T["XH%d" % t][:, HALF * h:HALF * h + HALF], [("XH%d" % t, h, h + 1)]
+                add(gr, "R", None, 0.0, [], reg, "r", "fo%d_%d" % (t, h), len(half), soft=last[-1:])
+                last.append(add(gr, "G", lambda q, xh=xh, t=t, h=h: q.remote_dma(xh, xh, T.sem["fb%d_%d" % (t, h)], T.sem.lsend, pid, rid,
+                                                                               topo.mask(core, home)),
+                                1.0, reg, [], "s", "lsend", len(es) * (len(last) + 1), soft=last[-1:]))
+    return gr
+
+
+def program(core, T, topo):
+    if T.rank_of(core) is not None:
+        return build(core, T, topo)
+    homes = [c for c in T.cores if helper(c, T, topo) == core]
+    return hand_back(core, homes[0], T, topo) if homes else None
+
+
 def rank_program(g, core, T, topo):
-    if T.rank_of(core) is None:
-        return
-    gr = build(core, T, topo)
-    emit_all(gr, schedule(gr), g, T)
+    gr = program(core, T, topo)
+    if gr and gr["nodes"]:
+        emit_all(gr, schedule(gr), g, T)

@@ -7,20 +7,32 @@ KS = 130
 SLOPE = 613 * 32 + MOD * KS
 OFF = MOD * 512
 BV = -256 - MOD * (9 * KS + 1) - OFF
-CHUNKS = ((128, 72, "V", "V"), (200, 56, "S", "V"), (0, 72, "V", "V"), (72, 56, "S", "V"))
-HEADS = ("VSVS", "VSSS", "VSSS", "VSSS")
-SHARE = ("VS", "FF", "FF", "FF")
-EXPAND = "VVVVVVVVVVVVGGGG"
-PIECE = {"V": 640, "S": 512, "head": 640, "share": 512}
-PASSES, WAKE, SELF = 6, 0.06, 0.06
-OV, OS = 0.02, 0.06
-SUBH = 0
-JOIN = 1
+SPLIT = ((64, 64), (76, 72), (76, 72), (76, 72))
+HEADS = (((("S", 64), ("S", 64)), (("V", 64), ("S", 64))),) * 4
+SCALE = "SSSS"
+SHARE = ("VV", "FF", "FF", "FF")
+EXPAND = "VVVVVVVVVVSSSSSS"
+PIECE = {"V": 640, "S": 512, "head": 320, "share": 512}
+PASSES = ((0.0, "fffflll"), (0.12, "fffflll"), (0.25, "fffflll"), (0.4, "fffflll"), (0.2, "flflfl"))
+CASES = ((1.0, 1.0, 1.0), (1.25, 0.7, 0.85), (0.75, 1.6, 1.0), (1.0, 1.0, 1.3))
+WAKE, SELF = 0.1, 0.1
+OV, OS = 0.005, 0.005
+QUART, NEAR = 1024, (2, 3, 0, 1)
+ARRIVE = (9.0, 14.0, 4.0, 5.0, 12.0, 4.0, 24.0)
+EARLY = 2
 BIG = float(1 << 24)
-CYC, GC, PEC = 0.83e-3 * 1.25, 1.56, 0.6e-3
+CYC, PEC = 0.83e-3 * 1.25, 0.52e-3
+
+
+GC, SC, GCALL = 1.56, 3.8, 0.8
+
+
+def gcost(n, scatter=False):
+    return 55.5 + int((SC if scatter else GC) * n)
+
 
 SCRATCH = {}
-SEMAPHORES = ["cv", "cs", "cp", "cg", "lsend"] + ["d%d" % j for j in range(30)] + ["ls%d" % j for j in range(18)]
+SEMAPHORES = ["cv", "cs", "cp", "cg", "lsend"] + ["d%d" % j for j in range(30)] + ["ls%d" % j for j in range(26)]
 SEMAPHORES += [s + "%d_%d" % (t, h) for s in ("fo", "fb") for t in range(RT) for h in range(2)]
 
 
@@ -31,27 +43,27 @@ def _buf(names, cols, dtype, where="sbuf", rows=128):
 
 B16, F32, I32, U16 = "bfloat16", "float32", "int32", "uint16"
 _buf("NB0 NB1 NB2 NB3", H + DUMMY, B16)
-_buf("FE HT XG0 XG1", 2048, B16)
+_buf("FE HT", 2048, B16)
+_buf("XG0 XG1 XG2 XG3", 4096, B16)
 _buf("FX0 FX1 FX2 FX3 XH0 XH1 XH2 XH3", 4096, B16)
-for _j, _c in enumerate(CHUNKS):
-    _buf("X%d SS%d" % (_j, _j) if _c[2] == "S" else "X%d" % _j, 16 * _c[1], B16)
-VW = 264
+_buf("X0 X1 SS0 SS1", 2048, B16)
+VW = 296
 _buf("NV0 NV1 NV2 NV3", RT * VW, B16)
 _buf("NL0 NL1 NL2 NL3", RT * 16, U16)
 for _t in range(RT - 1):
     for _a in range(NR):
-        SEMAPHORES += ["iv%d_%d" % (_a, _t), "il%d_%d" % (_a, _t)]
+        SEMAPHORES += ["iv%d_%d" % (_a, _t)]
 for _a in range(1, NR):
-    SEMAPHORES += ["n%d_0" % _a, "n%d_1" % _a]
+    SEMAPHORES += ["n%d_%d" % (_a, _h) for _h in range(4)]
 _buf("CMP", 1024, I32)
 _buf("LT", 1024, U16)
 _buf("HD", 64, I32)
-_buf("HDB BMW BMN BO BD ID IDN IDK", 128, B16)
+_buf("HDB BMW BO BD ID IDN IDK", 128, B16)
 _buf("RI", 160, F32)
 _buf("RG ONES", 128, F32)
 _buf("PI PM PG KI KJ", 2, I32)
 _buf("PF", 16, F32)
-_buf("MK", 16, F32)
+_buf("MK PL", 16, F32)
 _buf("DUP LF0 LF1 OF0 OF1", 8, F32)
 _buf("LU0 LU1", 8, U16)
 _buf("KV", 16, F32)
@@ -62,21 +74,20 @@ _buf("E1 E05 EX", 144, B16)
 _buf("FL0 FL1 OLD0 OLD1 DC0 DC1 LR0 LR1 WB0 WB1 WB2 WB3", 128, B16)
 _buf("C32 SQ CW", 256, F32)
 _buf("THR", 128, F32)
-_buf("GH0 GH1", 512, B16)
 _buf("CL0 CL1", 256, U16)
 _buf("LB0 LB1", 128, U16)
 _buf("TI CI", 256, I32)
 _buf("IDW", [8, 32], F32)
 _buf("DF", [8, 17], F32)
 _buf("CD", [16, 24], F32)
-_buf("RST0 RST1 RUN0 RUN1 GO0 GO1 PICK0 PICK1", 136, F32)
-_buf("EQ", [3, 8, 32], B16)
+_buf("RST0 RST1 RUN0 RUN1 RUN2 RUN3 GO0 GO1 GO2 GO3 PICK0 PICK1 PICK2 PICK3", 136, F32)
+_buf("EQ", [6, 8, 32], B16)
 _buf("ENDS", 16, B16)
 _buf("EQT0 EQT1", [8, 128], B16)
 _buf("KS1", 2, F32)
 _buf("YH8", 1024, F32, rows=8)
-_buf("B0 B1 B3 B4 B5 KEY0 KEY1", 512, F32, "psum")
-_buf("CT", [16, 32], F32, "psum")
+_buf("B0 B1 B3 B4 KEY0 KEY1", 512, F32, "psum")
+_buf("CT0 CT1", [16, 32], F32, "psum")
 PSUM = set(n for n in SCRATCH if SCRATCH[n][0] == "psum")
 CSEM = {"V": "cv", "S": "cs", "P": "cp", "G": "cg"}
 
@@ -118,7 +129,7 @@ def schedule(gr):
             succ[j].append((n["id"], gap))
             pred[n["id"]].append((j, gap))
 
-    def lay(rank, after, before, at):
+    def flow(rank, after, before, at, ahead):
         left = [len(b) for b in before]
         free, ready, end, order = {}, {}, [0.0] * len(nodes), []
         for n in nodes:
@@ -128,7 +139,8 @@ def schedule(gr):
                 ready[n["eng"]].add(n["id"])
         while len(order) < len(nodes):
             s, e = min((max(free[e], min(at[i] for i in ready[e])), e) for e in ready if ready[e])
-            i = max((k for k in ready[e] if at[k] <= s), key=lambda k: (rank[k], -k))
+            i = max((k for k in ready[e] if at[k] <= s + ahead), key=lambda k: (rank[k] - 4 * max(0.0, at[k] - s), -k))
+            s = max(s, at[i])
             ready[e].discard(i)
             end[i] = s + nodes[i]["cost"]
             if e != "R":
@@ -141,17 +153,57 @@ def schedule(gr):
                     ready[nodes[k]["eng"]].add(k)
         return order, end
 
+    def lay(rank, after, before, at, ahead):
+        left = [len(b) for b in before]
+        busy, end, placed = dict((n["eng"], []) for n in nodes), [0.0] * len(nodes), []
+        ready = set(n["id"] for n in nodes if left[n["id"]] == 0)
+        while ready:
+            i = max(ready, key=lambda k: (rank[k], -k))
+            ready.discard(i)
+            s, cost, line = at[i], nodes[i]["cost"], busy[nodes[i]["eng"]]
+            if nodes[i]["eng"] != "R":
+                lo, hi = 0, len(line)
+                while lo < hi:
+                    mid = (lo + hi) // 2
+                    lo, hi = (mid + 1, hi) if line[mid][1] <= s else (lo, mid)
+                while lo < len(line) and line[lo][0] < s + cost:
+                    s = max(s, line[lo][1])
+                    lo += 1
+                line.insert(lo, (s, s + cost))
+            end[i] = s + cost
+            placed.append((s, len(placed), i))
+            for k, gap in after[i]:
+                left[k] -= 1
+                at[k] = max(at[k], end[i] + gap)
+                if left[k] == 0:
+                    ready.add(k)
+        return [x[2] for x in sorted(placed)], end
+
     rank = [0.0] * len(nodes)
     for n in reversed(nodes):
         rank[n["id"]] = max([n["lat"]] + [rank[s] + gap for s, gap in succ[n["id"]]]) + n["cost"] + 0.05
-    best = None
-    for _ in range(PASSES):
-        order, end = lay(rank, succ, pred, [n["est"] for n in nodes])
-        total = max(end[n["id"]] + n["lat"] for n in nodes)
-        if best is None or total < best[0]:
-            best = (total, order)
-        rank = lay(end, pred, succ, [n["lat"] for n in nodes])[1]
-    gr["total"] = best[0]
+
+    def span(order, gather, wake, remote):
+        free, end = {}, [0.0] * len(nodes)
+        for i in order:
+            n = nodes[i]
+            s = max([n["est"] * remote, free.get(n["eng"], 0.0)]
+                    + [end[j] + gap * (remote if nodes[j]["eng"] == "R" else wake if nodes[j]["kind"] == "c" else 1.0) for j, gap in pred[i]])
+            end[i] = s + n["cost"] * (gather if n.get("gather") else 1.0)
+            if n["eng"] != "R":
+                free[n["eng"]] = end[i]
+        return max(end[n["id"]] + n["lat"] for n in nodes)
+
+    best, first = None, rank
+    for ahead, passes in PASSES:
+        rank = first
+        for rule in passes:
+            rule = flow if rule == "f" else lay
+            order, end = rule(rank, succ, pred, [n["est"] for n in nodes], ahead)
+            total = sum(span(order, *case) for case in CASES)
+            if best is None or total < best[0]:
+                best = (total, order)
+            rank = rule(end, pred, succ, [n["lat"] for n in nodes], ahead)[1]
     return best[1]
 
 
@@ -210,11 +262,16 @@ def build(core, T, topo):
     def W(n):
         return (n, 0, 1 << 20)
 
-    def vec(fn, cyc, reads, writes):
-        return add(gr, "V", fn, max(64, cyc) * CYC + OV, reads, writes)
+    def timed(eng, fn, cyc, reads, writes, soft=()):
+        i = add(gr, eng, fn, max(64, cyc) * CYC + OV, reads, writes, soft=soft)
+        gr["nodes"][i]["gather"] = cyc % 1 == 0.5
+        return i
 
-    def gps(fn, cyc, writes, reads=()):
-        return add(gr, "G", fn, cyc * CYC + 0.17, reads, writes)
+    def vec(fn, cyc, reads, writes):
+        return timed("V", fn, cyc, reads, writes)
+
+    def gps(fn, cyc, writes, reads=(), soft=()):
+        return add(gr, "G", fn, cyc * CYC + 0.17, reads, writes, soft=soft)
 
     def dma(eng, out, in_, lat, reads, writes, soft=()):
         s = "d%d" % nxt("d", 99)
@@ -243,7 +300,7 @@ def build(core, T, topo):
             if accum is not None:
                 return q.activation(out=out, in_=in_, func=func, bias=bias, scale=scale, accum_out=accum)
             return q.activation(out=out, in_=in_, func=func, bias=bias, scale=scale)
-        return add(gr, "S", f, max(64, cyc) * CYC + OS, reads, writes, soft=soft)
+        return timed("S", f, cyc, reads, writes, soft)
 
     def mms(lst, reads, writes, soft=()):
         def f(q):
@@ -252,10 +309,11 @@ def build(core, T, topo):
             return ins
         return add(gr, "P", f, sum(max(64, x[5]) for x in lst) * PEC + 0.03, reads, writes, soft=soft)
 
-    def extract(bank, c0, en, x, n, signs=False):
+    def extract(bank, c0, en, x, n, q0=0, signs=False):
         lst = [(T[bank][:, c0:c0 + n], T.BMW[:], T.HALVES[:, 0:n], True, False, n)] if signs else []
-        return mms(lst + [(T[bank][:, c0:c0 + n], T[en][:, 15 - i:143 - i], T[x][:, i:16 * n:16], i == 0 and not signs, i == 15, n)
-                          for i in range(16)], [(x, 0, 16 * n), W(en), W("BMW"), W("HALVES")], [(bank, c0, c0 + n)])
+        u = 16 * q0
+        return mms(lst + [(T[bank][:, c0:c0 + n], T[en][:, 15 - i:143 - i], T[x][:, u + i:u + 16 * n:16], i == 0 and not signs, i == 15, n)
+                          for i in range(16)], [(x, u, u + 16 * n), W(en), W("BMW"), W("HALVES")], [(bank, c0, c0 + n)])
 
     def pieces(n, most=512):
         step = -(-n // (32 * -(-n // most))) * 32
@@ -265,13 +323,18 @@ def build(core, T, topo):
         mms([(T[bank][:, 0:m], T.ID[:], T[fx][:, f0:f0 + m], True, False, m)], [W("ID"), (fx, f0, f0 + m)], [W(bank)])
         mms([(T[bank][:, 0:m], T.IDN[:], T[x][:, x0:x0 + m], False, True, m)], [W("IDN"), (x, x0, x0 + m)], [W(bank)])
 
+    cores = T.cores
+    onchip = [r for r in range(NR) if r != rank and topo.chip(cores[r]) == topo.chip(core)][0]
+    far = [r for r in range(NR) if topo.chip(cores[r]) != topo.chip(core)]
+    first = rank if (rank - 1) % NR in far else onchip
+
     def load(e, n, src, c0, c1, lat):
         dma(e, T[n][:, c0:c1], T[src][:, c0:c1], lat, [], [(n, c0, c1)])
     dma("Y", T.HD[:], T.hd[:], 2.2, [], [W("HD")])
     load("S", "FE", "feat", 1024, 1280, 2.6)
     load("S", "CMP", "comp", 0, 256, 3.2)
-    for h in (0, 1):
-        load("Y", "NB0", "lim", HALF * h, HALF * h + HALF, 6.0 + 2.5 * h)
+    for j, h in enumerate((0, 2, 1, 3) if rank == first else (0, 2, 3, 1)):
+        load("Y", "NB0", "lim", QUART * h, QUART * h + QUART, 4.2 + 1.2 * j)
     load("S", "FE", "feat", 0, 1024, 10.0)
     load("S", "FE", "feat", 1280, 2048, 11.0)
     load("Y", "CMP", "comp", 256, 1024, 13.0)
@@ -303,7 +366,7 @@ def build(core, T, topo):
         eqc(n, 144, 4, v)
     for n, v in (("ID", 1.0), ("IDN", -1.0), ("IDK", 4096.0)):
         eqc(n, 128, 0, v)
-    for n, v in (("BMW", 1.0), ("BMN", -1.0), ("BO", 2.0)):
+    for n, v in (("BMW", 1.0), ("BO", 2.0)):
         eqc(n, 128, 2, v, "RG")
     ts(T.DUP[:], T.DUP[:], T.PF[:, 1:2], A.add, 16, [W("DUP"), ("PF", 1, 2)], [W("DUP")])
     for y in range(16):
@@ -319,22 +382,22 @@ def build(core, T, topo):
         fill(T["RST%d" % w][:], 0.0, 136, W("RST%d" % w))
         for c in (slice(0, 1), slice(16, 136, 17)):
             fill(T["RST%d" % w][:, c], BIG if w else -BIG, 16, W("RST%d" % w))
-        fill(T["GO%d" % w][:, 0:1], 0.0, 16, W("GO%d" % w))
         fill(T.ENDS[:, 8 * w:8 * w + 8], BIG / 16 if w else -BIG / 16, 16, W("ENDS"))
     for w in range(4):
+        fill(T["GO%d" % w][:, 0:1], 0.0, 16, W("GO%d" % w))
         fill(T["WB%d" % w][:], 0.0, 64, W("WB%d" % w))
     fill(T.EQ[:, :, :, 24], 0.0, 24, W("EQ"))
     fill(T.ONES[:], 32.0, 128, W("ONES"))
     fill(T.KV[:, 0:4], float(BV), 4, ("KV", 0, 4))
     fill(T.HALVES[:], 0.5, 64, W("HALVES"))
     for t in range(RT - 1):
-        fill(T.NV0[:, VW * t + 256:VW * t + VW], 0.0, 4, ("NV0", VW * t + 256, VW * t + VW))
+        fill(T.NV0[:, VW * t + 256:VW * t + 264], 0.0, 4, ("NV0", VW * t + 256, VW * t + 264))
 
     def hilo(dst, hi, lo, src, n, reads):
-        cp(hi, src, n, reads, [W(dst)])
-        tt(lo, src, hi, A.subtract, 2 * n, reads + [W(dst)], [W(dst)])
+        cp(hi, src, n, reads, [dst])
+        tt(lo, src, hi, A.subtract, 2 * n, reads + [dst], [dst])
 
-    hilo("HDB", T.HDB[:, 0:64], T.HDB[:, 64:128], T.HD[:], 64, [W("HD")])
+    hilo(W("HDB"), T.HDB[:, 0:64], T.HDB[:, 64:128], T.HD[:], 64, [W("HD")])
 
     def sel(i, d):
         return T.MIP[:, 160 * i + 16 + i - d:160 * i + 144 + i - d]
@@ -352,29 +415,25 @@ def build(core, T, topo):
         c = 256 * t
         cp(T.LT[:, c:c + 256], T.CMP[:, c:c + 256], 256, [("CMP", c, c + 256)], [("LT", c, c + 256)])
 
-    def expand(t):
+    def expand(t, soft=()):
         fx, c = "FX%d" % t, 1024 + 256 * t
         done = []
         for k in range(16):
             out, in_, rd, wr = T[fx][:, k:4096:16], T.FE[:, c:c + 256], [("FE", c, c + 256)], [(fx + "k", k, k + 1)]
             e = EXPAND[k] if t == 0 else "G"
             if e == "G":
-                done.append(gps(lambda q, out=out, in_=in_: q.affine_select(out, in_, [[0, 256]], A.is_equal, 0.0, 0, 0), 512, wr, rd))
+                done.append(gps(lambda q, out=out, in_=in_: q.affine_select(out, in_, [[0, 256]], A.is_equal, 0.0, 0, 0), 512, wr, rd, soft))
             elif e == "V":
                 done.append(cp(out, in_, 128, rd, wr))
             else:
                 done.append(act(out, in_, F.Copy, 256, rd, wr))
         gr["acc"][fx] = [(j, 0, 4096, 1) for j in done]
 
-    cores = T.cores
-
     def rel(src, dst):
         return (src - dst) % NR
 
     def addr(dst):
         return topo.addr(cores[dst])[0:2]
-    onchip = [r for r in range(NR) if r != rank and topo.chip(cores[r]) == topo.chip(core)][0]
-    far = [r for r in range(NR) if topo.chip(cores[r]) != topo.chip(core)]
     cross = topo.engines(core, cores[far[0]])
     local = [e for e in topo.engines(core, cores[onchip]) if e not in cross]
     wide = local + cross
@@ -383,156 +442,146 @@ def build(core, T, topo):
     def emask(es):
         return sum(1 << e for e in es)
 
-    def send(src, h, dst, es):
+    def send(src, h, dst, es, n=1):
         s = "ls%d" % nxt("ls", 99)
         rid, pid = addr(dst)
         buf = "NB%d" % rel(src, rank)
-        out = T["NB%d" % rel(src, dst)][:, HALF * h:HALF * h + HALF]
-        in_ = T[buf][:, HALF * h:HALF * h + HALF]
+        c0, c1 = QUART * h, QUART * (h + n)
+        out, in_ = T["NB%d" % rel(src, dst)][:, c0:c1], T[buf][:, c0:c1]
         rs = T.sem["n%d_%d" % (rel(src, dst), h)]
-        bulk.append(add(gr, "G", lambda q: q.remote_dma(out, in_, rs, T.sem[s], pid, rid, emask(es)), 0.8,
-                        [(buf, HALF * h, HALF * h + HALF)], [], "s", s, len(es), 6.0, soft=bulk[-1:]))
+        bulk.append(add(gr, "G", lambda q: q.remote_dma(out, in_, rs, T.sem[s], pid, rid, emask(es)), GCALL,
+                        [(buf, c0, c1)], [], "s", s, len(es), 6.0, soft=bulk[-1:]))
 
-    def recv(src, h, est, n):
+    def recv(src, h, est, es, n=1):
         a = rel(src, rank)
-        add(gr, "R", None, 0.0, [], [("NB%d" % a, HALF * h, HALF * h + HALF)], "r", "n%d_%d" % (a, h), n, est=est)
+        add(gr, "R", None, 0.0, [], [("NB%d" % a, QUART * h, QUART * (h + n))], "r", "n%d_%d" % (a, h), len(es), est=est)
 
-    first = rank if (rank - 1) % NR in far else onchip
     o_first = [r for r in far if (r - 1) % NR not in far][0]
     o_second = [r for r in far if r != o_first][0]
     gate, mygate = (first - 1) % NR, (o_first - 1) % NR
-    nown = len(wide) if rank == first else len(local)
-    recv(onchip, 1, 14.0, nown)
-    recv(onchip, 0, 14.0, nown)
-    late = 0.0 if rank == mygate else 6.0
-    nin = len(cross) if rank == mygate else len(wide)
-    for src, e in ((o_first, 22.0), (o_second, 30.0)):
-        for h in range(2):
-            recv(src, h, e + late, nin)
-    if rank == first:
-        for h in range(2):
+    PORT = ((("first", 0), ("first", 1), ("second", 2), ("second", 3)), (("second", 0), ("first", 2), ("first", 3), ("second", 1)))
+    for j, h in enumerate(NEAR):
+        recv(onchip, h, 5.0 + (j + 1) * ARRIVE[0] / 4, local)
+    landed = {}
+    for port in PORT:
+        for j, (who, h) in enumerate(port):
+            landed[who, h] = 5.0 + (j + 1) * ARRIVE[1] / 4
+    for who, src, es, late in (("first", o_first, local, ARRIVE[2]), ("second", o_second, wide, ARRIVE[3])):
+        for h in range(4):
+            if rank == mygate:
+                recv(src, h, landed[who, h], cross)
+            elif h % 2 == 0:
+                recv(src, h, max(landed[who, h], landed[who, h + 1]) + late, es, 2)
+    mine = PORT[rank != first]
+    for j in range(4):
+        who, h = mine[j]
+        if j < 2 and (who == "first") == (rank == first):
             send(rank, h, gate, cross)
-        for h in range(2):
-            send(rank, h, onchip, local)
-    else:
-        for h in range(2):
-            send(rank, h, onchip, wide)
-        for h in range(2):
-            send(rank, h, gate, cross)
+            mine = mine[:j] + (None,) + mine[j + 1:]
+        send(rank, NEAR[j], onchip, local)
+    for x in mine:
+        if x:
+            send(first if x[0] == "first" else rank + onchip - first, x[1], gate, cross)
     if rank == mygate:
-        for src in (o_first, o_second):
-            for h in range(2):
-                send(src, h, onchip, wide)
+        for src, es in ((o_first, local), (o_second, wide)):
+            for h in (0, 2):
+                send(src, h, onchip, es, 2)
+    notes_sent = bulk[-1]
 
     def shares(t):
         fx, xh, n = "FX%d" % t, "XH%d" % t, 1024 + 256 * t
         for h in range(2):
-            for j, m in pieces(HALF, PIECE["share"] if SHARE[t][h] == "V" else 512):
+            for j, m in pieces(HALF, PIECE["share"]):
                 u = HALF * h + j
                 c = 256 * t + u // 16
                 src, rd = T.FE[:, 0:n].indirect(T.LT[:, c:c + m // 16]), [("FE", 0, n), ("LT", c, c + m // 16)]
                 if SHARE[t][h] == "V":
-                    tt(T[xh][:, u:u + m], src, T[fx][:, u:u + m], A.min, m * GC, rd + [(fx, u, u + m)], [(xh, u, u + m)])
-                elif SHARE[t][h] == "F":
-                    act(T["XG%d" % h][:, j:j + m], src, F.Copy, m * GC, rd, [("XG%d" % h, j, j + m)])
-                    if j + m == HALF:
-                        fold(t, h)
+                    tt(T[xh][:, u:u + m], src, T[fx][:, u:u + m], A.min, gcost(m), rd + [(fx, u, u + m)], [(xh, u, u + m)])
                 else:
-                    x = "GH%d" % nxt("h", 2)
-                    act(T[x][:, 0:m], src, F.Copy, m * GC, rd, [W(x)])
-                    subtract("B5", fx, u, x, 0, m)
-                    act(T[xh][:, u:u + m], T.B5[:, 0:m], F.Relu, m, [W("B5")], [(xh, u, u + m)])
+                    act(T["XG%d" % t][:, u:u + m], src, F.Copy, gcost(m), rd, [("XG%d" % t, u, u + m)])
+
+    def folds_of(t):
+        for h in range(2):
+            if SHARE[t][h] == "F":
+                fold(t, h)
 
     folds = []
 
     def fold(t, h):
-        fx, xh, xg, u = "FX%d" % t, "XH%d" % t, "XG%d" % h, slice(HALF * h, HALF * h + HALF)
+        fx, xh, xg, u = "FX%d" % t, "XH%d" % t, "XG%d" % t, slice(HALF * h, HALF * h + HALF)
         rid, pid = topo.addr(helper(core, T, topo))[0:2]
         s = "ls%d" % nxt("ls", 99)
 
         def f(q):
             tr = RemoteDMATransfer(dst_ids=[DstId(rid=rid, pnc=pid)], dma_engine_mask=emask(local), remote_sem=T.sem["fo%d_%d" % (t, h)],
-                                   srcs=[T[xg][:], T[fx][:, u]], dsts=[T[xh][:, u]], alu_op=3)
+                                   srcs=[T[xg][:, u], T[fx][:, u]], dsts=[T[xh][:, u]], alu_op=3)
             return q.remote_dma_fused([tr], local_sem=T.sem[s])
-        folds.append(add(gr, "G", f, 1.0, [W(xg), (fx, u.start, u.stop)], [], "s", s, len(local), 6.0, soft=folds[-1:] + [bulk[-1]]))
-        back = add(gr, "R", None, 0.0, [], [(xh, u.start, u.stop)], "r", "fb%d_%d" % (t, h), len(wide), 12.0)
+        folds.append(add(gr, "G", f, GCALL + 0.2, [(xg, u.start, u.stop), (fx, u.start, u.stop)], [], "s", s, len(local), 6.0, soft=folds[-1:] + [notes_sent]))
+        back = add(gr, "R", None, 0.0, [], [(xh, u.start, u.stop)], "r", "fb%d_%d" % (t, h), len(wide), ARRIVE[6 if t else 4])
         gr["nodes"][back]["soft"].add(folds[-1])
 
     def share_keys(t):
         xh = "XH%d" % t
         for h in range(2):
-            sg = "BMN" if SHARE[t][h] == "S" else "BMW"
             for k0 in (0, 8):
-                mms([(T["KEY%d" % h][:, k:136:17], T[xh][:, HALF * h + k:HALF * h + HALF:16], T[sg][:, 0:128:16], k == 0, False, 64)
-                     for k in range(k0, k0 + 8)], [(xh, HALF * h, HALF * h + HALF), W(sg)], [W("KEY%d" % h)])
+                mms([(T["KEY%d" % h][:, k:136:17], T[xh][:, HALF * h + k:HALF * h + HALF:16], T.BMW[:, 0:128:16], k == 0, False, 64)
+                     for k in range(k0, k0 + 8)], [(xh, HALF * h, HALF * h + HALF), W("BMW")], [W("KEY%d" % h)])
             ends(0, h, False)
 
     def ends(w, h, alone):
         mms([(T["KEY%d" % h][:, 16:136:17], T.ID[:], T.ENDS[:, 8 * w:8 * w + 8], alone, alone, 8)], [W("ID"), W("ENDS")], [("KEY%d" % h, 0, 136)])
 
     def gather_headings(t):
-        n, got = 1024 + 256 * t, [0, 0]
-        for j0, (m0, w, _, _) in enumerate(CHUNKS):
-            x, eng = "X%d" % j0, HEADS[t][j0]
-            for j, m in pieces(16 * w, PIECE["head"]):
-                c = 256 * t + m0 + j // 16
-                src = T.HT[:, 0:n].indirect(T.LT[:, c:c + m // 16])
-                rd, wr = [("HT", 0, n), ("LT", c, c + m // 16)], [(x, j, j + m)]
-                if eng == "V":
-                    cp(T[x][:, j:j + m], src, m * GC, rd, wr)
-                else:
-                    act(T[x][:, j:j + m], src, F.Copy, m * GC, rd, wr)
-            bank = "B%d" % (m0 // 128)
-            o = m0 % 128
-            extract(bank, o, "E1", x, w)
-            cp(T.CL0[:, m0:m0 + w], T[bank][:, o:o + w], w, [(bank, o, o + w)], [("CL0", m0, m0 + w)])
-            got[m0 // 128] += w
-            if JOIN:
-                if got[m0 // 128] % 128:
-                    continue
-                m0, w, o = m0 // 128 * 128, 128, 0
-            sl, pr, P = slice(m0, m0 + w), (bank, o, o + w), T[bank][:, o:o + w]
-            act(T.C32[:, sl], P, F.Identity, w, [pr, MOFF], [("C32", m0, m0 + w)], bias=T.PF[:, 7:8], scale=32.0)
-            act(T.SQ[:, sl], P, F.Square, w, [pr, P16], [("SQ", m0, m0 + w)], bias=T.PF[:, 8:9])
+        n = 1024 + 256 * t
+        for h in (1, 0):
+            x, bank, o = "X%d" % h, "B%d" % h, 0
+            for eng, w in HEADS[t][h]:
+                m0 = 128 * h + o
+                for j, m in pieces(16 * w, PIECE["head"]):
+                    c, u = 256 * t + m0 + j // 16, 16 * o + j
+                    src = T.HT[:, 0:n].indirect(T.LT[:, c:c + m // 16])
+                    rd, wr = [("HT", 0, n), ("LT", c, c + m // 16)], [(x, u, u + m)]
+                    if eng == "V":
+                        cp(T[x][:, u:u + m], src, gcost(m), rd, wr)
+                    else:
+                        act(T[x][:, u:u + m], src, F.Copy, gcost(m), rd, wr)
+                extract(bank, o, "E1", x, w, o)
+                cp(T.CL0[:, m0:m0 + w], T[bank][:, o:o + w], w, [(bank, o, o + w)], [("CL0", m0, m0 + w)])
+                o += w
+            m0 = 128 * h
+            sl, pr, P = slice(m0, m0 + 128), (bank, 0, 128), T[bank][:, 0:128]
+            act(T.C32[:, sl], P, F.Identity, 128, [pr, MOFF], [("C32", m0, m0 + 128)], bias=T.PF[:, 7:8], scale=32.0)
+            act(T.SQ[:, sl], P, F.Square, 128, [pr, P16], [("SQ", m0, m0 + 128)], bias=T.PF[:, 8:9])
 
     def visits(t):
-        fx, left, got = "FX%d" % t, [128, 128], [0, 0]
+        fx = "FX%d" % t
         for a in range(NR):
             nb, cl, cln = "NB%d" % a, "CL%d" % (a % 2), "CL%d" % (1 - a % 2)
             if a > 0 and t > 0:
                 apply_update(t - 1, a)
-            for j0, (m0, w, eng, first_op) in enumerate(CHUNKS):
+            for h in (1, 0):
+                x, s, bank, m0, w = "X%d" % h, "SS%d" % h, "B%d" % h, 128 * h, 128
+                v = SPLIT[t][h]
+                for eng, o, n in (("V", 0, v), ("S", v, 128 - v)):
+                    for j, m in pieces(16 * n, PIECE[eng]) if n else []:
+                        c, u = m0 + o + j // 16, 16 * o + j
+                        f0 = 16 * m0 + u
+                        src, rd = T[nb][:, 0:H].indirect(T[cl][:, c:c + m // 16]), [(nb, 0, H), (cl, c, c + m // 16)]
+                        if eng == "V":
+                            tt(T[x][:, u:u + m], src, T[fx][:, f0:f0 + m], A.is_lt, gcost(m), rd + [(fx, f0, f0 + m)], [(x, u, u + m)])
+                        else:
+                            db = "B%d" % (3 + nxt("u", 2))
+                            act(T[x][:, u:u + m], src, F.Copy, gcost(m), rd, [(x, u, u + m)])
+                            subtract(db, fx, f0, x, u, m)
+                            act(T[s][:, u:u + m], T[db][:, 0:m], F.Sign, m, [W(db), HLF], [(s, u, u + m)], bias=T.PF[:, 6:7])
+                    if n:
+                        extract(bank, o, "E1" if eng == "V" else "E05", x if eng == "V" else s, n, o, eng == "S")
                 sl = slice(m0, m0 + w)
-                bank = "B%d" % (m0 // 128)
-                win = T[nb][:, 0:H]
 
                 def C(n):
                     return (n, m0, m0 + w)
-                x, s = "X%d" % j0, "SS%d" % j0
-                for j, m in pieces(16 * w, PIECE[eng]):
-                    c, u = m0 + j // 16, 16 * m0 + j
-                    src, rd = win.indirect(T[cl][:, c:c + m // 16]), [(nb, 0, H), (cl, c, c + m // 16)]
-                    if eng == "V":
-                        tt(T[x][:, j:j + m], src, T[fx][:, u:u + m], A.is_lt, m * GC, rd + [(fx, u, u + m)], [(x, j, j + m)])
-                    else:
-                        act(T[x][:, j:j + m], src, F.Copy, m * GC, rd, [(x, j, j + m)])
-                if eng == "V":
-                    extract(bank, m0 % 128, "E1", x, w)
-                else:
-                    for j, m in pieces(16 * w):
-                        db = "B%d" % (3 + (m0 // 128 if SUBH else nxt("u", 2)))
-                        subtract(db, fx, 16 * m0 + j, x, j, m)
-                        act(T[s][:, j:j + m], T[db][:, 0:m], F.Sign, m, [W(db), HLF], [(s, j, j + m)], bias=T.PF[:, 6:7])
-                    extract(bank, m0 % 128, "E05", s, w, True)
-                got[m0 // 128] += w
-                if JOIN:
-                    if got[m0 // 128] % 128:
-                        continue
-                    m0, w = m0 // 128 * 128, 128
-                    sl = slice(m0, m0 + w)
-                o = m0 % 128
-                P, pr, kc = T[bank][:, o:o + w], (bank, o, o + w), 4 * t + a
-                if first_op == "V":
+                P, pr, kc = T[bank][:, 0:w], (bank, 0, w), 4 * t + a
+                if SCALE[a] == "V":
                     ts(P, P, float(SLOPE), A.mult, w, [pr, ("KV", kc, kc + 1)], [pr], T.KV[:, kc:kc + 1], A.add)
                 else:
                     act(P, P, F.Identity, w, [pr, ("KV", kc, kc + 1)], [pr], bias=T.KV[:, kc:kc + 1], scale=float(SLOPE))
@@ -545,31 +594,29 @@ def build(core, T, topo):
                     act(T.SQ[:, sl], T.C32[:, sl], F.Square, w, [C("C32"), SQB], [C("SQ")], bias=T.PF[:, 5:6], scale=1.0 / 32)
                 else:
                     cp(T.CW[:, sl], T.CI[:, sl], w, [C("CI")], [C("CW")])
-                    left[m0 // 128] -= w
-                    if left[m0 // 128] == 0:
-                        finish(t, m0 // 128)
+                    finish(t, h)
 
     def election(h):
-        key, s = "KEY%d" % h, slice(8 * h, 8 * h + 8)
-        c, rd, ct, cd = T.CW[:, 128 * h:128 * h + 128], ("CW", 128 * h, 128 * h + 128), ("CT", h, h + 1), ("CD", h, h + 1)
-        mms([(T.CT[:, s, :], c, T.IDW[:], True, True, 4 * 256)], [rd, W("IDW")], [ct])
+        key, s, CT = "KEY%d" % h, slice(8 * h, 8 * h + 8), T["CT%d" % h]
+        c, rd, ct, cd = T.CW[:, 128 * h:128 * h + 128], ("CW", 128 * h, 128 * h + 128), W("CT%d" % h), ("CD", h, h + 1)
+        mms([(CT[:, 0:8, :], c, T.IDW[:], True, True, 4 * 256)], [rd, W("IDW")], [ct])
         mms([(T[key][:, 136:272], c, T.DF[:], False, False, 4 * 136)], [rd, W("DF")], [W(key)])
-        act(T.CD[:, s, :], T.CT[:, s, 0:24], F.Copy, 192, [ct], [cd])
+        act(T.CD[:, s, :], CT[:, 0:8, 0:24], F.Copy, 192, [ct], [cd])
         for d in range(1, 9):
-            j, b = nxt("e", 3), (d if d < 8 else 0)
+            j, b = 3 * h + d % 3, (d if d < 8 else 0)
             e = ("EQ", j, j + 1)
-            tt(T.EQ[:, j, :, 8 - b:24], T.CT[:, s, 8 - b + d:24 + d], T.CD[:, s, 8 - b:24], A.is_equal, 8 * (16 + b), [ct, cd], [e])
+            tt(T.EQ[:, j, :, 8 - b:24], CT[:, 0:8, 8 - b + d:24 + d], T.CD[:, s, 8 - b:24], A.is_equal, 8 * (16 + b), [ct, cd], [e])
             mms([(T[key][:, 0:136], T.IDK[:], T.EQ[:, j, :, o:o + 17], False, d == 8, 136) for o in ((8, 8 - d) if d < 8 else (8,))],
                 [e, W("IDK")], [W(key)])
 
     def pick(w, h):
-        key, run, go, pk, wb = "KEY%d" % h, "RUN%d" % w, "GO%d" % w, "PICK%d" % w, "WB%d" % (2 * w + h)
+        key, (run, go, pk, wb) = "KEY%d" % h, (n + str(2 * w + h) for n in ("RUN", "GO", "PICK", "WB"))
         if w:
             ends(1, h, True)
         scan(T[run][:], T["RST%d" % w][:], T[key][:, 0:136], A.add, A.min if w else A.max, 136, [W("RST%d" % w), (key, 0, 136)], [W(run)])
         tt(T[go][:, 1:136], T[key][:, 1:136], T[run][:, 0:135], A.is_ge if w else A.is_le, 136, [(key, 0, 136), W(run)], [W(go)])
         scan(T[pk][:], T[key][:, 136:272], T[go][:], A.add, A.mult, 136, [(key, 136, 272), W(go)], [W(pk)])
-        hilo(wb, T[wb][:, 0:128:16], T[wb][:, 1:128:16], T[pk][:, 16:136:17], 8, [W(pk)])
+        hilo(W(wb), T[wb][:, 0:128:16], T[wb][:, 1:128:16], T[pk][:, 16:136:17], 8, [W(pk)])
 
     def row(w, h, c0):
         key, wb = "KEY%d" % h, "WB%d" % (2 * w + h)
@@ -590,8 +637,8 @@ def build(core, T, topo):
 
     def write_yh(t):
         c, y = 1024 + 256 * t, ("YH8", 256 * t, 256 * t + 256)
-        mms([(T.CT[0:8, 0:8, :], T.BMW[:, 0:128:16], T.HT[:, c:c + 256], True, True, 256)], [W("BMW"), ("HT", c, c + 256)], [W("CT")])
-        act(T.YH8[:, 256 * t:256 * t + 256], T.CT[0:8, 0:8, :], F.Copy, 256, [W("CT")], [y])
+        mms([(T.CT0[0:8, 0:8, :], T.BMW[:, 0:128:16], T.HT[:, c:c + 256], True, True, 256)], [W("BMW"), ("HT", c, c + 256)], [W("CT0")])
+        act(T.YH8[:, 256 * t:256 * t + 256], T.CT0[0:8, 0:8, :], F.Copy, 256, [W("CT0")], [y])
         dma("Y", T.yh[:, 256 * t:256 * t + 256], T.YH8[:, 256 * t:256 * t + 256], 2.5, [y], [])
 
     def notes(t, h):
@@ -609,7 +656,7 @@ def build(core, T, topo):
         for mb in range(8):
             n = 128 - 16 * mb
             ts(T[eqt][:, mb, 0:n], T[lb][:, 16 * mb:128], T[lf][:, mb:mb + 1], A.is_equal, n * 0.5, [W(lb), W(lf)], [(eqt, mb, mb + 1)])
-        act(T[old][:], T.NB0[:, 0:H].indirect(T[lu][:]), F.Copy, 128 * GC, [("NB0", 0, H), W(lu)], [W(old)])
+        act(T[old][:], T.NB0[:, 0:H].indirect(T[lu][:]), F.Copy, gcost(128), [("NB0", 0, H), W(lu)], [W(old)])
         mms([(K[:, 272:400], T.ID[:], T.FE[:, c:c + 128], True, False, 128), (K[:, 272:400], T.IDN[:], T[old][:], False, True, 128)],
             [W("ID"), W("IDN"), ("FE", c, c + 128), W(old)], [r3])
         mms([(K[:, 16 * mb + 16:128], T.BO[:], T[eqt][:, mb, 16:128 - 16 * mb], mb == 0, False, 112 - 16 * mb) for mb in range(7)]
@@ -624,12 +671,15 @@ def build(core, T, topo):
         act(T.NV0[:, ov:ov + 128], K[:, 128:256], F.Copy, 128, [r1], [("NV0", ov, ov + 128)])
         tt(T[of][:], T[of][:], T[lf][:], A.max, 16, [W(of), W(lf)], [W(of)])
         cp(T.NL0[:, ol:ol + 8], T[of][:], 8, [W(of)], [("NL0", ol, ol + 8)])
+        if t + 1 < RT:
+            hi = VW * t + 264 + 8 * h
+            hilo(("NV0", hi, hi + 24), T.NV0[:, hi:hi + 8], T.NV0[:, hi + 16:hi + 24], T[of][:], 8, [W(of)])
 
     def scatter(t, a):
         nb, nv, nl = "NB%d" % a, "NV%d" % a, "NL%d" % a
         for h in (1, 0):
             ov, ol = VW * t + 128 * h, 16 * t + 8 * h
-            cp(T[nb][:, 0:H + DUMMY].indirect(T[nl][:, ol:ol + 8]), T[nv][:, ov:ov + 128], 128 * 3.8,
+            cp(T[nb][:, 0:H + DUMMY].indirect(T[nl][:, ol:ol + 8]), T[nv][:, ov:ov + 128], gcost(128, True),
                [(nv, ov, ov + 128), (nl, ol, ol + 8)], [(nb, 0, H + DUMMY)])
 
     def bias(t, a):
@@ -638,40 +688,45 @@ def build(core, T, topo):
 
     def kappa(t):
         k = VW * t + 256
-        mms([(T.CT[:, 0, 0:1], T.ONES[:], T.KS1[:, h:h + 1], h == 0, h == 1, 256) for h in range(2)], [W("ONES"), W("KS1")], [W("CT")])
-        cp(T.KI[:, 0:1], T.CT[:, 0, 0:1], 1, [W("CT")], [W("KI")])
+        mms([(T.CT1[:, 0, 0:1], T.ONES[:], T.KS1[:, h:h + 1], h == 0, h == 1, 256) for h in range(2)], [W("ONES"), W("KS1")], [W("CT1")])
+        cp(T.KI[:, 0:1], T.CT1[:, 0, 0:1], 1, [W("CT1")], [W("KI")])
         ts(T.KJ[:, 0:1], T.KI[:, 0:1], 255 * 32, A.bitwise_and, 1, [W("KI")], [W("KJ")])
         cp(T.NV0[:, k:k + 1], T.KJ[:, 0:1], 1, [W("KJ")], [("NV0", k, k + 1)])
         bias(t, 0)
 
     sent = {}
-    UPDATE = (("NV%d", VW, "iv%d_%d"), ("NL%d", 16, "il%d_%d"))
+
+    def lanes(other):
+        return cross
 
     def send_update(t):
-        dsts = [(rank - a) % NR for a in range(1, NR)]
-        ids = [DstId(rid=addr(x)[0], pnc=addr(x)[1]) for x in dsts]
-        for nm, w, sm in UPDATE:
-            def f(q, nm=nm, w=w, sm=sm):
-                tr = RemoteDMATransfer(dst_ids=ids, dma_engine_mask=emask(cross), remote_sem=T.sem[sm % (rank, t)],
-                                       srcs=[T[nm % 0][:, w * t:w * t + w]], dsts=[T[nm % rel(rank, x)][:, w * t:w * t + w] for x in dsts])
-                return q.remote_dma_fused([tr], local_sem=T.sem.lsend)
-            num["lsend"] += len(cross)
-            bulk.append(add(gr, "G", f, 1.2, [(nm % 0, w * t, w * t + w)], [], "s", "lsend", num["lsend"], soft=bulk[-1:]))
-        sent[t] = bulk[-1]
+        c = slice(VW * t, VW * t + VW)
+        for a in range(1, NR):
+            dst = (rank - a) % NR
+            (rid, pid), es = addr(dst), lanes(dst)
+            num["lsend"] += len(es)
+            bulk.append(add(gr, "G", lambda q, a=a, rid=rid, pid=pid, es=es: q.remote_dma(
+                T["NV%d" % a][:, c], T.NV0[:, c], T.sem["iv%d_%d" % (a, t)], T.sem.lsend, pid, rid, emask(es)),
+                GCALL, [("NV0", c.start, c.stop)], [], "s", "lsend", num["lsend"], soft=bulk[-1:]))
+            sent[t, a] = bulk[-1]
 
     def apply_update(t, a):
-        src = (rank + a) % NR
-        for nm, w, sm in UPDATE:
-            gr["nodes"][add(gr, "R", None, 0.0, [], [(nm % a, w * t, w * t + w)], "r", sm % (src, t), len(cross), 3.5)]["soft"].add(sent[t])
+        nv, nl, c = "NV%d" % a, "NL%d" % a, VW * t
+        add(gr, "R", None, 0.0, [], [(nv, c, c + VW)], "r", "iv%d_%d" % (a, t), len(lanes((rank + a) % NR)), ARRIVE[5], soft=[sent[t, a]])
         bias(t, a)
+        tt(T.PL[:], T[nv][:, c + 264:c + 280], T[nv][:, c + 280:c + 296], A.add, 32, [(nv, c + 264, c + 296)], [W("PL")])
+        cp(T[nl][:, 16 * t:16 * t + 16], T.PL[:], 16, [W("PL")], [(nl, 16 * t, 16 * t + 16)])
         scatter(t, a)
 
     for t in range(RT):
         lists(t)
+    for t in range(EARLY):
         expand(t)
     gather_headings(0)
     for t in range(RT):
         shares(t)
+    for t in range(EARLY):
+        folds_of(t)
     for t in range(RT):
         share_keys(t)
         visits(t)
@@ -680,6 +735,9 @@ def build(core, T, topo):
             gather_headings(t + 1)
             kappa(t)
             send_update(t)
+        if t + EARLY < RT:
+            expand(t + EARLY, bulk[-1:])
+            folds_of(t + EARLY)
         write_yh(t)
     for j, e in ((0, "S"), (1, "Y")):
         dma(e, T.yl[:, HALF * j:HALF * j + HALF], T.NB0[:, HALF * j:HALF * j + HALF], 5.0, [("NB0", HALF * j, HALF * j + HALF)], [])

@@ -7,18 +7,20 @@ KS = 130
 SLOPE = 613 * 32 + MOD * KS
 OFF = MOD * 512
 BV = -256 - MOD * (9 * KS + 1) - OFF
-SPLIT = ((64, 64), (76, 72), (76, 72), (76, 72))
-HEADS = (((("S", 64), ("S", 64)), (("V", 64), ("S", 64))),) * 4
+SPLIT = (((72, 72),) * 4, ((72, 68),) * 4)
+HEADS = (((("V", 64), ("S", 64)), (("V", 64), ("S", 64))),) + (((("V", 64), ("S", 64)), (("S", 64), ("S", 64))),) * 3
 SCALE = "SSSS"
-SHARE = ("VV", "FF", "FF", "FF")
+SHARE = ("VS", "LL", "LL", "LL")
 EXPAND = "VVVVVVVVVVSSSSSS"
 PIECE = {"V": 640, "S": 512, "head": 320, "share": 512}
 PASSES = ((0.0, "fffflll"), (0.12, "fffflll"), (0.25, "fffflll"), (0.4, "fffflll"), (0.2, "flflfl"))
 CASES = ((1.0, 1.0, 1.0), (1.25, 0.7, 0.85), (0.75, 1.6, 1.0), (1.0, 1.0, 1.3))
+SHORT = (0.0,)
 WAKE, SELF = 0.1, 0.1
 OV, OS = 0.005, 0.005
 QUART, NEAR = 1024, (2, 3, 0, 1)
-ARRIVE = (9.0, 14.0, 4.0, 5.0, 12.0, 4.0, 24.0)
+ARRIVE = (9.0, 14.0, 4.0, 5.0, 12.0, 4.0, 22.0, 7.0)
+WHOLE = 0
 EARLY = 2
 BIG = float(1 << 24)
 CYC, PEC = 0.83e-3 * 1.25, 0.52e-3
@@ -52,13 +54,13 @@ _buf("NV0 NV1 NV2 NV3", RT * VW, B16)
 _buf("NL0 NL1 NL2 NL3", RT * 16, U16)
 for _t in range(RT - 1):
     for _a in range(NR):
-        SEMAPHORES += ["iv%d_%d" % (_a, _t)]
+        SEMAPHORES += ["iv%d_%d" % (_a, _t) if _a else "wh%d" % _t]
 for _a in range(1, NR):
     SEMAPHORES += ["n%d_%d" % (_a, _h) for _h in range(4)]
 _buf("CMP", 1024, I32)
 _buf("LT", 1024, U16)
 _buf("HD", 64, I32)
-_buf("HDB BMW BO BD ID IDN IDK", 128, B16)
+_buf("HDB BMW BMN ID IDN IDK", 128, B16)
 _buf("RI", 160, F32)
 _buf("RG ONES", 128, F32)
 _buf("PI PM PG KI KJ", 2, I32)
@@ -70,10 +72,9 @@ _buf("KV", 16, F32)
 _buf("HALVES", 128, B16)
 _buf("MB", 160, B16)
 _buf("MIP", 16 * 160, B16)
-_buf("E1 E05 EX", 144, B16)
-_buf("FL0 FL1 OLD0 OLD1 DC0 DC1 LR0 LR1 WB0 WB1 WB2 WB3", 128, B16)
+_buf("E1 E05", 144, B16)
+_buf("OLD0 OLD1 DC0 DC1 LR0 LR1 WB0 WB1 WB2 WB3", 128, B16)
 _buf("C32 SQ CW", 256, F32)
-_buf("THR", 128, F32)
 _buf("CL0 CL1", 256, U16)
 _buf("LB0 LB1", 128, U16)
 _buf("TI CI", 256, I32)
@@ -82,8 +83,9 @@ _buf("DF", [8, 17], F32)
 _buf("CD", [16, 24], F32)
 _buf("RST0 RST1 RUN0 RUN1 RUN2 RUN3 GO0 GO1 GO2 GO3 PICK0 PICK1 PICK2 PICK3", 136, F32)
 _buf("EQ", [6, 8, 32], B16)
-_buf("ENDS", 16, B16)
-_buf("EQT0 EQT1", [8, 128], B16)
+_buf("ENDS", 8, B16)
+_buf("EQT0 EQT1 FL0 FL1 EARLIER", 576, B16)
+RUNS = [(144 * b, 16 * b + 16) if b < 4 else (144 * (8 - b) - 16 * b - 16, 16 * b + 16) for b in range(8)]
 _buf("KS1", 2, F32)
 _buf("YH8", 1024, F32, rows=8)
 _buf("B0 B1 B3 B4 KEY0 KEY1", 512, F32, "psum")
@@ -195,10 +197,11 @@ def schedule(gr):
         return max(end[n["id"]] + n["lat"] for n in nodes)
 
     best, first = None, rank
-    for ahead, passes in PASSES:
+    for ahead, passes, short in [p + (s,) for p in PASSES for s in SHORT]:
         rank = first
         for rule in passes:
             rule = flow if rule == "f" else lay
+            rank = [r + (0.0 if n.get("gather") else short) for r, n in zip(rank, nodes)]
             order, end = rule(rank, succ, pred, [n["est"] for n in nodes], ahead)
             total = sum(span(order, *case) for case in CASES)
             if best is None or total < best[0]:
@@ -309,19 +312,21 @@ def build(core, T, topo):
             return ins
         return add(gr, "P", f, sum(max(64, x[5]) for x in lst) * PEC + 0.03, reads, writes, soft=soft)
 
-    def extract(bank, c0, en, x, n, q0=0, signs=False):
-        lst = [(T[bank][:, c0:c0 + n], T.BMW[:], T.HALVES[:, 0:n], True, False, n)] if signs else []
+    def extract(bank, c0, en, x, n, q0=0, signs=False, out=None):
+        out = T[bank][:, c0:c0 + n] if out is None else out
+        lst = [(out, T.BMW[:], T.HALVES[:, 0:n], True, False, n)] if signs else []
         u = 16 * q0
-        return mms(lst + [(T[bank][:, c0:c0 + n], T[en][:, 15 - i:143 - i], T[x][:, u + i:u + 16 * n:16], i == 0 and not signs, i == 15, n)
+        return mms(lst + [(out, T[en][:, 15 - i:143 - i], T[x][:, u + i:u + 16 * n:16], i == 0 and not signs, i == 15, n)
                           for i in range(16)], [(x, u, u + 16 * n), W(en), W("BMW"), W("HALVES")], [(bank, c0, c0 + n)])
 
     def pieces(n, most=512):
         step = -(-n // (32 * -(-n // most))) * 32
         return [(j, min(step, n - j)) for j in range(0, n, step)]
 
-    def subtract(bank, fx, f0, x, x0, m):
-        mms([(T[bank][:, 0:m], T.ID[:], T[fx][:, f0:f0 + m], True, False, m)], [W("ID"), (fx, f0, f0 + m)], [W(bank)])
-        mms([(T[bank][:, 0:m], T.IDN[:], T[x][:, x0:x0 + m], False, True, m)], [W("IDN"), (x, x0, x0 + m)], [W(bank)])
+    def subtract(bank, fx, f0, x, x0, m, out=None):
+        out = T[bank][:, 0:m] if out is None else out
+        mms([(out, T.ID[:], T[fx][:, f0:f0 + m], True, False, m)], [W("ID"), (fx, f0, f0 + m)], [W(bank)])
+        mms([(out, T.IDN[:], T[x][:, x0:x0 + m], False, True, m)], [W("IDN"), (x, x0, x0 + m)], [W(bank)])
 
     cores = T.cores
     onchip = [r for r in range(NR) if r != rank and topo.chip(cores[r]) == topo.chip(core)][0]
@@ -350,7 +355,7 @@ def build(core, T, topo):
         ts(T.PF[:, c:c + 1], T[s][:, 0:1], d, A.add, 1, [W(s)], [("PF", c, c + 1)])
     for c, v in ((5, OFF // 32 + 16), (6, -0.5), (7, -OFF), (8, 16)):
         fill(T.PF[:, c:c + 1], float(v), 1, ("PF", c, c + 1))
-    SQB, HLF, MOFF, P16, P2 = ("PF", 5, 6), ("PF", 6, 7), ("PF", 7, 8), ("PF", 8, 9), ("PF", 9, 10)
+    SQB, HLF, MOFF, P16 = ("PF", 5, 6), ("PF", 6, 7), ("PF", 7, 8), ("PF", 8, 9)
 
     def eqc(name, n, col, val, src="RI"):
         ts(T[name][:, 0:n], T[src][:, 0:n], T.PF[:, col:col + 1], A.is_equal, n, [W(src), ("PF", col, col + 1)], [W(name)], val, A.mult)
@@ -362,27 +367,25 @@ def build(core, T, topo):
             act(out, T.MB[:], F.Copy, 160, rd, wr, scale=T.MK[:, y:y + 1], soft=[lastd["S"]])
         else:
             ts(out, T.MB[:], T.MK[:, y:y + 1], A.mult, 80, rd, wr)
-    for n, v in (("E1", 1.0), ("E05", 0.5), ("EX", 0.0625)):
+    for n, v in (("E1", 1.0), ("E05", 0.5)):
         eqc(n, 144, 4, v)
     for n, v in (("ID", 1.0), ("IDN", -1.0), ("IDK", 4096.0)):
         eqc(n, 128, 0, v)
-    for n, v in (("BMW", 1.0), ("BO", 2.0)):
-        eqc(n, 128, 2, v, "RG")
+    eqc("BMW", 128, 2, 1.0, "RG")
+    eqc("BMN", 128, 2, -1.0, "RG")
     ts(T.DUP[:], T.DUP[:], T.PF[:, 1:2], A.add, 16, [W("DUP"), ("PF", 1, 2)], [W("DUP")])
-    for y in range(16):
-        fill(T.THR[:, y:128:16], 2.0 ** (1 - y), 16, W("THR"))
-    tt(T.CW[:, 0:16], T.THR[:, 0:16], T.MK[:], A.mult, 32, [W("THR"), W("MK")], [W("CW")])
-    act(T.CW[:, 16:32], T.CW[:, 0:16], F.Copy, 16, [W("CW")], [W("CW"), P2], scale=0.5, accum=T.PF[:, 9:10])
-    ts(T.BD[:], T.BMW[:], T.PF[:, 9:10], A.mult, 64, [W("BMW"), P2], [W("BD")])
+    for x0, n in RUNS:
+        ts(T.EARLIER[:, x0:x0 + n], T.RI[:, 0:n], T.PF[:, 1:2], A.add, n, [W("RI"), ("PF", 1, 2)], [("EARLIER", x0, x0 + n)], 15.0, A.is_gt)
     ts(T.IDW[:], T.IDW[:], T.PF[:, 0:1], A.is_equal, 256, [W("IDW"), ("PF", 0, 1)], [W("IDW")])
     fill(T.DF[:], 0.0, 136, W("DF"))
-    ts(T.DF[:, :, 0:16], T.IDW[:, :, 8:24], -1.0, A.mult, 128, [W("IDW")], [W("DF")])
-    tt(T.DF[:, :, 1:17], T.DF[:, :, 1:17], T.IDW[:, :, 8:24], A.add, 256, [W("IDW"), W("DF")], [W("DF")])
+    tt(T.DF[:, :, 0:15], T.IDW[:, :, 8:23], T.IDW[:, :, 9:24], A.subtract, 240, [W("IDW")], [W("DF")])
+    cp(T.DF[:, :, 15], T.IDW[:, :, 23], 8, [W("IDW")], [W("DF")])
     for w in (0, 1):
         fill(T["RST%d" % w][:], 0.0, 136, W("RST%d" % w))
-        for c in (slice(0, 1), slice(16, 136, 17)):
-            fill(T["RST%d" % w][:, c], BIG if w else -BIG, 16, W("RST%d" % w))
-        fill(T.ENDS[:, 8 * w:8 * w + 8], BIG / 16 if w else -BIG / 16, 16, W("ENDS"))
+    fill(T.RST0[:, 16:136:17], -BIG, 8, W("RST0"))
+    fill(T.RST0[:, 0:1], -BIG, 8, W("RST0"))
+    fill(T.RST1[:, 0:136:17], BIG, 8, W("RST1"))
+    fill(T.ENDS[:], -BIG / 16, 8, W("ENDS"))
     for w in range(4):
         fill(T["GO%d" % w][:, 0:1], 0.0, 16, W("GO%d" % w))
         fill(T["WB%d" % w][:], 0.0, 64, W("WB%d" % w))
@@ -488,9 +491,11 @@ def build(core, T, topo):
                 send(src, h, onchip, es, 2)
     notes_sent = bulk[-1]
 
-    def shares(t):
+    def shares(t, kinds, soft=()):
         fx, xh, n = "FX%d" % t, "XH%d" % t, 1024 + 256 * t
         for h in range(2):
+            if SHARE[t][h] not in kinds:
+                continue
             for j, m in pieces(HALF, PIECE["share"]):
                 u = HALF * h + j
                 c = 256 * t + u // 16
@@ -498,14 +503,18 @@ def build(core, T, topo):
                 if SHARE[t][h] == "V":
                     tt(T[xh][:, u:u + m], src, T[fx][:, u:u + m], A.min, gcost(m), rd + [(fx, u, u + m)], [(xh, u, u + m)])
                 else:
-                    act(T["XG%d" % t][:, u:u + m], src, F.Copy, gcost(m), rd, [("XG%d" % t, u, u + m)])
+                    act(T["XG%d" % t][:, u:u + m], src, F.Copy, gcost(m), rd, [("XG%d" % t, u, u + m)], soft=soft)
+                if SHARE[t][h] == "S":
+                    ct = "CT%d" % nxt("h", 2)
+                    subtract(ct, fx, u, "XG%d" % t, u, m, T[ct][:])
+                    act(T[xh][:, u:u + m], T[ct][:], F.Relu, m, [W(ct)], [(xh, u, u + m)])
 
-    def folds_of(t):
+    def folds_of(t, kinds):
         for h in range(2):
-            if SHARE[t][h] == "F":
+            if SHARE[t][h] in kinds:
                 fold(t, h)
 
-    folds = []
+    folds, signs = [], []
 
     def fold(t, h):
         fx, xh, xg, u = "FX%d" % t, "XH%d" % t, "XG%d" % t, slice(HALF * h, HALF * h + HALF)
@@ -523,13 +532,11 @@ def build(core, T, topo):
     def share_keys(t):
         xh = "XH%d" % t
         for h in range(2):
+            sg = "BMN" if SHARE[t][h] == "S" else "BMW"
             for k0 in (0, 8):
-                mms([(T["KEY%d" % h][:, k:136:17], T[xh][:, HALF * h + k:HALF * h + HALF:16], T.BMW[:, 0:128:16], k == 0, False, 64)
-                     for k in range(k0, k0 + 8)], [(xh, HALF * h, HALF * h + HALF), W("BMW")], [W("KEY%d" % h)])
-            ends(0, h, False)
-
-    def ends(w, h, alone):
-        mms([(T["KEY%d" % h][:, 16:136:17], T.ID[:], T.ENDS[:, 8 * w:8 * w + 8], alone, alone, 8)], [W("ID"), W("ENDS")], [("KEY%d" % h, 0, 136)])
+                mms([(T["KEY%d" % h][:, k:136:17], T[xh][:, HALF * h + k:HALF * h + HALF:16], T[sg][:, 0:128:16], k == 0, False, 64)
+                     for k in range(k0, k0 + 8)], [(xh, HALF * h, HALF * h + HALF), W(sg)], [W("KEY%d" % h)])
+            mms([(T["KEY%d" % h][:, 16:136:17], T.ID[:], T.ENDS[:], False, False, 8)], [W("ID"), W("ENDS")], [W("KEY%d" % h)])
 
     def gather_headings(t):
         n = 1024 + 256 * t
@@ -557,11 +564,11 @@ def build(core, T, topo):
         fx = "FX%d" % t
         for a in range(NR):
             nb, cl, cln = "NB%d" % a, "CL%d" % (a % 2), "CL%d" % (1 - a % 2)
-            if a > 0 and t > 0:
-                apply_update(t - 1, a)
+            if a == 1 and t > 0:
+                apply_updates(t - 1)
             for h in (1, 0):
                 x, s, bank, m0, w = "X%d" % h, "SS%d" % h, "B%d" % h, 128 * h, 128
-                v = SPLIT[t][h]
+                v = SPLIT[t > 0][a][h]
                 for eng, o, n in (("V", 0, v), ("S", v, 128 - v)):
                     for j, m in pieces(16 * n, PIECE[eng]) if n else []:
                         c, u = m0 + o + j // 16, 16 * o + j
@@ -573,7 +580,7 @@ def build(core, T, topo):
                             db = "B%d" % (3 + nxt("u", 2))
                             act(T[x][:, u:u + m], src, F.Copy, gcost(m), rd, [(x, u, u + m)])
                             subtract(db, fx, f0, x, u, m)
-                            act(T[s][:, u:u + m], T[db][:, 0:m], F.Sign, m, [W(db), HLF], [(s, u, u + m)], bias=T.PF[:, 6:7])
+                            signs.append(act(T[s][:, u:u + m], T[db][:, 0:m], F.Sign, m, [W(db), HLF], [(s, u, u + m)], bias=T.PF[:, 6:7]))
                     if n:
                         extract(bank, o, "E1" if eng == "V" else "E05", x if eng == "V" else s, n, o, eng == "S")
                 sl = slice(m0, m0 + w)
@@ -611,21 +618,19 @@ def build(core, T, topo):
 
     def pick(w, h):
         key, (run, go, pk, wb) = "KEY%d" % h, (n + str(2 * w + h) for n in ("RUN", "GO", "PICK", "WB"))
-        if w:
-            ends(1, h, True)
         scan(T[run][:], T["RST%d" % w][:], T[key][:, 0:136], A.add, A.min if w else A.max, 136, [W("RST%d" % w), (key, 0, 136)], [W(run)])
         tt(T[go][:, 1:136], T[key][:, 1:136], T[run][:, 0:135], A.is_ge if w else A.is_le, 136, [(key, 0, 136), W(run)], [W(go)])
-        scan(T[pk][:], T[key][:, 136:272], T[go][:], A.add, A.mult, 136, [(key, 136, 272), W(go)], [W(pk)])
-        hilo(W(wb), T[wb][:, 0:128:16], T[wb][:, 1:128:16], T[pk][:, 16:136:17], 8, [W(pk)])
+        scan(T[pk][:], T[go][:], T[key][:, 136:272], A.mult, A.add, 136, [(key, 136, 272), W(go)], [W(pk)])
+        hilo(W(wb), T[wb][:, 0:128:16], T[wb][:, 1:128:16], T[pk][:, 15:136:17], 8, [W(pk)])
 
-    def row(w, h, c0):
-        key, wb = "KEY%d" % h, "WB%d" % (2 * w + h)
-        mms([(T[key][:, c0:c0 + 128], T[wb][:], T.ID[:], True, True, 128)], [W(wb), W("ID")], [(key, c0, c0 + 128)])
+    def row(w, h, out, reg):
+        wb = "WB%d" % (2 * w + h)
+        mms([(out, T[wb][:], T.ID[:], True, True, 128)], [W(wb), W("ID")], [reg])
 
     def headings_out(t, h):
-        key, c = "KEY%d" % h, 1024 + 256 * t + 128 * h
-        row(0, h, 272)
-        act(T.HT[:, c:c + 128], T[key][:, 272:400], F.Copy, 128, [(key, 272, 400)], [("HT", c, c + 128), ("KS1", h, h + 1)],
+        bank, c = "B%d" % h, 1024 + 256 * t + 128 * h
+        row(0, h, T[bank][:, 0:128], (bank, 0, 128))
+        act(T.HT[:, c:c + 128], T[bank][:, 0:128], F.Copy, 128, [(bank, 0, 128)], [("HT", c, c + 128), ("KS1", h, h + 1)],
             accum=T.KS1[:, h:h + 1])
 
     def finish(t, h):
@@ -642,33 +647,29 @@ def build(core, T, topo):
         dma("Y", T.yh[:, 256 * t:256 * t + 256], T.YH8[:, 256 * t:256 * t + 256], 2.5, [y], [])
 
     def notes(t, h):
-        key, c, ov, ol = "KEY%d" % h, 1024 + 256 * t + 128 * h, VW * t + 128 * h, 16 * t + 8 * h
-        K = T[key]
+        c, ov, ol = 1024 + 256 * t + 128 * h, VW * t + 128 * h, 16 * t + 8 * h
         lr, lb, lf, lu, old, dc, fl, of, eqt = (n + str(h) for n in ("LR", "LB", "LF", "LU", "OLD", "DC", "FL", "OF", "EQT"))
-        r0, r1, r2, r3 = (key, 0, 128), (key, 128, 256), (key, 256, 272), (key, 272, 400)
-        row(1, h, 0)
-        act(T[lr][:], K[:, 0:128], F.Copy, 128, [r0], [W(lr)])
-        mms([(K[:, 128:256], T.BMW[:], T[lr][:], True, True, 128)], [W("BMW"), W(lr)], [r1])
-        extract(key, 256, "E1", lr, 8)
-        cp(T[lb][:], K[:, 128:256], 128, [r1], [W(lb)])
+        ct = "CT%d" % h
+        (q0, Q0), (q1, Q1), (q3, Q3) = (((ct, 32 * j, 32 * j + 128), T[ct][:, j:j + 4, :]) for j in (0, 4, 12))
+        q2, Q2 = (ct, 256, 264), T[ct][:, 8, 0:8]
+        row(1, h, Q0, q0)
+        act(T[lr][:], Q0, F.Copy, 128, [q0], [W(lr)])
+        mms([(Q1, T.BMW[:], T[lr][:, ::-1], True, True, 128)], [W("BMW"), W(lr)], [q1])
+        extract(ct, 256, "E1", lr, 8, out=Q2)
+        cp(T[lb][:], Q1, 128, [q1], [W(lb)])
         for n in (lf, lu):
-            cp(T[n][:], K[:, 256:264], 8, [r2], [W(n)])
-        for mb in range(8):
-            n = 128 - 16 * mb
-            ts(T[eqt][:, mb, 0:n], T[lb][:, 16 * mb:128], T[lf][:, mb:mb + 1], A.is_equal, n * 0.5, [W(lb), W(lf)], [(eqt, mb, mb + 1)])
+            cp(T[n][:], Q2, 8, [q2], [W(n)])
+        for mb, (x0, n) in enumerate(RUNS):
+            ts(T[eqt][:, x0:x0 + n], T[lb][:, 128 - n:128], T[lf][:, mb:mb + 1], A.is_equal, 64, [W(lb), W(lf)], [(eqt, mb, mb + 1)])
+        scan(T[fl][:], T[eqt][:], T.EARLIER[:], A.max, A.mult, 288, [W(eqt), W("EARLIER")], [W(fl)])
+        tt(T[of][:, 0:4], T[fl][:, 15:576:160], T.DUP[:, 0:4], A.mult, 8, [W(fl), W("DUP")], [(of, 0, 4)])
+        tt(T[of][:, 7:3:-1], T[fl][:, 143:576:144], T.DUP[:, 4:8], A.mult, 8, [W(fl), W("DUP")], [(of, 4, 8)])
         act(T[old][:], T.NB0[:, 0:H].indirect(T[lu][:]), F.Copy, gcost(128), [("NB0", 0, H), W(lu)], [W(old)])
-        mms([(K[:, 272:400], T.ID[:], T.FE[:, c:c + 128], True, False, 128), (K[:, 272:400], T.IDN[:], T[old][:], False, True, 128)],
-            [W("ID"), W("IDN"), ("FE", c, c + 128), W(old)], [r3])
-        mms([(K[:, 16 * mb + 16:128], T.BO[:], T[eqt][:, mb, 16:128 - 16 * mb], mb == 0, False, 112 - 16 * mb) for mb in range(7)]
-            + [(K[:, 0:16], T.BD[:], T[eqt][:, 0, 0:16], False, False, 16), (K[:, 16:128], T.BD[:], T[eqt][:, 1:8, 0:16], False, True, 112)],
-            [W("BO"), W("BD"), W(eqt)], [r0])
-        tt(T[fl][:], K[:, 0:128], T.THR[:], A.is_ge, 128, [r0, W("THR")], [W(fl)])
-        ts(T[dc][:], K[:, 272:400], 32.0, A.min, 128, [r3], [W(dc)], -32.0, A.max)
-        mms([(K[:, 128:256], T.ID[:], T[old][:], True, False, 128), (K[:, 128:256], T.ID[:], T[dc][:], False, True, 128)],
-            [W("ID"), W(old), W(dc)], [r1])
-        extract(key, 256, "EX", fl, 8)
-        tt(T[of][:], K[:, 256:264], T.DUP[:], A.mult, 8, [r2, W("DUP")], [W(of)])
-        act(T.NV0[:, ov:ov + 128], K[:, 128:256], F.Copy, 128, [r1], [("NV0", ov, ov + 128)])
+        mms([(Q3, T.ID[:], T.FE[:, c:c + 128], True, False, 128), (Q3, T.IDN[:], T[old][:], False, True, 128)],
+            [W("ID"), W("IDN"), ("FE", c, c + 128), W(old)], [q3])
+        ts(T[dc][:], Q3, 32.0, A.min, 128, [q3], [W(dc)], -32.0, A.max)
+        mms([(Q0, T.ID[:], T[old][:], True, False, 128), (Q0, T.ID[:], T[dc][:], False, True, 128)], [W("ID"), W(old), W(dc)], [q0])
+        act(T.NV0[:, ov:ov + 128], Q0, F.Copy, 128, [q0], [("NV0", ov, ov + 128)])
         tt(T[of][:], T[of][:], T[lf][:], A.max, 16, [W(of), W(lf)], [W(of)])
         cp(T.NL0[:, ol:ol + 8], T[of][:], 8, [W(of)], [("NL0", ol, ol + 8)])
         if t + 1 < RT:
@@ -688,35 +689,40 @@ def build(core, T, topo):
 
     def kappa(t):
         k = VW * t + 256
-        mms([(T.CT1[:, 0, 0:1], T.ONES[:], T.KS1[:, h:h + 1], h == 0, h == 1, 256) for h in range(2)], [W("ONES"), W("KS1")], [W("CT1")])
-        cp(T.KI[:, 0:1], T.CT1[:, 0, 0:1], 1, [W("CT1")], [W("KI")])
+        mms([(T.B3[:, 0:1], T.ONES[:], T.KS1[:, h:h + 1], h == 0, h == 1, 256) for h in range(2)], [W("ONES"), W("KS1")], [W("B3")])
+        cp(T.KI[:, 0:1], T.B3[:, 0:1], 1, [W("B3")], [W("KI")])
         ts(T.KJ[:, 0:1], T.KI[:, 0:1], 255 * 32, A.bitwise_and, 1, [W("KI")], [W("KJ")])
         cp(T.NV0[:, k:k + 1], T.KJ[:, 0:1], 1, [W("KJ")], [("NV0", k, k + 1)])
         bias(t, 0)
 
     sent = {}
 
-    def lanes(other):
-        return cross
-
     def send_update(t):
         c = slice(VW * t, VW * t + VW)
         for a in range(1, NR):
             dst = (rank - a) % NR
-            (rid, pid), es = addr(dst), lanes(dst)
+            (rid, pid), es = addr(dst), cross
             num["lsend"] += len(es)
             bulk.append(add(gr, "G", lambda q, a=a, rid=rid, pid=pid, es=es: q.remote_dma(
                 T["NV%d" % a][:, c], T.NV0[:, c], T.sem["iv%d_%d" % (a, t)], T.sem.lsend, pid, rid, emask(es)),
                 GCALL, [("NV0", c.start, c.stop)], [], "s", "lsend", num["lsend"], soft=bulk[-1:]))
             sent[t, a] = bulk[-1]
 
-    def apply_update(t, a):
-        nv, nl, c = "NV%d" % a, "NL%d" % a, VW * t
-        add(gr, "R", None, 0.0, [], [(nv, c, c + VW)], "r", "iv%d_%d" % (a, t), len(lanes((rank + a) % NR)), ARRIVE[5], soft=[sent[t, a]])
-        bias(t, a)
-        tt(T.PL[:], T[nv][:, c + 264:c + 280], T[nv][:, c + 280:c + 296], A.add, 32, [(nv, c + 264, c + 296)], [W("PL")])
-        cp(T[nl][:, 16 * t:16 * t + 16], T.PL[:], 16, [W("PL")], [(nl, 16 * t, 16 * t + 16)])
-        scatter(t, a)
+    def apply_updates(t):
+        for a in range(1, NR):
+            nv, nl, c = "NV%d" % a, "NL%d" % a, VW * t
+            add(gr, "R", None, 0.0, [], [(nv, c, c + VW)], "r", "iv%d_%d" % (a, t), len(cross), ARRIVE[5], soft=[sent[t, a]])
+            bias(t, a)
+            if a < NR - 1 or not WHOLE:
+                tt(T.PL[:], T[nv][:, c + 264:c + 280], T[nv][:, c + 280:c + 296], A.add, 32, [(nv, c + 264, c + 296)], [W("PL")])
+                cp(T[nl][:, 16 * t:16 * t + 16], T.PL[:], 16, [W("PL")], [(nl, 16 * t, 16 * t + 16)])
+                scatter(t, a)
+        if WHOLE:
+            nb, nv, s = "NB%d" % rel(onchip - 1, rank), "NV%d" % rel(onchip, rank), "ls%d" % nxt("ls", 99)
+            rid, pid = addr(onchip)
+            bulk.append(add(gr, "G", lambda q: q.remote_dma(T.NB3[:, 0:H], T[nb][:, 0:H], T.sem["wh%d" % t], T.sem[s], pid, rid, emask(wide)),
+                            GCALL, [(nb, 0, H), (nv, VW * t, VW * t + VW)], [], "s", s, len(wide), ARRIVE[7], soft=bulk[-1:]))
+            add(gr, "R", None, 0.0, [], [("NB3", 0, H)], "r", "wh%d" % t, len(wide), ARRIVE[7] + (2.0 if rank == first else 0.0), soft=bulk[-1:])
 
     for t in range(RT):
         lists(t)
@@ -724,20 +730,21 @@ def build(core, T, topo):
         expand(t)
     gather_headings(0)
     for t in range(RT):
-        shares(t)
-    for t in range(EARLY):
-        folds_of(t)
+        shares(t, "VSF")
+    folds_of(1, "F")
     for t in range(RT):
         share_keys(t)
         visits(t)
         scatter(t, 0)
         if t + 1 < RT:
+            shares(t + 1, "L", signs[-1:])
             gather_headings(t + 1)
             kappa(t)
             send_update(t)
+            folds_of(t + 1, "L")
         if t + EARLY < RT:
             expand(t + EARLY, bulk[-1:])
-            folds_of(t + EARLY)
+            folds_of(t + EARLY, "F")
         write_yh(t)
     for j, e in ((0, "S"), (1, "Y")):
         dma(e, T.yl[:, HALF * j:HALF * j + HALF], T.NB0[:, HALF * j:HALF * j + HALF], 5.0, [("NB0", HALF * j, HALF * j + HALF)], [])
@@ -756,7 +763,7 @@ def hand_back(core, home, T, topo):
     last = []
     for t in range(RT):
         for h in range(2):
-            if SHARE[t][h] == "F":
+            if SHARE[t][h] in "FL":
                 xh, reg = T["XH%d" % t][:, HALF * h:HALF * h + HALF], [("XH%d" % t, h, h + 1)]
                 add(gr, "R", None, 0.0, [], reg, "r", "fo%d_%d" % (t, h), len(half), soft=last[-1:])
                 last.append(add(gr, "G", lambda q, xh=xh, t=t, h=h: q.remote_dma(xh, xh, T.sem["fb%d_%d" % (t, h)], T.sem.lsend, pid, rid,

from concourse.bass import DstId, RemoteDMATransfer
from concourse.mybir import AluOpType as A, ActivationFunctionType as F

NR, RT, H, DUMMY, HALF = 4, 4, 4096, 256, 2048
MOD = 131072
KS = 130
SLOPE = 613 * 32 + MOD * KS
OFF = MOD * 512
BV = -256 - MOD * (9 * KS + 1) - OFF
SPLIT = (((72, 72),) * 4, ((72, 68),) * 4)
HEADS = (((("V", 64), ("S", 64)), (("V", 64), ("S", 64))),) + (((("V", 64), ("S", 64)), (("S", 64), ("S", 64))),) * 3
SCALE = "SSSS"
SHARE = ("VS", "LL", "LL", "LL")
EXPAND = "VVVVVVVVVVSSSSSS"
PIECE = {"V": 640, "S": 512, "head": 320, "share": 512}
PASSES = ((0.0, "fffflll"), (0.12, "fffflll"), (0.25, "fffflll"), (0.4, "fffflll"), (0.2, "flflfl"))
CASES = ((1.0, 1.0, 1.0), (1.25, 0.7, 0.85), (0.75, 1.6, 1.0), (1.0, 1.0, 1.3))
SHORT = (0.0,)
WAKE, SELF = 0.1, 0.1
OV, OS = 0.005, 0.005
QUART, NEAR = 1024, (2, 3, 0, 1)
ARRIVE = (9.0, 14.0, 4.0, 5.0, 12.0, 4.0, 22.0, 7.0)
WHOLE = 0
EARLY = 2
BIG = float(1 << 24)
CYC, PEC = 0.83e-3 * 1.25, 0.52e-3


GC, SC, GCALL = 1.56, 3.8, 0.8


def gcost(n, scatter=False):
    return 55.5 + int((SC if scatter else GC) * n)


SCRATCH = {}
SEMAPHORES = ["cv", "cs", "cp", "cg", "lsend"] + ["d%d" % j for j in range(30)] + ["ls%d" % j for j in range(26)]
SEMAPHORES += [s + "%d_%d" % (t, h) for s in ("fo", "fb") for t in range(RT) for h in range(2)]


def _buf(names, cols, dtype, where="sbuf", rows=128):
    for n in names.split():
        SCRATCH[n] = (where, [rows] + (cols if isinstance(cols, list) else [cols]), dtype)


B16, F32, I32, U16 = "bfloat16", "float32", "int32", "uint16"
_buf("NB0 NB1 NB2 NB3", H + DUMMY, B16)
_buf("FE HT", 2048, B16)
_buf("XG0 XG1 XG2 XG3", 4096, B16)
_buf("FX0 FX1 FX2 FX3 XH0 XH1 XH2 XH3", 4096, B16)
_buf("X0 X1 SS0 SS1", 2048, B16)
VW = 296
_buf("NV0 NV1 NV2 NV3", RT * VW, B16)
_buf("NL0 NL1 NL2 NL3", RT * 16, U16)
for _t in range(RT - 1):
    for _a in range(NR):
        SEMAPHORES += ["iv%d_%d" % (_a, _t) if _a else "wh%d" % _t]
for _a in range(1, NR):
    SEMAPHORES += ["n%d_%d" % (_a, _h) for _h in range(4)]
_buf("CMP", 1024, I32)
_buf("LT", 1024, U16)
_buf("HD", 64, I32)
_buf("HDB BMW BMN ID IDN IDK", 128, B16)
_buf("RI", 160, F32)
_buf("RG ONES", 128, F32)
_buf("PI PM PG KI KJ", 2, I32)
_buf("PF", 16, F32)
_buf("MK PL", 16, F32)
_buf("DUP LF0 LF1 OF0 OF1", 8, F32)
_buf("LU0 LU1", 8, U16)
_buf("KV", 16, F32)
_buf("HALVES", 128, B16)
_buf("MB", 160, B16)
_buf("MIP", 16 * 160, B16)
_buf("E1 E05", 144, B16)
_buf("OLD0 OLD1 DC0 DC1 LR0 LR1 WB0 WB1 WB2 WB3", 128, B16)
_buf("C32 SQ CW", 256, F32)
_buf("CL0 CL1", 256, U16)
_buf("LB0 LB1", 128, U16)
_buf("TI CI", 256, I32)
_buf("IDW", [8, 32], F32)
_buf("DF", [8, 17], F32)
_buf("CD", [16, 24], F32)
_buf("RST0 RST1 RUN0 RUN1 RUN2 RUN3 GO0 GO1 GO2 GO3 PICK0 PICK1 PICK2 PICK3", 136, F32)
_buf("EQ", [6, 8, 32], B16)
_buf("ENDS", 8, B16)
_buf("EQT0 EQT1 FL0 FL1 EARLIER", 576, B16)
RUNS = [(144 * b, 16 * b + 16) if b < 4 else (144 * (8 - b) - 16 * b - 16, 16 * b + 16) for b in range(8)]
_buf("KS1", 2, F32)
_buf("YH8", 1024, F32, rows=8)
_buf("B0 B1 B3 B4 KEY0 KEY1", 512, F32, "psum")
_buf("CT0 CT1", [16, 32], F32, "psum")
PSUM = set(n for n in SCRATCH if SCRATCH[n][0] == "psum")
CSEM = {"V": "cv", "S": "cs", "P": "cp", "G": "cg"}


def add(gr, eng, emit, cost, reads=(), writes=(), kind="c", sem=None, val=0, lat=0.0, est=0.0, soft=()):
    nodes = gr["nodes"]
    i = len(nodes)
    deps = set()
    for w, regs in ((0, reads), (1, writes)):
        for (b, c0, c1) in regs:
            if b in PSUM:
                st = gr["bank"].setdefault(b, [[], [], None])
                if st[2] != eng:
                    st[0], st[1], st[2] = st[1], [], eng
                deps.update(e[0] for e in st[0])
                deps.update(j for (j, d0, d1, dw) in st[1] if d0 < c1 and c0 < d1 and (w or dw))
                st[1].append((i, c0, c1, w))
            else:
                keep = []
                for e in gr["acc"].get(b, []):
                    j, d0, d1, dw = e
                    if d0 < c1 and c0 < d1 and (w or dw):
                        deps.add(j)
                    if not (w and j != i and c0 <= d0 and d1 <= c1):
                        keep.append(e)
                gr["acc"][b] = keep + [(i, c0, c1, w)]
    deps.discard(i)
    nodes.append({"id": i, "eng": eng, "emit": emit, "cost": cost, "kind": kind, "sem": sem, "val": val, "deps": deps,
                  "soft": set(soft) - deps, "lat": lat, "est": est, "done": (sem, val)})
    return i


def schedule(gr):
    nodes = gr["nodes"]
    succ, pred = [[] for _ in nodes], [[] for _ in nodes]
    for n in nodes:
        for j in n["deps"] | n["soft"]:
            gap = nodes[j]["lat"] + (WAKE if nodes[j]["eng"] != n["eng"] else SELF * (n["eng"] != "P")) if j in n["deps"] else 0.0
            succ[j].append((n["id"], gap))
            pred[n["id"]].append((j, gap))

    def flow(rank, after, before, at, ahead):
        left = [len(b) for b in before]
        free, ready, end, order = {}, {}, [0.0] * len(nodes), []
        for n in nodes:
            free[n["eng"]] = 0.0
            ready.setdefault(n["eng"], set())
            if left[n["id"]] == 0:
                ready[n["eng"]].add(n["id"])
        while len(order) < len(nodes):
            s, e = min((max(free[e], min(at[i] for i in ready[e])), e) for e in ready if ready[e])
            i = max((k for k in ready[e] if at[k] <= s + ahead), key=lambda k: (rank[k] - 4 * max(0.0, at[k] - s), -k))
            s = max(s, at[i])
            ready[e].discard(i)
            end[i] = s + nodes[i]["cost"]
            if e != "R":
                free[e] = end[i]
            order.append(i)
            for k, gap in after[i]:
                left[k] -= 1
                at[k] = max(at[k], end[i] + gap)
                if left[k] == 0:
                    ready[nodes[k]["eng"]].add(k)
        return order, end

    def lay(rank, after, before, at, ahead):
        left = [len(b) for b in before]
        busy, end, placed = dict((n["eng"], []) for n in nodes), [0.0] * len(nodes), []
        ready = set(n["id"] for n in nodes if left[n["id"]] == 0)
        while ready:
            i = max(ready, key=lambda k: (rank[k], -k))
            ready.discard(i)
            s, cost, line = at[i], nodes[i]["cost"], busy[nodes[i]["eng"]]
            if nodes[i]["eng"] != "R":
                lo, hi = 0, len(line)
                while lo < hi:
                    mid = (lo + hi) // 2
                    lo, hi = (mid + 1, hi) if line[mid][1] <= s else (lo, mid)
                while lo < len(line) and line[lo][0] < s + cost:
                    s = max(s, line[lo][1])
                    lo += 1
                line.insert(lo, (s, s + cost))
            end[i] = s + cost
            placed.append((s, len(placed), i))
            for k, gap in after[i]:
                left[k] -= 1
                at[k] = max(at[k], end[i] + gap)
                if left[k] == 0:
                    ready.add(k)
        return [x[2] for x in sorted(placed)], end

    rank = [0.0] * len(nodes)
    for n in reversed(nodes):
        rank[n["id"]] = max([n["lat"]] + [rank[s] + gap for s, gap in succ[n["id"]]]) + n["cost"] + 0.05

    def span(order, gather, wake, remote):
        free, end = {}, [0.0] * len(nodes)
        for i in order:
            n = nodes[i]
            s = max([n["est"] * remote, free.get(n["eng"], 0.0)]
                    + [end[j] + gap * (remote if nodes[j]["eng"] == "R" else wake if nodes[j]["kind"] == "c" else 1.0) for j, gap in pred[i]])
            end[i] = s + n["cost"] * (gather if n.get("gather") else 1.0)
            if n["eng"] != "R":
                free[n["eng"]] = end[i]
        return max(end[n["id"]] + n["lat"] for n in nodes)

    best, first = None, rank
    for ahead, passes, short in [p + (s,) for p in PASSES for s in SHORT]:
        rank = first
        for rule in passes:
            rule = flow if rule == "f" else lay
            rank = [r + (0.0 if n.get("gather") else short) for r, n in zip(rank, nodes)]
            order, end = rule(rank, succ, pred, [n["est"] for n in nodes], ahead)
            total = sum(span(order, *case) for case in CASES)
            if best is None or total < best[0]:
                best = (total, order)
            rank = rule(end, pred, succ, [n["lat"] for n in nodes], ahead)[1]
    return best[1]


def emit_all(gr, order, g, T):
    q = {"V": g.vector, "S": g.scalar, "P": g.tensor, "G": g, "Y": g.sync}
    nodes, clk = gr["nodes"], {}
    known = dict((e, {}) for e in q)
    final = {}
    for i in order:
        n = nodes[i]
        if n["kind"] == "r":
            final[n["sem"]] = n["val"]
            continue
        e = n["eng"]
        cl = dict(known[e])
        need = {}
        for j in n["deps"]:
            d = nodes[j]
            if not (e == "P" and d["eng"] == "P"):
                s, v = d["done"]
                need[s] = max(need.get(s, 0), v)
        items = sorted(need.items(), key=lambda x: (-x[1], x[0]))
        for s, v in items:
            if cl.get(s, 0) >= v or any(s2 != s and clk.get((s2, v2), {}).get(s, 0) >= v and known[e].get(s2, 0) < v2
                                        for s2, v2 in items):
                continue
            q[e].wait_ge(T.sem[s], int(v))
            cl[s] = v
            for s3, v3 in clk.get((s, v), {}).items():
                cl[s3] = max(cl.get(s3, 0), v3)
        known[e] = cl
        ins = n["emit"](q[e])
        if n["kind"] == "c":
            s = CSEM[e]
            n["done"] = (s, final.get(s, 0) + 1)
            ins.then_inc(T.sem[s], 1)
        elif n["kind"] == "d":
            ins.then_inc(T.sem[n["sem"]], 16)
        final[n["done"][0]] = max(final.get(n["done"][0], 0), n["done"][1])
        clk[n["done"]] = cl
    for s in sorted(final):
        if known["G"].get(s, 0) < final[s]:
            g.wait_ge(T.sem[s], int(final[s]))


def build(core, T, topo):
    rank = T.rank_of(core)
    gr = {"nodes": [], "acc": {}, "bank": {}}
    num = {"d": 0, "ls": 0, "x": 0, "s": 0, "b": 0, "h": 0, "u": 0, "e": 0, "lsend": 0}
    lastd = {}

    def nxt(k, n):
        num[k] += 1
        return (num[k] - 1) % n

    def W(n):
        return (n, 0, 1 << 20)

    def timed(eng, fn, cyc, reads, writes, soft=()):
        i = add(gr, eng, fn, max(64, cyc) * CYC + OV, reads, writes, soft=soft)
        gr["nodes"][i]["gather"] = cyc % 1 == 0.5
        return i

    def vec(fn, cyc, reads, writes):
        return timed("V", fn, cyc, reads, writes)

    def gps(fn, cyc, writes, reads=(), soft=()):
        return add(gr, "G", fn, cyc * CYC + 0.17, reads, writes, soft=soft)

    def dma(eng, out, in_, lat, reads, writes, soft=()):
        s = "d%d" % nxt("d", 99)
        lastd[eng] = add(gr, eng, lambda q: q.dma_start(out, in_), 0.06, reads, writes, "d", s, 16, lat,
                         soft=list(soft) + ([lastd[eng]] if eng in lastd else []))

    def tt(out, in0, in1, op, cyc, reads, writes):
        return vec(lambda q: q.tensor_tensor(out=out, in0=in0, in1=in1, op=op), cyc, reads, writes)

    def ts(out, in0, s1, op0, cyc, reads, writes, s2=None, op1=None):
        if op1 is None:
            return vec(lambda q: q.tensor_scalar(out=out, in0=in0, scalar1=s1, scalar2=None, op0=op0), cyc, reads, writes)
        return vec(lambda q: q.tensor_scalar(out=out, in0=in0, scalar1=s1, scalar2=s2, op0=op0, op1=op1), cyc, reads, writes)

    def cp(out, in_, cyc, reads, writes):
        return vec(lambda q: q.tensor_copy(out=out, in_=in_), cyc, reads, writes)

    def scan(out, d0, d1, op0, op1, cyc, reads, writes):
        return vec(lambda q: q.tensor_tensor_scan(out, d0, d1, 0.0, op0, op1), cyc, reads, writes)

    def fill(ap, val, n, reg):
        vec(lambda q: q.memset(ap, val), n, [], [reg])

    def act(out, in_, func, cyc, reads, writes, bias=0.0, scale=1.0, accum=None, soft=()):
        def f(q):
            if accum is not None:
                return q.activation(out=out, in_=in_, func=func, bias=bias, scale=scale, accum_out=accum)
            return q.activation(out=out, in_=in_, func=func, bias=bias, scale=scale)
        return timed("S", f, cyc, reads, writes, soft)

    def mms(lst, reads, writes, soft=()):
        def f(q):
            for (o, l, r, st, sp, _) in lst:
                ins = q.matmul(o, l, r, st, sp)
            return ins
        return add(gr, "P", f, sum(max(64, x[5]) for x in lst) * PEC + 0.03, reads, writes, soft=soft)

    def extract(bank, c0, en, x, n, q0=0, signs=False, out=None):
        out = T[bank][:, c0:c0 + n] if out is None else out
        lst = [(out, T.BMW[:], T.HALVES[:, 0:n], True, False, n)] if signs else []
        u = 16 * q0
        return mms(lst + [(out, T[en][:, 15 - i:143 - i], T[x][:, u + i:u + 16 * n:16], i == 0 and not signs, i == 15, n)
                          for i in range(16)], [(x, u, u + 16 * n), W(en), W("BMW"), W("HALVES")], [(bank, c0, c0 + n)])

    def pieces(n, most=512):
        step = -(-n // (32 * -(-n // most))) * 32
        return [(j, min(step, n - j)) for j in range(0, n, step)]

    def subtract(bank, fx, f0, x, x0, m, out=None):
        out = T[bank][:, 0:m] if out is None else out
        mms([(out, T.ID[:], T[fx][:, f0:f0 + m], True, False, m)], [W("ID"), (fx, f0, f0 + m)], [W(bank)])
        mms([(out, T.IDN[:], T[x][:, x0:x0 + m], False, True, m)], [W("IDN"), (x, x0, x0 + m)], [W(bank)])

    cores = T.cores
    onchip = [r for r in range(NR) if r != rank and topo.chip(cores[r]) == topo.chip(core)][0]
    far = [r for r in range(NR) if topo.chip(cores[r]) != topo.chip(core)]
    first = rank if (rank - 1) % NR in far else onchip

    def load(e, n, src, c0, c1, lat):
        dma(e, T[n][:, c0:c1], T[src][:, c0:c1], lat, [], [(n, c0, c1)])
    dma("Y", T.HD[:], T.hd[:], 2.2, [], [W("HD")])
    load("S", "FE", "feat", 1024, 1280, 2.6)
    load("S", "CMP", "comp", 0, 256, 3.2)
    for j, h in enumerate((0, 2, 1, 3) if rank == first else (0, 2, 3, 1)):
        load("Y", "NB0", "lim", QUART * h, QUART * h + QUART, 4.2 + 1.2 * j)
    load("S", "FE", "feat", 0, 1024, 10.0)
    load("S", "FE", "feat", 1280, 2048, 11.0)
    load("Y", "CMP", "comp", 256, 1024, 13.0)

    gps(lambda q: q.iota(T.PI[:, 0:1], [[1, 1]], 0, 1), 2, [W("PI")])
    for ap, n, pat, base, c in ((T.RI[:], "RI", [[1, 160]], 0, 320), (T.RG[:], "RG", [[16, 8], [0, 16]], 0, 256),
                                (T.IDW[:, :, 0:8], "IDW", [[16, 8], [1, 8]], 8, 128), (T.IDW[:, :, 8:24], "IDW", [[16, 8], [1, 16]], 0, 256),
                                (T.IDW[:, :, 24:32], "IDW", [[16, 8], [1, 8]], 0, 128), (T.DUP[:], "DUP", [[16, 8]], H, 32)):
        gps(lambda q, ap=ap, pat=pat, base=base: q.iota(ap, pat, base, 0, allow_small_or_imprecise_dtypes=True), c, [W(n)])
    ts(T.PM[:, 0:1], T.PI[:, 0:1], 15, A.bitwise_and, 1, [W("PI")], [W("PM")])
    ts(T.PG[:, 0:1], T.PI[:, 0:1], 112, A.bitwise_and, 1, [W("PI")], [W("PG")])
    for c, s, d in ((0, "PI", 0), (1, "PM", 0), (2, "PG", 0), (3, "PI", 16), (4, "PG", 15)):
        ts(T.PF[:, c:c + 1], T[s][:, 0:1], d, A.add, 1, [W(s)], [("PF", c, c + 1)])
    for c, v in ((5, OFF // 32 + 16), (6, -0.5), (7, -OFF), (8, 16)):
        fill(T.PF[:, c:c + 1], float(v), 1, ("PF", c, c + 1))
    SQB, HLF, MOFF, P16 = ("PF", 5, 6), ("PF", 6, 7), ("PF", 7, 8), ("PF", 8, 9)

    def eqc(name, n, col, val, src="RI"):
        ts(T[name][:, 0:n], T[src][:, 0:n], T.PF[:, col:col + 1], A.is_equal, n, [W(src), ("PF", col, col + 1)], [W(name)], val, A.mult)
    eqc("MB", 160, 3, 1.0)
    eqc("MK", 16, 1, 1.0)
    for y in range(16):
        out, rd, wr = T.MIP[:, 160 * y:160 * y + 160], [W("MB"), W("MK")], [("MIP", 160 * y, 160 * y + 160)]
        if y % 3 == 0:
            act(out, T.MB[:], F.Copy, 160, rd, wr, scale=T.MK[:, y:y + 1], soft=[lastd["S"]])
        else:
            ts(out, T.MB[:], T.MK[:, y:y + 1], A.mult, 80, rd, wr)
    for n, v in (("E1", 1.0), ("E05", 0.5)):
        eqc(n, 144, 4, v)
    for n, v in (("ID", 1.0), ("IDN", -1.0), ("IDK", 4096.0)):
        eqc(n, 128, 0, v)
    eqc("BMW", 128, 2, 1.0, "RG")
    eqc("BMN", 128, 2, -1.0, "RG")
    ts(T.DUP[:], T.DUP[:], T.PF[:, 1:2], A.add, 16, [W("DUP"), ("PF", 1, 2)], [W("DUP")])
    for x0, n in RUNS:
        ts(T.EARLIER[:, x0:x0 + n], T.RI[:, 0:n], T.PF[:, 1:2], A.add, n, [W("RI"), ("PF", 1, 2)], [("EARLIER", x0, x0 + n)], 15.0, A.is_gt)
    ts(T.IDW[:], T.IDW[:], T.PF[:, 0:1], A.is_equal, 256, [W("IDW"), ("PF", 0, 1)], [W("IDW")])
    fill(T.DF[:], 0.0, 136, W("DF"))
    tt(T.DF[:, :, 0:15], T.IDW[:, :, 8:23], T.IDW[:, :, 9:24], A.subtract, 240, [W("IDW")], [W("DF")])
    cp(T.DF[:, :, 15], T.IDW[:, :, 23], 8, [W("IDW")], [W("DF")])
    for w in (0, 1):
        fill(T["RST%d" % w][:], 0.0, 136, W("RST%d" % w))
    fill(T.RST0[:, 16:136:17], -BIG, 8, W("RST0"))
    fill(T.RST0[:, 0:1], -BIG, 8, W("RST0"))
    fill(T.RST1[:, 0:136:17], BIG, 8, W("RST1"))
    fill(T.ENDS[:], -BIG / 16, 8, W("ENDS"))
    for w in range(4):
        fill(T["GO%d" % w][:, 0:1], 0.0, 16, W("GO%d" % w))
        fill(T["WB%d" % w][:], 0.0, 64, W("WB%d" % w))
    fill(T.EQ[:, :, :, 24], 0.0, 24, W("EQ"))
    fill(T.ONES[:], 32.0, 128, W("ONES"))
    fill(T.KV[:, 0:4], float(BV), 4, ("KV", 0, 4))
    fill(T.HALVES[:], 0.5, 64, W("HALVES"))
    for t in range(RT - 1):
        fill(T.NV0[:, VW * t + 256:VW * t + 264], 0.0, 4, ("NV0", VW * t + 256, VW * t + 264))

    def hilo(dst, hi, lo, src, n, reads):
        cp(hi, src, n, reads, [dst])
        tt(lo, src, hi, A.subtract, 2 * n, reads + [dst], [dst])

    hilo(W("HDB"), T.HDB[:, 0:64], T.HDB[:, 64:128], T.HD[:], 64, [W("HD")])

    def sel(i, d):
        return T.MIP[:, 160 * i + 16 + i - d:160 * i + 144 + i - d]
    for b in range(2):
        bank = "B%d" % b
        mms([(T[bank][:, 64 * y:64 * y + 64], sel(8 * b + y, d), T.HDB[:, 64 * d:64 * d + 64], d == 0, d == 1, 64)
             for y in range(8) for d in (0, 1)], [("MIP", 1280 * b, 1280 * b + 1280), W("HDB")], [(bank, 0, 512)])
        out, rd, wr = T.HT[:, 512 * b:512 * b + 512], [(bank, 0, 512)], [("HT", 512 * b, 512 * b + 512)]
        if b:
            cp(out, T[bank][:], 512, rd, wr)
        else:
            act(out, T[bank][:], F.Copy, 512, rd, wr)

    def lists(t):
        c = 256 * t
        cp(T.LT[:, c:c + 256], T.CMP[:, c:c + 256], 256, [("CMP", c, c + 256)], [("LT", c, c + 256)])

    def expand(t, soft=()):
        fx, c = "FX%d" % t, 1024 + 256 * t
        done = []
        for k in range(16):
            out, in_, rd, wr = T[fx][:, k:4096:16], T.FE[:, c:c + 256], [("FE", c, c + 256)], [(fx + "k", k, k + 1)]
            e = EXPAND[k] if t == 0 else "G"
            if e == "G":
                done.append(gps(lambda q, out=out, in_=in_: q.affine_select(out, in_, [[0, 256]], A.is_equal, 0.0, 0, 0), 512, wr, rd, soft))
            elif e == "V":
                done.append(cp(out, in_, 128, rd, wr))
            else:
                done.append(act(out, in_, F.Copy, 256, rd, wr))
        gr["acc"][fx] = [(j, 0, 4096, 1) for j in done]

    def rel(src, dst):
        return (src - dst) % NR

    def addr(dst):
        return topo.addr(cores[dst])[0:2]
    cross = topo.engines(core, cores[far[0]])
    local = [e for e in topo.engines(core, cores[onchip]) if e not in cross]
    wide = local + cross
    bulk = []

    def emask(es):
        return sum(1 << e for e in es)

    def send(src, h, dst, es, n=1):
        s = "ls%d" % nxt("ls", 99)
        rid, pid = addr(dst)
        buf = "NB%d" % rel(src, rank)
        c0, c1 = QUART * h, QUART * (h + n)
        out, in_ = T["NB%d" % rel(src, dst)][:, c0:c1], T[buf][:, c0:c1]
        rs = T.sem["n%d_%d" % (rel(src, dst), h)]
        bulk.append(add(gr, "G", lambda q: q.remote_dma(out, in_, rs, T.sem[s], pid, rid, emask(es)), GCALL,
                        [(buf, c0, c1)], [], "s", s, len(es), 6.0, soft=bulk[-1:]))

    def recv(src, h, est, es, n=1):
        a = rel(src, rank)
        add(gr, "R", None, 0.0, [], [("NB%d" % a, QUART * h, QUART * (h + n))], "r", "n%d_%d" % (a, h), len(es), est=est)

    o_first = [r for r in far if (r - 1) % NR not in far][0]
    o_second = [r for r in far if r != o_first][0]
    gate, mygate = (first - 1) % NR, (o_first - 1) % NR
    PORT = ((("first", 0), ("first", 1), ("second", 2), ("second", 3)), (("second", 0), ("first", 2), ("first", 3), ("second", 1)))
    for j, h in enumerate(NEAR):
        recv(onchip, h, 5.0 + (j + 1) * ARRIVE[0] / 4, local)
    landed = {}
    for port in PORT:
        for j, (who, h) in enumerate(port):
            landed[who, h] = 5.0 + (j + 1) * ARRIVE[1] / 4
    for who, src, es, late in (("first", o_first, local, ARRIVE[2]), ("second", o_second, wide, ARRIVE[3])):
        for h in range(4):
            if rank == mygate:
                recv(src, h, landed[who, h], cross)
            elif h % 2 == 0:
                recv(src, h, max(landed[who, h], landed[who, h + 1]) + late, es, 2)
    mine = PORT[rank != first]
    for j in range(4):
        who, h = mine[j]
        if j < 2 and (who == "first") == (rank == first):
            send(rank, h, gate, cross)
            mine = mine[:j] + (None,) + mine[j + 1:]
        send(rank, NEAR[j], onchip, local)
    for x in mine:
        if x:
            send(first if x[0] == "first" else rank + onchip - first, x[1], gate, cross)
    if rank == mygate:
        for src, es in ((o_first, local), (o_second, wide)):
            for h in (0, 2):
                send(src, h, onchip, es, 2)
    notes_sent = bulk[-1]

    def shares(t, kinds, soft=()):
        fx, xh, n = "FX%d" % t, "XH%d" % t, 1024 + 256 * t
        for h in range(2):
            if SHARE[t][h] not in kinds:
                continue
            for j, m in pieces(HALF, PIECE["share"]):
                u = HALF * h + j
                c = 256 * t + u // 16
                src, rd = T.FE[:, 0:n].indirect(T.LT[:, c:c + m // 16]), [("FE", 0, n), ("LT", c, c + m // 16)]
                if SHARE[t][h] == "V":
                    tt(T[xh][:, u:u + m], src, T[fx][:, u:u + m], A.min, gcost(m), rd + [(fx, u, u + m)], [(xh, u, u + m)])
                else:
                    act(T["XG%d" % t][:, u:u + m], src, F.Copy, gcost(m), rd, [("XG%d" % t, u, u + m)], soft=soft)
                if SHARE[t][h] == "S":
                    ct = "CT%d" % nxt("h", 2)
                    subtract(ct, fx, u, "XG%d" % t, u, m, T[ct][:])
                    act(T[xh][:, u:u + m], T[ct][:], F.Relu, m, [W(ct)], [(xh, u, u + m)])

    def folds_of(t, kinds):
        for h in range(2):
            if SHARE[t][h] in kinds:
                fold(t, h)

    folds, signs = [], []

    def fold(t, h):
        fx, xh, xg, u = "FX%d" % t, "XH%d" % t, "XG%d" % t, slice(HALF * h, HALF * h + HALF)
        rid, pid = topo.addr(helper(core, T, topo))[0:2]
        s = "ls%d" % nxt("ls", 99)

        def f(q):
            tr = RemoteDMATransfer(dst_ids=[DstId(rid=rid, pnc=pid)], dma_engine_mask=emask(local), remote_sem=T.sem["fo%d_%d" % (t, h)],
                                   srcs=[T[xg][:, u], T[fx][:, u]], dsts=[T[xh][:, u]], alu_op=3)
            return q.remote_dma_fused([tr], local_sem=T.sem[s])
        folds.append(add(gr, "G", f, GCALL + 0.2, [(xg, u.start, u.stop), (fx, u.start, u.stop)], [], "s", s, len(local), 6.0, soft=folds[-1:] + [notes_sent]))
        back = add(gr, "R", None, 0.0, [], [(xh, u.start, u.stop)], "r", "fb%d_%d" % (t, h), len(wide), ARRIVE[6 if t else 4])
        gr["nodes"][back]["soft"].add(folds[-1])

    def share_keys(t):
        xh = "XH%d" % t
        for h in range(2):
            sg = "BMN" if SHARE[t][h] == "S" else "BMW"
            for k0 in (0, 8):
                mms([(T["KEY%d" % h][:, k:136:17], T[xh][:, HALF * h + k:HALF * h + HALF:16], T[sg][:, 0:128:16], k == 0, False, 64)
                     for k in range(k0, k0 + 8)], [(xh, HALF * h, HALF * h + HALF), W(sg)], [W("KEY%d" % h)])
            mms([(T["KEY%d" % h][:, 16:136:17], T.ID[:], T.ENDS[:], False, False, 8)], [W("ID"), W("ENDS")], [W("KEY%d" % h)])

    def gather_headings(t):
        n = 1024 + 256 * t
        for h in (1, 0):
            x, bank, o = "X%d" % h, "B%d" % h, 0
            for eng, w in HEADS[t][h]:
                m0 = 128 * h + o
                for j, m in pieces(16 * w, PIECE["head"]):
                    c, u = 256 * t + m0 + j // 16, 16 * o + j
                    src = T.HT[:, 0:n].indirect(T.LT[:, c:c + m // 16])
                    rd, wr = [("HT", 0, n), ("LT", c, c + m // 16)], [(x, u, u + m)]
                    if eng == "V":
                        cp(T[x][:, u:u + m], src, gcost(m), rd, wr)
                    else:
                        act(T[x][:, u:u + m], src, F.Copy, gcost(m), rd, wr)
                extract(bank, o, "E1", x, w, o)
                cp(T.CL0[:, m0:m0 + w], T[bank][:, o:o + w], w, [(bank, o, o + w)], [("CL0", m0, m0 + w)])
                o += w
            m0 = 128 * h
            sl, pr, P = slice(m0, m0 + 128), (bank, 0, 128), T[bank][:, 0:128]
            act(T.C32[:, sl], P, F.Identity, 128, [pr, MOFF], [("C32", m0, m0 + 128)], bias=T.PF[:, 7:8], scale=32.0)
            act(T.SQ[:, sl], P, F.Square, 128, [pr, P16], [("SQ", m0, m0 + 128)], bias=T.PF[:, 8:9])

    def visits(t):
        fx = "FX%d" % t
        for a in range(NR):
            nb, cl, cln = "NB%d" % a, "CL%d" % (a % 2), "CL%d" % (1 - a % 2)
            if a == 1 and t > 0:
                apply_updates(t - 1)
            for h in (1, 0):
                x, s, bank, m0, w = "X%d" % h, "SS%d" % h, "B%d" % h, 128 * h, 128
                v = SPLIT[t > 0][a][h]
                for eng, o, n in (("V", 0, v), ("S", v, 128 - v)):
                    for j, m in pieces(16 * n, PIECE[eng]) if n else []:
                        c, u = m0 + o + j // 16, 16 * o + j
                        f0 = 16 * m0 + u
                        src, rd = T[nb][:, 0:H].indirect(T[cl][:, c:c + m // 16]), [(nb, 0, H), (cl, c, c + m // 16)]
                        if eng == "V":
                            tt(T[x][:, u:u + m], src, T[fx][:, f0:f0 + m], A.is_lt, gcost(m), rd + [(fx, f0, f0 + m)], [(x, u, u + m)])
                        else:
                            db = "B%d" % (3 + nxt("u", 2))
                            act(T[x][:, u:u + m], src, F.Copy, gcost(m), rd, [(x, u, u + m)])
                            subtract(db, fx, f0, x, u, m)
                            signs.append(act(T[s][:, u:u + m], T[db][:, 0:m], F.Sign, m, [W(db), HLF], [(s, u, u + m)], bias=T.PF[:, 6:7]))
                    if n:
                        extract(bank, o, "E1" if eng == "V" else "E05", x if eng == "V" else s, n, o, eng == "S")
                sl = slice(m0, m0 + w)

                def C(n):
                    return (n, m0, m0 + w)
                P, pr, kc = T[bank][:, 0:w], (bank, 0, w), 4 * t + a
                if SCALE[a] == "V":
                    ts(P, P, float(SLOPE), A.mult, w, [pr, ("KV", kc, kc + 1)], [pr], T.KV[:, kc:kc + 1], A.add)
                else:
                    act(P, P, F.Identity, w, [pr, ("KV", kc, kc + 1)], [pr], bias=T.KV[:, kc:kc + 1], scale=float(SLOPE))
                tt(P, P, T.SQ[:, sl], A.add, w, [pr, C("SQ")], [pr])
                tt(T.TI[:, sl], P, T.C32[:, sl], A.max, w, [pr, C("C32")], [C("TI")])
                ts(T.CI[:, sl], T.TI[:, sl], 5, A.arith_shift_right, w, [C("TI")], [C("CI")], 4095, A.bitwise_and)
                if a < NR - 1:
                    cp(T[cln][:, sl], T.CI[:, sl], w, [C("CI")], [C(cln)])
                    ts(T.C32[:, sl], T.CI[:, sl], 32.0, A.mult, w, [C("CI")], [C("C32")], float(-OFF), A.add)
                    act(T.SQ[:, sl], T.C32[:, sl], F.Square, w, [C("C32"), SQB], [C("SQ")], bias=T.PF[:, 5:6], scale=1.0 / 32)
                else:
                    cp(T.CW[:, sl], T.CI[:, sl], w, [C("CI")], [C("CW")])
                    finish(t, h)

    def election(h):
        key, s, CT = "KEY%d" % h, slice(8 * h, 8 * h + 8), T["CT%d" % h]
        c, rd, ct, cd = T.CW[:, 128 * h:128 * h + 128], ("CW", 128 * h, 128 * h + 128), W("CT%d" % h), ("CD", h, h + 1)
        mms([(CT[:, 0:8, :], c, T.IDW[:], True, True, 4 * 256)], [rd, W("IDW")], [ct])
        mms([(T[key][:, 136:272], c, T.DF[:], False, False, 4 * 136)], [rd, W("DF")], [W(key)])
        act(T.CD[:, s, :], CT[:, 0:8, 0:24], F.Copy, 192, [ct], [cd])
        for d in range(1, 9):
            j, b = 3 * h + d % 3, (d if d < 8 else 0)
            e = ("EQ", j, j + 1)
            tt(T.EQ[:, j, :, 8 - b:24], CT[:, 0:8, 8 - b + d:24 + d], T.CD[:, s, 8 - b:24], A.is_equal, 8 * (16 + b), [ct, cd], [e])
            mms([(T[key][:, 0:136], T.IDK[:], T.EQ[:, j, :, o:o + 17], False, d == 8, 136) for o in ((8, 8 - d) if d < 8 else (8,))],
                [e, W("IDK")], [W(key)])

    def pick(w, h):
        key, (run, go, pk, wb) = "KEY%d" % h, (n + str(2 * w + h) for n in ("RUN", "GO", "PICK", "WB"))
        scan(T[run][:], T["RST%d" % w][:], T[key][:, 0:136], A.add, A.min if w else A.max, 136, [W("RST%d" % w), (key, 0, 136)], [W(run)])
        tt(T[go][:, 1:136], T[key][:, 1:136], T[run][:, 0:135], A.is_ge if w else A.is_le, 136, [(key, 0, 136), W(run)], [W(go)])
        scan(T[pk][:], T[go][:], T[key][:, 136:272], A.mult, A.add, 136, [(key, 136, 272), W(go)], [W(pk)])
        hilo(W(wb), T[wb][:, 0:128:16], T[wb][:, 1:128:16], T[pk][:, 15:136:17], 8, [W(pk)])

    def row(w, h, out, reg):
        wb = "WB%d" % (2 * w + h)
        mms([(out, T[wb][:], T.ID[:], True, True, 128)], [W(wb), W("ID")], [reg])

    def headings_out(t, h):
        bank, c = "B%d" % h, 1024 + 256 * t + 128 * h
        row(0, h, T[bank][:, 0:128], (bank, 0, 128))
        act(T.HT[:, c:c + 128], T[bank][:, 0:128], F.Copy, 128, [(bank, 0, 128)], [("HT", c, c + 128), ("KS1", h, h + 1)],
            accum=T.KS1[:, h:h + 1])

    def finish(t, h):
        election(h)
        pick(0, h)
        pick(1, h)
        headings_out(t, h)
        notes(t, h)

    def write_yh(t):
        c, y = 1024 + 256 * t, ("YH8", 256 * t, 256 * t + 256)
        mms([(T.CT0[0:8, 0:8, :], T.BMW[:, 0:128:16], T.HT[:, c:c + 256], True, True, 256)], [W("BMW"), ("HT", c, c + 256)], [W("CT0")])
        act(T.YH8[:, 256 * t:256 * t + 256], T.CT0[0:8, 0:8, :], F.Copy, 256, [W("CT0")], [y])
        dma("Y", T.yh[:, 256 * t:256 * t + 256], T.YH8[:, 256 * t:256 * t + 256], 2.5, [y], [])

    def notes(t, h):
        c, ov, ol = 1024 + 256 * t + 128 * h, VW * t + 128 * h, 16 * t + 8 * h
        lr, lb, lf, lu, old, dc, fl, of, eqt = (n + str(h) for n in ("LR", "LB", "LF", "LU", "OLD", "DC", "FL", "OF", "EQT"))
        ct = "CT%d" % h
        (q0, Q0), (q1, Q1), (q3, Q3) = (((ct, 32 * j, 32 * j + 128), T[ct][:, j:j + 4, :]) for j in (0, 4, 12))
        q2, Q2 = (ct, 256, 264), T[ct][:, 8, 0:8]
        row(1, h, Q0, q0)
        act(T[lr][:], Q0, F.Copy, 128, [q0], [W(lr)])
        mms([(Q1, T.BMW[:], T[lr][:, ::-1], True, True, 128)], [W("BMW"), W(lr)], [q1])
        extract(ct, 256, "E1", lr, 8, out=Q2)
        cp(T[lb][:], Q1, 128, [q1], [W(lb)])
        for n in (lf, lu):
            cp(T[n][:], Q2, 8, [q2], [W(n)])
        for mb, (x0, n) in enumerate(RUNS):
            ts(T[eqt][:, x0:x0 + n], T[lb][:, 128 - n:128], T[lf][:, mb:mb + 1], A.is_equal, 64, [W(lb), W(lf)], [(eqt, mb, mb + 1)])
        scan(T[fl][:], T[eqt][:], T.EARLIER[:], A.max, A.mult, 288, [W(eqt), W("EARLIER")], [W(fl)])
        tt(T[of][:, 0:4], T[fl][:, 15:576:160], T.DUP[:, 0:4], A.mult, 8, [W(fl), W("DUP")], [(of, 0, 4)])
        tt(T[of][:, 7:3:-1], T[fl][:, 143:576:144], T.DUP[:, 4:8], A.mult, 8, [W(fl), W("DUP")], [(of, 4, 8)])
        act(T[old][:], T.NB0[:, 0:H].indirect(T[lu][:]), F.Copy, gcost(128), [("NB0", 0, H), W(lu)], [W(old)])
        mms([(Q3, T.ID[:], T.FE[:, c:c + 128], True, False, 128), (Q3, T.IDN[:], T[old][:], False, True, 128)],
            [W("ID"), W("IDN"), ("FE", c, c + 128), W(old)], [q3])
        ts(T[dc][:], Q3, 32.0, A.min, 128, [q3], [W(dc)], -32.0, A.max)
        mms([(Q0, T.ID[:], T[old][:], True, False, 128), (Q0, T.ID[:], T[dc][:], False, True, 128)], [W("ID"), W(old), W(dc)], [q0])
        act(T.NV0[:, ov:ov + 128], Q0, F.Copy, 128, [q0], [("NV0", ov, ov + 128)])
        tt(T[of][:], T[of][:], T[lf][:], A.max, 16, [W(of), W(lf)], [W(of)])
        cp(T.NL0[:, ol:ol + 8], T[of][:], 8, [W(of)], [("NL0", ol, ol + 8)])
        if t + 1 < RT:
            hi = VW * t + 264 + 8 * h
            hilo(("NV0", hi, hi + 24), T.NV0[:, hi:hi + 8], T.NV0[:, hi + 16:hi + 24], T[of][:], 8, [W(of)])

    def scatter(t, a):
        nb, nv, nl = "NB%d" % a, "NV%d" % a, "NL%d" % a
        for h in (1, 0):
            ov, ol = VW * t + 128 * h, 16 * t + 8 * h
            cp(T[nb][:, 0:H + DUMMY].indirect(T[nl][:, ol:ol + 8]), T[nv][:, ov:ov + 128], gcost(128, True),
               [(nv, ov, ov + 128), (nl, ol, ol + 8)], [(nb, 0, H + DUMMY)])

    def bias(t, a):
        c, nv, k = 4 * (t + 1) + a, "NV%d" % a, VW * t + 256
        act(T.KV[:, c:c + 1], T.KV[:, 0:1], F.Identity, 1, [(nv, k, k + 1), ("KV", 0, 1)], [("KV", c, c + 1)], bias=T[nv][:, k:k + 1])

    def kappa(t):
        k = VW * t + 256
        mms([(T.B3[:, 0:1], T.ONES[:], T.KS1[:, h:h + 1], h == 0, h == 1, 256) for h in range(2)], [W("ONES"), W("KS1")], [W("B3")])
        cp(T.KI[:, 0:1], T.B3[:, 0:1], 1, [W("B3")], [W("KI")])
        ts(T.KJ[:, 0:1], T.KI[:, 0:1], 255 * 32, A.bitwise_and, 1, [W("KI")], [W("KJ")])
        cp(T.NV0[:, k:k + 1], T.KJ[:, 0:1], 1, [W("KJ")], [("NV0", k, k + 1)])
        bias(t, 0)

    sent = {}

    def send_update(t):
        c = slice(VW * t, VW * t + VW)
        for a in range(1, NR):
            dst = (rank - a) % NR
            (rid, pid), es = addr(dst), cross
            num["lsend"] += len(es)
            bulk.append(add(gr, "G", lambda q, a=a, rid=rid, pid=pid, es=es: q.remote_dma(
                T["NV%d" % a][:, c], T.NV0[:, c], T.sem["iv%d_%d" % (a, t)], T.sem.lsend, pid, rid, emask(es)),
                GCALL, [("NV0", c.start, c.stop)], [], "s", "lsend", num["lsend"], soft=bulk[-1:]))
            sent[t, a] = bulk[-1]

    def apply_updates(t):
        for a in range(1, NR):
            nv, nl, c = "NV%d" % a, "NL%d" % a, VW * t
            add(gr, "R", None, 0.0, [], [(nv, c, c + VW)], "r", "iv%d_%d" % (a, t), len(cross), ARRIVE[5], soft=[sent[t, a]])
            bias(t, a)
            if a < NR - 1 or not WHOLE:
                tt(T.PL[:], T[nv][:, c + 264:c + 280], T[nv][:, c + 280:c + 296], A.add, 32, [(nv, c + 264, c + 296)], [W("PL")])
                cp(T[nl][:, 16 * t:16 * t + 16], T.PL[:], 16, [W("PL")], [(nl, 16 * t, 16 * t + 16)])
                scatter(t, a)
        if WHOLE:
            nb, nv, s = "NB%d" % rel(onchip - 1, rank), "NV%d" % rel(onchip, rank), "ls%d" % nxt("ls", 99)
            rid, pid = addr(onchip)
            bulk.append(add(gr, "G", lambda q: q.remote_dma(T.NB3[:, 0:H], T[nb][:, 0:H], T.sem["wh%d" % t], T.sem[s], pid, rid, emask(wide)),
                            GCALL, [(nb, 0, H), (nv, VW * t, VW * t + VW)], [], "s", s, len(wide), ARRIVE[7], soft=bulk[-1:]))
            add(gr, "R", None, 0.0, [], [("NB3", 0, H)], "r", "wh%d" % t, len(wide), ARRIVE[7] + (2.0 if rank == first else 0.0), soft=bulk[-1:])

    for t in range(RT):
        lists(t)
    for t in range(EARLY):
        expand(t)
    gather_headings(0)
    for t in range(RT):
        shares(t, "VSF")
    folds_of(1, "F")
    for t in range(RT):
        share_keys(t)
        visits(t)
        scatter(t, 0)
        if t + 1 < RT:
            shares(t + 1, "L", signs[-1:])
            gather_headings(t + 1)
            kappa(t)
            send_update(t)
            folds_of(t + 1, "L")
        if t + EARLY < RT:
            expand(t + EARLY, bulk[-1:])
            folds_of(t + EARLY, "F")
        write_yh(t)
    for j, e in ((0, "S"), (1, "Y")):
        dma(e, T.yl[:, HALF * j:HALF * j + HALF], T.NB0[:, HALF * j:HALF * j + HALF], 5.0, [("NB0", HALF * j, HALF * j + HALF)], [])
    return gr


def helper(core, T, topo):
    return [c for c in topo.cores_of(core) if topo.die(c) == topo.die(core) and T.rank_of(c) is None][0]


def hand_back(core, home, T, topo):
    gr = {"nodes": [], "acc": {}, "bank": {}}
    es = topo.engines(core, home)
    half = [e for e in es if e not in topo.engines(home, [c for c in T.cores if topo.chip(c) != topo.chip(home)][0])]
    rid, pid = topo.addr(home)[0:2]
    last = []
    for t in range(RT):
        for h in range(2):
            if SHARE[t][h] in "FL":
                xh, reg = T["XH%d" % t][:, HALF * h:HALF * h + HALF], [("XH%d" % t, h, h + 1)]
                add(gr, "R", None, 0.0, [], reg, "r", "fo%d_%d" % (t, h), len(half), soft=last[-1:])
                last.append(add(gr, "G", lambda q, xh=xh, t=t, h=h: q.remote_dma(xh, xh, T.sem["fb%d_%d" % (t, h)], T.sem.lsend, pid, rid,
                                                                               topo.mask(core, home)),
                                1.0, reg, [], "s", "lsend", len(es) * (len(last) + 1), soft=last[-1:]))
    return gr


def program(core, T, topo):
    if T.rank_of(core) is not None:
        return build(core, T, topo)
    homes = [c for c in T.cores if helper(c, T, topo) == core]
    return hand_back(core, homes[0], T, topo) if homes else None


def rank_program(g, core, T, topo):
    gr = program(core, T, topo)
    if gr and gr["nodes"]:
        emit_all(gr, schedule(gr), g, T)
